import numpy as np
import ml_dtypes


def mxq(x, axis, fmt="e4m3"):
    dtype, down = {"e4m3": (ml_dtypes.float8_e4m3fn, 7), "e5m2": (ml_dtypes.float8_e5m2, 14)}[fmt]
    v = np.moveaxis(np.asarray(x, np.float32).astype(ml_dtypes.bfloat16).astype(np.float64), axis, -1)
    blocks = v.reshape(v.shape[:-1] + (-1, 32))
    amax = np.abs(blocks).max(-1, keepdims=True)
    byte = np.maximum(np.where(amax > 0, np.frexp(amax)[1] - 1 + 127, 0) - down, 1)
    scale = np.exp2(byte - 127.0)
    codes = (blocks / scale).astype(np.float32).astype(dtype).astype(np.float64)
    return np.moveaxis((codes * scale).reshape(v.shape), -1, axis)


WIDE = False


def mx_kscale(k):
    if not WIDE:
        return np.ones(k)
    levels = np.array([24, -24, 12, -12, 0])
    if k % 512:
        return np.exp2(np.random.permutation(np.resize(levels, k // 32))).repeat(32)
    a = np.empty((k // 512, 16))
    for p in range(k // 512):
        a[p, :8] = np.random.permutation(np.resize(levels, 8))
        for g in range(8):
            far = levels[np.abs(levels - a[p, g]) >= 10]
            a[p, g + 8] = far[np.random.randint(len(far))]
    return np.exp2(a.ravel()).repeat(32)


def f64(x):
    return np.asarray(x).astype(np.float64)


def striped(idx):
    return np.tile(idx.reshape(-1, 16).T, (8, 1)).astype(np.uint16)


def unstriped(offs):
    return offs[:16].T.reshape(-1).astype(np.int64)


E2M1 = np.array([0.0, 0.5, 1.0, 1.5, 2.0, 3.0, 4.0, 6.0, -0.0, -0.5, -1.0, -1.5, -2.0, -3.0, -4.0, -6.0])


def pack_weight(w, fmt):
    k, n = w.shape
    w = f64(np.asarray(w, np.float32).astype(ml_dtypes.bfloat16)).reshape(k // 32, 32, n)
    amax = np.abs(w).max(1)
    if fmt == "e4m3":
        byte = np.frexp(amax)[1] - 1 + 127 - 7
    else:
        mant, ex = np.frexp(amax / 6.0)
        byte = np.where(mant > 0.5, ex, ex - 1) + 127
    byte = np.clip(np.where(amax > 0, byte, 1), 1, 254)
    scaled = (w * np.exp2(127.0 - byte)[:, None, :]).reshape(k, n).astype(np.float32)
    by_word = np.ascontiguousarray(scaled.reshape(k // 512, 128, 4, n).transpose(0, 1, 3, 2))
    if fmt == "e4m3":
        words = by_word.astype(ml_dtypes.float8_e4m3fn).view(np.uint8)
    else:
        c = by_word.astype(ml_dtypes.float4_e2m1fn).view(np.uint8) & 0xF
        words = (c[..., 0::2] | (c[..., 1::2] << 4)).reshape(k // 512, 128, 2 * n)
    return np.ascontiguousarray(words), np.ascontiguousarray(byte.astype(np.uint8).reshape(k // 512, 16, n))


def unpack_weight(words, scales, fmt):
    g, _, n = scales.shape
    words = np.ascontiguousarray(words).reshape(g, 128, n, -1)
    if fmt == "e4m3":
        vals = words.view(ml_dtypes.float8_e4m3fn).astype(np.float64)
    else:
        nib = np.empty((g, 128, n, 4), np.uint8)
        nib[..., 0::2] = words & 0xF
        nib[..., 1::2] = words >> 4
        vals = E2M1[nib]
    vals = vals * np.repeat(np.exp2(scales.astype(np.float64) - 127.0), 8, axis=1)[..., None]
    return vals.transpose(0, 1, 3, 2).reshape(g * 512, n)


def pack_table4(v):
    words, scales = pack_weight(v, "e2m1")
    g, t = words.shape[0] // 2, v.shape[1]
    return np.ascontiguousarray(words.reshape(g, 2, 128, t, 2).transpose(0, 2, 3, 1, 4).reshape(g, 128, t, 4)), scales


def unpack_table4(words, scales):
    g, _, t, _ = words.shape
    return unpack_weight(words.reshape(g, 128, t, 2, 2).transpose(0, 3, 1, 2, 4).reshape(2 * g, 128, 2 * t), scales, "e2m1")


def planes(y):
    n, m = y.shape
    v = y.astype(np.float32).astype(ml_dtypes.bfloat16).astype(np.float64).reshape(n // 32, 32, m)
    top = np.abs(v).max(1)
    byte = np.clip(np.where(top > 0, np.frexp(top)[1] - 1 + 127 - 7, 1), 1, 254)
    codes = (v * np.exp2(127.0 - byte)[:, None, :]).reshape(n, m).astype(np.float32).astype(ml_dtypes.float8_e4m3fn).view(np.uint8)
    words = codes.reshape(n // 512, 128, 4, m).transpose(0, 1, 3, 2)
    return np.ascontiguousarray(words), np.ascontiguousarray(byte.astype(np.uint8).reshape(n // 512, 16, m))


def silu(f):
    return f / (1.0 + np.exp(-np.maximum(f, -700.0)))


K, R, N, T, J = 1024, 512, 512, 2048, 1024


def setup_inputs():
    n = np.random.standard_normal
    s = mx_kscale(K)[:, None]
    u = mx_kscale(R)[:, None]
    p_tab = pack_table4(n((K, T)) * s)
    p_wu = pack_weight(n((K, R)) / np.sqrt(K) / s * u.T, "e4m3")
    p_wd = pack_weight(n((R, N)) / np.sqrt(R) / u, "e2m1")
    return {
        "tab_words": p_tab[0],
        "tab_scales": p_tab[1],
        "wg": (n((K, R)) / np.sqrt(K) / s).astype(np.float32),
        "wu_words": p_wu[0],
        "wu_scales": p_wu[1],
        "wd_words": p_wd[0],
        "wd_scales": p_wd[1],
        "rT": (n((N, T))).astype(np.float32),
        "wgo": np.tile(np.random.uniform(0.5, 2.0, J), (128, 1)).astype(np.float32),
        "offs": striped(np.random.permutation(T)[:J]),
    }


def reference(tab_words, tab_scales, wg, wu_words, wu_scales, wd_words, wd_scales, rT, wgo, offs):
    idx = unstriped(offs)
    tab_ = unpack_table4(tab_words, tab_scales)[:, idx]
    wg_ = mxq(f64(wg), 0, "e4m3")
    wu_ = unpack_weight(wu_words, wu_scales, "e4m3")
    ga = wg_.T @ tab_
    ub = wu_.T @ tab_
    h = silu(ga) * ub
    h_ = mxq(h, 0, "e4m3")
    wd_ = unpack_weight(wd_words, wd_scales, "e2m1")
    y = wd_.T @ h_
    out = np.zeros((N, T))
    out[:, idx] = f64(wgo)[0] * (y + f64(rT)[:, idx])
    return (out,) + planes(out)

@@ -1,0 +1,240 @@
+from contextlib import ExitStack
+
+import concourse.mybir as mybir
+
+K, R, N, T, J = 1024, 512, 512, 2048, 1024
+FLOPS = 2 * J * (2 * K * R + R * N)
+
+F32 = mybir.dt.float32
+BF16 = mybir.dt.bfloat16
+I32 = mybir.dt.int32
+U32 = mybir.dt.uint32
+U16 = mybir.dt.uint16
+U8 = mybir.dt.uint8
+FP8X4 = mybir.dt.float8_e4m3fn_x4
+FP4X4 = mybir.dt.float4_e2m1fn_x4
+MULT = mybir.AluOpType.mult
+ADD = mybir.AluOpType.add
+SILU = mybir.ActivationFunctionType.Silu
+
+P = 128
+PACK = 4
+PASSES = K // (P * PACK)
+TOK = 128
+QUARTER = 256
+HALF = 512
+GATHERS = ((0, 256), (256, 512), (512, 1024))
+CHUNK = 256
+SPLIT = 64
+
+
+def tile_list_modp_gsilu_resP_kernel(
+    tc, tab_words, tab_scales, wg, wu_words, wu_scales, wd_words, wd_scales, rT, wgo, offs, out_0, out_1, out_2
+):
+    nc = tc.nc
+    with ExitStack() as ctx:
+        held = ctx.enter_context(tc.tile_pool(name="held", bufs=1))
+        ring = ctx.enter_context(tc.tile_pool(name="ring", bufs=3))
+        pair = ctx.enter_context(tc.tile_pool(name="pair", bufs=2))
+        ps3 = ctx.enter_context(tc.psum_pool(name="ps3", bufs=3))
+        ps2 = ctx.enter_context(tc.psum_pool(name="ps2", bufs=2))
+
+        def keep(shape, dtype, name, tag=None):
+            return held.tile(shape, dtype, name=name, tag=tag or name, align_bytes=64)
+
+        offsets = held.tile([P, J // 16], U16, name="offsets")
+        nc.sync.dma_start(offsets[:], offs)
+
+        def listed(j0, j1):
+            return offsets[:, j0 // 16 : j1 // 16]
+
+        tab_sc = keep([P, T], U8, "tab_sc", "slot_s")
+        for q in range(4):
+            nc.sync.dma_start(
+                tab_sc[32 * q + 24 : 32 * q + 32, :].bitcast(I32), tab_scales[:, 4 * q : 4 * q + 4, :].bitcast(I32)
+            )
+        wg_raw = [keep([P, PACK, R], F32, "wg_raw%d" % a, "slot_%s" % "ab"[a]) for a in range(PASSES)]
+        for a in range(PASSES):
+            nc.sync.dma_start(wg_raw[a][:], wg[512 * a : 512 * (a + 1), :].rearrange("(p j) r -> p j r", j=PACK))
+        tab_w = keep([P, T], I32, "tab_w", "slot_w")
+        nc.sync.dma_start(tab_w[:], tab_words[0].rearrange("p t b -> p (t b)").bitcast(I32))
+
+        wu_sc_raw = keep([P, PASSES, R], U8, "wu_sc_raw")
+        v_sc = keep([P, PASSES, J], U8, "v_sc")
+        nc.vector.memset(wu_sc_raw[:].bitcast(I32), 0)
+        for q in range(4):
+            nc.vector.memset(tab_sc[32 * q : 32 * q + 24, :].bitcast(I32), 0)
+        warm = keep([P, 8], F32, "warm")
+        warm_out = keep([P, 8], F32, "warm_out")
+        nc.vector.memset(warm[:], 0.0)
+        nc.scalar.activation(warm_out[:], warm[:], SILU)
+        nc.vector.memset(v_sc[:].bitcast(I32), 0)
+        for q in range(4):
+            nc.sync.dma_start(
+                wu_sc_raw[32 * q : 32 * q + 4, :, :].bitcast(I32),
+                wu_scales[:, 4 * q : 4 * q + 4, :].rearrange("a r n -> r a n").bitcast(I32),
+            )
+        wu_raw = keep([P, PASSES, R], I32, "wu_raw", "slot_d")
+        nc.sync.dma_start(wu_raw[:], wu_words.rearrange("a p r i -> p a (r i)").bitcast(I32))
+        wd_raw = keep([P, 2 * N], U8, "wd_raw")
+        nc.sync.dma_start(wd_raw[:].bitcast(I32), wd_words[0].bitcast(I32))
+
+        picked_sc = keep([P, J], U8, "picked_sc", "slot_p")
+        nc.vector.tensor_copy(picked_sc[:], tab_sc[:].indirect(offsets[:]))
+        for a in range(PASSES):
+            nc.gpsimd.dma_start(
+                v_sc[0:100, a, :].bitcast(I32), picked_sc[24 + 4 * a : 124 + 4 * a, :].bitcast(I32)
+            )
+
+        wd_sc_raw = keep([P, N], U8, "wd_sc_raw", "slot_s")
+        nc.vector.memset(wd_sc_raw[:].bitcast(I32), 0)
+        for q in range(4):
+            nc.gpsimd.dma_start(
+                wd_sc_raw[32 * q : 32 * q + 4, :].bitcast(I32), wd_scales[0, 4 * q : 4 * q + 4, :].bitcast(I32)
+            )
+
+        wg_c, wg_s = [], []
+        for a in range(PASSES):
+            bf = keep([P, R * PACK], BF16, "wg_bf%d" % a)
+            src = wg_raw[a][:].rearrange("p j (m t) -> p m j t", t=PACK)
+            dst = bf[:].rearrange("p (t m j) -> p m j t", t=PACK, j=PACK)
+            if a == 0:
+                nc.scalar.copy(dst, src)
+            else:
+                nc.scalar.copy(dst[:, SPLIT:], src[:, SPLIT:])
+                nc.vector.tensor_copy(dst[:, :SPLIT], src[:, :SPLIT])
+            codes = keep([P, R], U32, "wg_c%d" % a)
+            scales = keep([P, R], U8, "wg_s%d" % a)
+            nc.vector.quantize_mx(codes[:].bitcast(FP8X4), scales[:], bf[:])
+            wg_c.append(codes)
+            wg_s.append(scales)
+
+        rT_rows = rT.rearrange("(p i) t -> p i t", i=PACK)
+        res = [keep([P, T], F32, "res0", "slot_p")]
+        nc.sync.dma_start(res[0][:], rT_rows[:, 0, :])
+        gate = keep([P, J], F32, "gate", "slot_a")
+        nc.sync.dma_start(gate[:], wgo)
+
+        wu_s = keep([P, PASSES, R], U8, "wu_s")
+        nc.vector.tensor_copy(
+            wu_s[:].rearrange("p a (t m) -> p a m t", t=PACK), wu_sc_raw[:].rearrange("p a (m t) -> p a m t", t=PACK)
+        )
+
+        v_w = []
+        wu_c = keep([P, PASSES, R], I32, "wu_c", "slot_c")
+        for g, (j0, j1) in enumerate(GATHERS):
+            both = keep([P, j1 - j0], U32, "both%d" % g, "slot_g%d" % g)
+            nc.vector.tensor_copy(both[:], tab_w[:].bitcast(U32).indirect(listed(j0, j1)))
+            parted = keep([P, PASSES, 2 * (j1 - j0)], U8, "parted%d" % g, "slot_h%d" % g)
+            nc.vector.tensor_copy(parted[:].bitcast(U16), both[:].bitcast(U16).rearrange("p (j d) -> p d j", d=2))
+            v_w.append(parted)
+            if g == 0:
+                nc.vector.tensor_copy(
+                    wu_c[:].rearrange("p a (t m) -> p a m t", t=PACK),
+                    wu_raw[:].rearrange("p a (m t) -> p a m t", t=PACK),
+                )
+
+        for i, slot in ((1, "slot_w"), (2, "slot_g2"), (3, "slot_h0")):
+            res.append(keep([P, T], F32, "res%d" % i, slot))
+            nc.sync.dma_start(res[i][:], rT_rows[:, i, :])
+
+        wd_c = keep([P, 2 * N], U8, "wd_c")
+        wd_s = keep([P, N], U8, "wd_s")
+        nc.vector.tensor_copy(
+            wd_c[:].bitcast(U16).rearrange("p (i m) -> p m i", i=PACK),
+            wd_raw[:].bitcast(U16).rearrange("p (m i) -> p m i", i=PACK),
+        )
+        nc.vector.tensor_copy(
+            wd_s[:].rearrange("p (i m) -> p m i", i=PACK), wd_sc_raw[:].rearrange("p (m i) -> p m i", i=PACK)
+        )
+
+        pages = [keep([P, T], F32, "page0", "slot_d")]
+        nc.vector.memset(pages[0][:], 0.0)
+
+        def moving(a, j0):
+            g = [x for x, (lo, hi) in enumerate(GATHERS) if lo <= j0 < hi][0]
+            c = j0 - GATHERS[g][0]
+            return v_w[g][:, a, 2 * c : 2 * (c + TOK)].bitcast(FP4X4), v_sc[:, a, j0 : j0 + TOK]
+
+        def stage1(bank, words, scales, j0):
+            for t in range(PACK):
+                for a in range(PASSES):
+                    rhs, rhs_s = moving(a, j0)
+                    nc.tensor.matmul_mx(
+                        bank[:, t, :], lhsT=words(a, t), lhsT_scale=scales(a, t), rhs=rhs, rhs_scale=rhs_s,
+                        start=(a == 0), stop=(a == PASSES - 1),
+                    )
+
+        h_c = keep([P, J], U32, "h_c")
+        h_s = keep([P, J], U8, "h_s")
+        y = [keep([P, J], F32, "y%d" % i) for i in range(PACK)]
+
+        def stage2(i, j0, j1):
+            bank = ps2.tile([P, HALF], F32, name="y_bank")
+            nc.tensor.matmul_mx(
+                bank[:, : j1 - j0],
+                lhsT=wd_c[:, 2 * P * i : 2 * P * (i + 1)].bitcast(FP4X4), lhsT_scale=wd_s[:, P * i : P * (i + 1)],
+                rhs=h_c[:, j0:j1].bitcast(FP8X4), rhs_scale=h_s[:, j0:j1], start=True, stop=True,
+            )
+            nc.scalar.copy(y[i][:, j0:j1], bank[:, : j1 - j0])
+
+        def place(i, j0, j1):
+            z = pair.tile([P, J], F32, name="z")
+            nc.vector.tensor_tensor(z[:, : j1 - j0], res[i][:].indirect(listed(j0, j1)), y[i][:, j0:j1], ADD)
+            nc.vector.tensor_tensor(pages[i][:].indirect(listed(j0, j1)), z[:, : j1 - j0], gate[:, j0:j1], MULT)
+
+        for q in range(J // QUARTER):
+            h_bf = pair.tile([P, QUARTER, PACK], BF16, name="h_bf", align_bytes=64)
+            for c in range(QUARTER // TOK):
+                j0 = q * QUARTER + c * TOK
+                g_bank = ps3.tile([P, PACK, TOK], F32, name="g_bank")
+                u_bank = ps3.tile([P, PACK, TOK], F32, name="u_bank")
+                stage1(
+                    g_bank, lambda a, t: wg_c[a][:, P * t : P * (t + 1)].bitcast(FP8X4),
+                    lambda a, t: wg_s[a][:, P * t : P * (t + 1)], j0,
+                )
+                stage1(
+                    u_bank, lambda a, t: wu_c[:, a, P * t : P * (t + 1)].bitcast(FP8X4),
+                    lambda a, t: wu_s[:, a, P * t : P * (t + 1)], j0,
+                )
+                act = ring.tile([P, TOK, PACK], F32, name="act")
+                nc.scalar.activation(act[:], g_bank[:].rearrange("p t j -> p j t"), SILU)
+                nc.vector.tensor_tensor(
+                    h_bf[:, c * TOK : (c + 1) * TOK, :], u_bank[:].rearrange("p t j -> p j t"), act[:], MULT
+                )
+            cols = slice(q * QUARTER, (q + 1) * QUARTER)
+            nc.vector.quantize_mx(h_c[:, cols].bitcast(FP8X4), h_s[:, cols], h_bf[:].rearrange("p j t -> p (j t)"))
+            stage2(0, cols.start, cols.stop)
+            if q > 0:
+                place(0, cols.start - QUARTER, cols.start)
+        place(0, J - QUARTER, J)
+
+        out_rows = out_0.rearrange("(p i) t -> p i t", i=PACK)
+        woven = [keep([P, CHUNK, PACK], BF16, "woven%d" % c) for c in range(T // CHUNK)]
+        out_c = keep([P, T], U32, "out_c")
+        out_s = keep([P, T], U8, "out_s")
+        for i in range(PACK):
+            if i > 0:
+                for j0 in range(0, J, HALF):
+                    stage2(i, j0, j0 + HALF)
+                pages.append(keep([P, T], F32, "page%d" % i, "slot_%s" % "cpw"[i - 1]))
+                nc.gpsimd.memset(pages[i][:], 0.0)
+                place(i, 0, J)
+            nc.sync.dma_start(out_rows[:, i, :], pages[i][:])
+            for c in range(T // CHUNK):
+                cols = slice(c * CHUNK, (c + 1) * CHUNK)
+                if i == 2 and c % 2 == 0:
+                    nc.scalar.copy(woven[c][:, :, 2:4], pages[i][:, cols].unsqueeze(2).to_broadcast([P, CHUNK, 2]))
+                elif i == 3 and c % 2 == 0:
+                    nc.vector.tensor_copy(woven[c][:, :, i], pages[i][:, cols])
+                else:
+                    nc.scalar.copy(woven[c][:, :, i], pages[i][:, cols])
+        words_out = out_1[0].rearrange("p t b -> p (t b)").bitcast(I32)
+        for c in range(T // CHUNK):
+            cols = slice(c * CHUNK, (c + 1) * CHUNK)
+            nc.vector.quantize_mx(out_c[:, cols].bitcast(FP8X4), out_s[:, cols], woven[c][:].rearrange("p t i -> p (t i)"))
+            if c % 2 == 1:
+                two = slice((c - 1) * CHUNK, (c + 1) * CHUNK)
+                nc.sync.dma_start(words_out[:, two], out_c[:, two].bitcast(I32))
+        for q in range(4):
+            nc.sync.dma_start(out_2[0, 4 * q : 4 * q + 4, :].bitcast(I32), out_s[32 * q : 32 * q + 4, :].bitcast(I32))

@@ -23,9 +23,9 @@ PASSES = K // (P * PACK)
 TOK = 128
 QUARTER = 256
 HALF = 512
-GATHERS = ((0, 256), (256, 512), (512, 1024))
+GATHERS = ((0, 512), (512, 1024))
 CHUNK = 256
-SPLIT = 64
+SPLIT = 80
 
 
 def tile_list_modp_gsilu_resP_kernel(
@@ -53,14 +53,16 @@ def tile_list_modp_gsilu_resP_kernel(
             nc.sync.dma_start(
                 tab_sc[32 * q + 24 : 32 * q + 32, :].bitcast(I32), tab_scales[:, 4 * q : 4 * q + 4, :].bitcast(I32)
             )
+        tab_w = keep([P, T], I32, "tab_w", "slot_w")
+        nc.sync.dma_start(tab_w[:], tab_words[0].rearrange("p t b -> p (t b)").bitcast(I32))
         wg_raw = [keep([P, PACK, R], F32, "wg_raw%d" % a, "slot_%s" % "ab"[a]) for a in range(PASSES)]
         for a in range(PASSES):
             nc.sync.dma_start(wg_raw[a][:], wg[512 * a : 512 * (a + 1), :].rearrange("(p j) r -> p j r", j=PACK))
-        tab_w = keep([P, T], I32, "tab_w", "slot_w")
-        nc.sync.dma_start(tab_w[:], tab_words[0].rearrange("p t b -> p (t b)").bitcast(I32))
+        wu_raw = keep([P, PASSES, R], I32, "wu_raw", "slot_d")
+        nc.sync.dma_start(wu_raw[:], wu_words.rearrange("a p r i -> p a (r i)").bitcast(I32))
 
         wu_sc_raw = keep([P, PASSES, R], U8, "wu_sc_raw")
-        v_sc = keep([P, PASSES, J], U8, "v_sc")
+        v_sc = [keep([P, J], U8, "v_sc%d" % a) for a in range(PASSES)]
         nc.vector.memset(wu_sc_raw[:].bitcast(I32), 0)
         for q in range(4):
             nc.vector.memset(tab_sc[32 * q : 32 * q + 24, :].bitcast(I32), 0)
@@ -68,29 +70,36 @@ def tile_list_modp_gsilu_resP_kernel(
         warm_out = keep([P, 8], F32, "warm_out")
         nc.vector.memset(warm[:], 0.0)
         nc.scalar.activation(warm_out[:], warm[:], SILU)
-        nc.vector.memset(v_sc[:].bitcast(I32), 0)
+        for a in range(PASSES):
+            nc.vector.memset(v_sc[a][96:128, :].bitcast(I32), 0)
         for q in range(4):
             nc.sync.dma_start(
                 wu_sc_raw[32 * q : 32 * q + 4, :, :].bitcast(I32),
                 wu_scales[:, 4 * q : 4 * q + 4, :].rearrange("a r n -> r a n").bitcast(I32),
             )
-        wu_raw = keep([P, PASSES, R], I32, "wu_raw", "slot_d")
-        nc.sync.dma_start(wu_raw[:], wu_words.rearrange("a p r i -> p a (r i)").bitcast(I32))
-        wd_raw = keep([P, 2 * N], U8, "wd_raw")
-        nc.sync.dma_start(wd_raw[:].bitcast(I32), wd_words[0].bitcast(I32))
 
-        picked_sc = keep([P, J], U8, "picked_sc", "slot_p")
+        picked_sc = keep([P, J], U8, "picked_sc")
         nc.vector.tensor_copy(picked_sc[:], tab_sc[:].indirect(offsets[:]))
         for a in range(PASSES):
-            nc.gpsimd.dma_start(
-                v_sc[0:100, a, :].bitcast(I32), picked_sc[24 + 4 * a : 124 + 4 * a, :].bitcast(I32)
-            )
+            nc.sync.dma_start(v_sc[a][0:100, :].bitcast(I32), picked_sc[24 + 4 * a : 124 + 4 * a, :].bitcast(I32))
+        rT_rows = rT.rearrange("(p i) t -> p i t", i=PACK)
+        res = [keep([P, T], F32, "res0", "slot_s")]
+        nc.sync.dma_start(res[0][:], rT_rows[:, 0, :])
 
-        wd_sc_raw = keep([P, N], U8, "wd_sc_raw", "slot_s")
-        nc.vector.memset(wd_sc_raw[:].bitcast(I32), 0)
+        v_w = []
+        for g, (j0, j1) in enumerate(GATHERS):
+            both = keep([P, j1 - j0], U32, "both%d" % g, "slot_g%d" % g)
+            nc.vector.tensor_copy(both[:], tab_w[:].bitcast(U32).indirect(listed(j0, j1)))
+            parted = keep([P, PASSES, 2 * (j1 - j0)], U8, "parted%d" % g, "slot_h%d" % g)
+            nc.vector.tensor_copy(parted[:].bitcast(U16), both[:].bitcast(U16).rearrange("p (j d) -> p d j", d=2))
+            v_w.append(parted)
+
+        wd_raw = keep([P, 3 * N], U8, "wd_raw", "slot_w")
+        nc.vector.memset(wd_raw[:, 2 * N :].bitcast(I32), 0)
+        nc.sync.dma_start(wd_raw[:, : 2 * N].bitcast(I32), wd_words[0].bitcast(I32))
         for q in range(4):
-            nc.gpsimd.dma_start(
-                wd_sc_raw[32 * q : 32 * q + 4, :].bitcast(I32), wd_scales[0, 4 * q : 4 * q + 4, :].bitcast(I32)
+            nc.sync.dma_start(
+                wd_raw[32 * q : 32 * q + 4, 2 * N :].bitcast(I32), wd_scales[0, 4 * q : 4 * q + 4, :].bitcast(I32)
             )
 
         wg_c, wg_s = [], []
@@ -109,32 +118,19 @@ def tile_list_modp_gsilu_resP_kernel(
             wg_c.append(codes)
             wg_s.append(scales)
 
-        rT_rows = rT.rearrange("(p i) t -> p i t", i=PACK)
-        res = [keep([P, T], F32, "res0", "slot_p")]
-        nc.sync.dma_start(res[0][:], rT_rows[:, 0, :])
         gate = keep([P, J], F32, "gate", "slot_a")
         nc.sync.dma_start(gate[:], wgo)
 
         wu_s = keep([P, PASSES, R], U8, "wu_s")
+        wu_c = keep([P, PASSES, R], I32, "wu_c", "slot_c")
+        nc.vector.tensor_copy(
+            wu_c[:].rearrange("p a (t m) -> p a m t", t=PACK), wu_raw[:].rearrange("p a (m t) -> p a m t", t=PACK)
+        )
         nc.vector.tensor_copy(
             wu_s[:].rearrange("p a (t m) -> p a m t", t=PACK), wu_sc_raw[:].rearrange("p a (m t) -> p a m t", t=PACK)
         )
 
-        v_w = []
-        wu_c = keep([P, PASSES, R], I32, "wu_c", "slot_c")
-        for g, (j0, j1) in enumerate(GATHERS):
-            both = keep([P, j1 - j0], U32, "both%d" % g, "slot_g%d" % g)
-            nc.vector.tensor_copy(both[:], tab_w[:].bitcast(U32).indirect(listed(j0, j1)))
-            parted = keep([P, PASSES, 2 * (j1 - j0)], U8, "parted%d" % g, "slot_h%d" % g)
-            nc.vector.tensor_copy(parted[:].bitcast(U16), both[:].bitcast(U16).rearrange("p (j d) -> p d j", d=2))
-            v_w.append(parted)
-            if g == 0:
-                nc.vector.tensor_copy(
-                    wu_c[:].rearrange("p a (t m) -> p a m t", t=PACK),
-                    wu_raw[:].rearrange("p a (m t) -> p a m t", t=PACK),
-                )
-
-        for i, slot in ((1, "slot_w"), (2, "slot_g2"), (3, "slot_h0")):
+        for i, slot in ((1, "slot_b"), (2, "slot_d"), (3, "slot_h0")):
             res.append(keep([P, T], F32, "res%d" % i, slot))
             nc.sync.dma_start(res[i][:], rT_rows[:, i, :])
 
@@ -142,19 +138,19 @@ def tile_list_modp_gsilu_resP_kernel(
         wd_s = keep([P, N], U8, "wd_s")
         nc.vector.tensor_copy(
             wd_c[:].bitcast(U16).rearrange("p (i m) -> p m i", i=PACK),
-            wd_raw[:].bitcast(U16).rearrange("p (m i) -> p m i", i=PACK),
+            wd_raw[:, : 2 * N].bitcast(U16).rearrange("p (m i) -> p m i", i=PACK),
         )
         nc.vector.tensor_copy(
-            wd_s[:].rearrange("p (i m) -> p m i", i=PACK), wd_sc_raw[:].rearrange("p (m i) -> p m i", i=PACK)
+            wd_s[:].rearrange("p (i m) -> p m i", i=PACK), wd_raw[:, 2 * N :].rearrange("p (m i) -> p m i", i=PACK)
         )
 
-        pages = [keep([P, T], F32, "page0", "slot_d")]
+        pages = [keep([P, T], F32, "page0", "slot_g1")]
         nc.vector.memset(pages[0][:], 0.0)
 
         def moving(a, j0):
             g = [x for x, (lo, hi) in enumerate(GATHERS) if lo <= j0 < hi][0]
             c = j0 - GATHERS[g][0]
-            return v_w[g][:, a, 2 * c : 2 * (c + TOK)].bitcast(FP4X4), v_sc[:, a, j0 : j0 + TOK]
+            return v_w[g][:, a, 2 * c : 2 * (c + TOK)].bitcast(FP4X4), v_sc[a][:, j0 : j0 + TOK]
 
         def stage1(bank, words, scales, j0):
             for t in range(PACK):
@@ -207,6 +203,9 @@ def tile_list_modp_gsilu_resP_kernel(
             stage2(0, cols.start, cols.stop)
             if q > 0:
                 place(0, cols.start - QUARTER, cols.start)
+        for i in range(1, PACK):
+            for j0 in range(0, J, HALF):
+                stage2(i, j0, j0 + HALF)
         place(0, J - QUARTER, J)
 
         out_rows = out_0.rearrange("(p i) t -> p i t", i=PACK)
@@ -215,9 +214,7 @@ def tile_list_modp_gsilu_resP_kernel(
         out_s = keep([P, T], U8, "out_s")
         for i in range(PACK):
             if i > 0:
-                for j0 in range(0, J, HALF):
-                    stage2(i, j0, j0 + HALF)
-                pages.append(keep([P, T], F32, "page%d" % i, "slot_%s" % "cpw"[i - 1]))
+                pages.append(keep([P, T], F32, "page%d" % i, "slot_%s" % "csb"[i - 1]))
                 nc.gpsimd.memset(pages[i][:], 0.0)
                 place(i, 0, J)
             nc.sync.dma_start(out_rows[:, i, :], pages[i][:])

@@ -24,8 +24,7 @@ TOK = 128
 QUARTER = 256
 HALF = 512
 GATHERS = ((0, 512), (512, 1024))
-CHUNK = 256
-SPLIT = 80
+CHUNK = 512
 
 
 def tile_list_modp_gsilu_resP_kernel(
@@ -61,7 +60,7 @@ def tile_list_modp_gsilu_resP_kernel(
         wu_raw = keep([P, PASSES, R], I32, "wu_raw", "slot_d")
         nc.sync.dma_start(wu_raw[:], wu_words.rearrange("a p r i -> p a (r i)").bitcast(I32))
 
-        wu_sc_raw = keep([P, PASSES, R], U8, "wu_sc_raw")
+        wu_sc_raw = keep([P, PASSES, R], U8, "wu_sc_raw", "slot_u")
         v_sc = [keep([P, J], U8, "v_sc%d" % a) for a in range(PASSES)]
         nc.vector.memset(wu_sc_raw[:].bitcast(I32), 0)
         for q in range(4):
@@ -104,14 +103,13 @@ def tile_list_modp_gsilu_resP_kernel(
 
         wg_c, wg_s = [], []
         for a in range(PASSES):
-            bf = keep([P, R * PACK], BF16, "wg_bf%d" % a)
+            bf = keep([P, R * PACK], BF16, "wg_bf%d" % a, "slot_f%d" % a)
             src = wg_raw[a][:].rearrange("p j (m t) -> p m j t", t=PACK)
             dst = bf[:].rearrange("p (t m j) -> p m j t", t=PACK, j=PACK)
             if a == 0:
                 nc.scalar.copy(dst, src)
             else:
-                nc.scalar.copy(dst[:, SPLIT:], src[:, SPLIT:])
-                nc.vector.tensor_copy(dst[:, :SPLIT], src[:, :SPLIT])
+                nc.vector.tensor_copy(dst, src)
             codes = keep([P, R], U32, "wg_c%d" % a)
             scales = keep([P, R], U8, "wg_s%d" % a)
             nc.vector.quantize_mx(codes[:].bitcast(FP8X4), scales[:], bf[:])
@@ -122,7 +120,7 @@ def tile_list_modp_gsilu_resP_kernel(
         nc.sync.dma_start(gate[:], wgo)
 
         wu_s = keep([P, PASSES, R], U8, "wu_s")
-        wu_c = keep([P, PASSES, R], I32, "wu_c", "slot_c")
+        wu_c = keep([P, PASSES, R], I32, "wu_c")
         nc.vector.tensor_copy(
             wu_c[:].rearrange("p a (t m) -> p a m t", t=PACK), wu_raw[:].rearrange("p a (m t) -> p a m t", t=PACK)
         )
@@ -130,7 +128,7 @@ def tile_list_modp_gsilu_resP_kernel(
             wu_s[:].rearrange("p a (t m) -> p a m t", t=PACK), wu_sc_raw[:].rearrange("p a (m t) -> p a m t", t=PACK)
         )
 
-        for i, slot in ((1, "slot_b"), (2, "slot_d"), (3, "slot_h0")):
+        for i, slot in ((1, "slot_b"), (2, "slot_u"), (3, "slot_h0")):
             res.append(keep([P, T], F32, "res%d" % i, slot))
             nc.sync.dma_start(res[i][:], rT_rows[:, i, :])
 
@@ -144,8 +142,9 @@ def tile_list_modp_gsilu_resP_kernel(
             wd_s[:].rearrange("p (i m) -> p m i", i=PACK), wd_raw[:, 2 * N :].rearrange("p (m i) -> p m i", i=PACK)
         )
 
-        pages = [keep([P, T], F32, "page0", "slot_g1")]
-        nc.vector.memset(pages[0][:], 0.0)
+        pages = [keep([P, T], F32, "page%d" % i, slot) for i, slot in enumerate((None, "slot_g1", "slot_d", "slot_f1"))]
+        for page in pages:
+            nc.vector.memset(page[:], 0.0)
 
         def moving(a, j0):
             g = [x for x, (lo, hi) in enumerate(GATHERS) if lo <= j0 < hi][0]
@@ -212,26 +211,27 @@ def tile_list_modp_gsilu_resP_kernel(
         woven = [keep([P, CHUNK, PACK], BF16, "woven%d" % c) for c in range(T // CHUNK)]
         out_c = keep([P, T], U32, "out_c")
         out_s = keep([P, T], U8, "out_s")
+        mid = CHUNK // 2
         for i in range(PACK):
             if i > 0:
-                pages.append(keep([P, T], F32, "page%d" % i, "slot_%s" % "csb"[i - 1]))
-                nc.gpsimd.memset(pages[i][:], 0.0)
                 place(i, 0, J)
             nc.sync.dma_start(out_rows[:, i, :], pages[i][:])
+            if i < 2:
+                for c in range(T // CHUNK):
+                    nc.scalar.copy(woven[c][:, :, i], pages[i][:, c * CHUNK : (c + 1) * CHUNK])
+                continue
             for c in range(T // CHUNK):
-                cols = slice(c * CHUNK, (c + 1) * CHUNK)
-                if i == 2 and c % 2 == 0:
-                    nc.scalar.copy(woven[c][:, :, 2:4], pages[i][:, cols].unsqueeze(2).to_broadcast([P, CHUNK, 2]))
-                elif i == 3 and c % 2 == 0:
-                    nc.vector.tensor_copy(woven[c][:, :, i], pages[i][:, cols])
+                low = pages[i][:, c * CHUNK : c * CHUNK + mid]
+                if i == 2:
+                    nc.scalar.copy(woven[c][:, :mid, 2:4], low.unsqueeze(2).to_broadcast([P, mid, 2]))
                 else:
-                    nc.scalar.copy(woven[c][:, :, i], pages[i][:, cols])
+                    nc.vector.tensor_copy(woven[c][:, :mid, i], low)
+            for c in range(T // CHUNK):
+                nc.scalar.copy(woven[c][:, mid:, i], pages[i][:, c * CHUNK + mid : (c + 1) * CHUNK])
         words_out = out_1[0].rearrange("p t b -> p (t b)").bitcast(I32)
         for c in range(T // CHUNK):
             cols = slice(c * CHUNK, (c + 1) * CHUNK)
             nc.vector.quantize_mx(out_c[:, cols].bitcast(FP8X4), out_s[:, cols], woven[c][:].rearrange("p t i -> p (t i)"))
-            if c % 2 == 1:
-                two = slice((c - 1) * CHUNK, (c + 1) * CHUNK)
-                nc.sync.dma_start(words_out[:, two], out_c[:, two].bitcast(I32))
+            nc.sync.dma_start(words_out[:, cols], out_c[:, cols].bitcast(I32))
         for q in range(4):
             nc.sync.dma_start(out_2[0, 4 * q : 4 * q + 4, :].bitcast(I32), out_s[32 * q : 32 * q + 4, :].bitcast(I32))

@@ -33,7 +33,6 @@ def tile_list_modp_gsilu_resP_kernel(
     nc = tc.nc
     with ExitStack() as ctx:
         held = ctx.enter_context(tc.tile_pool(name="held", bufs=1))
-        ring = ctx.enter_context(tc.tile_pool(name="ring", bufs=3))
         pair = ctx.enter_context(tc.tile_pool(name="pair", bufs=2))
         ps3 = ctx.enter_context(tc.psum_pool(name="ps3", bufs=3))
         ps2 = ctx.enter_context(tc.psum_pool(name="ps2", bufs=2))
@@ -104,8 +103,8 @@ def tile_list_modp_gsilu_resP_kernel(
         wg_c, wg_s = [], []
         for a in range(PASSES):
             bf = keep([P, R * PACK], BF16, "wg_bf%d" % a, "slot_f%d" % a)
-            src = wg_raw[a][:].rearrange("p j (m t) -> p m j t", t=PACK)
-            dst = bf[:].rearrange("p (t m j) -> p m j t", t=PACK, j=PACK)
+            src = wg_raw[a][:].rearrange("p j (m t) -> p m t j", t=PACK)
+            dst = bf[:].rearrange("p (t m j) -> p m t j", t=PACK, j=PACK)
             if a == 0:
                 nc.scalar.copy(dst, src)
             else:
@@ -122,10 +121,11 @@ def tile_list_modp_gsilu_resP_kernel(
         wu_s = keep([P, PASSES, R], U8, "wu_s")
         wu_c = keep([P, PASSES, R], I32, "wu_c")
         nc.vector.tensor_copy(
-            wu_c[:].rearrange("p a (t m) -> p a m t", t=PACK), wu_raw[:].rearrange("p a (m t) -> p a m t", t=PACK)
+            wu_c[:].rearrange("p a (t c m) -> p a c t m", t=PACK, m=4),
+            wu_raw[:].rearrange("p a (c m t) -> p a c t m", t=PACK, m=4),
         )
         nc.vector.tensor_copy(
-            wu_s[:].rearrange("p a (t m) -> p a m t", t=PACK), wu_sc_raw[:].rearrange("p a (m t) -> p a m t", t=PACK)
+            wu_s[:].rearrange("p a (t m) -> p a t m", t=PACK), wu_sc_raw[:].rearrange("p a (m t) -> p a t m", t=PACK)
         )
 
         for i, slot in ((1, "slot_b"), (2, "slot_u"), (3, "slot_h0")):
@@ -135,11 +135,11 @@ def tile_list_modp_gsilu_resP_kernel(
         wd_c = keep([P, 2 * N], U8, "wd_c")
         wd_s = keep([P, N], U8, "wd_s")
         nc.vector.tensor_copy(
-            wd_c[:].bitcast(U16).rearrange("p (i m) -> p m i", i=PACK),
-            wd_raw[:, : 2 * N].bitcast(U16).rearrange("p (m i) -> p m i", i=PACK),
+            wd_c[:].bitcast(U16).rearrange("p (i m) -> p i m", i=PACK),
+            wd_raw[:, : 2 * N].bitcast(U16).rearrange("p (m i) -> p i m", i=PACK),
         )
         nc.vector.tensor_copy(
-            wd_s[:].rearrange("p (i m) -> p m i", i=PACK), wd_raw[:, 2 * N :].rearrange("p (m i) -> p m i", i=PACK)
+            wd_s[:].rearrange("p (i m) -> p i m", i=PACK), wd_raw[:, 2 * N :].rearrange("p (m i) -> p i m", i=PACK)
         )
 
         pages = [keep([P, T], F32, "page%d" % i, slot) for i, slot in enumerate((None, "slot_g1", "slot_d", "slot_f1"))]
@@ -173,10 +173,16 @@ def tile_list_modp_gsilu_resP_kernel(
             )
             nc.scalar.copy(y[i][:, j0:j1], bank[:, : j1 - j0])
 
+        def pick(z, i, j0, j1):
+            nc.vector.tensor_tensor(z[:], res[i][:].indirect(listed(j0, j1)), y[i][:, j0:j1], ADD)
+
+        def put(z, i, j0, j1):
+            nc.vector.tensor_tensor(pages[i][:].indirect(listed(j0, j1)), z[:], gate[:, j0:j1], MULT)
+
         def place(i, j0, j1):
-            z = pair.tile([P, J], F32, name="z")
-            nc.vector.tensor_tensor(z[:, : j1 - j0], res[i][:].indirect(listed(j0, j1)), y[i][:, j0:j1], ADD)
-            nc.vector.tensor_tensor(pages[i][:].indirect(listed(j0, j1)), z[:, : j1 - j0], gate[:, j0:j1], MULT)
+            z = pair.tile([P, j1 - j0], F32, name="z")
+            pick(z, i, j0, j1)
+            put(z, i, j0, j1)
 
         for q in range(J // QUARTER):
             h_bf = pair.tile([P, QUARTER, PACK], BF16, name="h_bf", align_bytes=64)
@@ -192,23 +198,28 @@ def tile_list_modp_gsilu_resP_kernel(
                     u_bank, lambda a, t: wu_c[:, a, P * t : P * (t + 1)].bitcast(FP8X4),
                     lambda a, t: wu_s[:, a, P * t : P * (t + 1)], j0,
                 )
-                act = ring.tile([P, TOK, PACK], F32, name="act")
+                act = keep([P, TOK, PACK], F32, "act%d" % (j0 // TOK))
                 nc.scalar.activation(act[:], g_bank[:].rearrange("p t j -> p j t"), SILU)
                 nc.vector.tensor_tensor(
                     h_bf[:, c * TOK : (c + 1) * TOK, :], u_bank[:].rearrange("p t j -> p j t"), act[:], MULT
                 )
             cols = slice(q * QUARTER, (q + 1) * QUARTER)
+            if q > 0:
+                z = keep([P, QUARTER], F32, "z%d" % q, "act%d" % (2 * q + 1))
+                pick(z, 0, cols.start - QUARTER, cols.start)
             nc.vector.quantize_mx(h_c[:, cols].bitcast(FP8X4), h_s[:, cols], h_bf[:].rearrange("p j t -> p (j t)"))
             stage2(0, cols.start, cols.stop)
             if q > 0:
-                place(0, cols.start - QUARTER, cols.start)
+                put(z, 0, cols.start - QUARTER, cols.start)
         for i in range(1, PACK):
             for j0 in range(0, J, HALF):
                 stage2(i, j0, j0 + HALF)
         place(0, J - QUARTER, J)
 
         out_rows = out_0.rearrange("(p i) t -> p i t", i=PACK)
-        woven = [keep([P, CHUNK, PACK], BF16, "woven%d" % c) for c in range(T // CHUNK)]
+        woven = [
+            keep([P, CHUNK, PACK], BF16, "woven%d" % c, slot) for c, slot in enumerate(("h_c", "h_s", "wd_c", "wd_s"))
+        ]
         out_c = keep([P, T], U32, "out_c")
         out_s = keep([P, T], U8, "out_s")
         mid = CHUNK // 2

@@ -25,6 +25,7 @@ QUARTER = 256
 HALF = 512
 GATHERS = ((0, 512), (512, 1024))
 CHUNK = 512
+ORDER = (0, 2, 1, 3)
 
 
 def tile_list_modp_gsilu_resP_kernel(
@@ -53,15 +54,22 @@ def tile_list_modp_gsilu_resP_kernel(
             )
         tab_w = keep([P, T], I32, "tab_w", "slot_w")
         nc.sync.dma_start(tab_w[:], tab_words[0].rearrange("p t b -> p (t b)").bitcast(I32))
-        wg_raw = [keep([P, PACK, R], F32, "wg_raw%d" % a, "slot_%s" % "ab"[a]) for a in range(PASSES)]
-        for a in range(PASSES):
-            nc.sync.dma_start(wg_raw[a][:], wg[512 * a : 512 * (a + 1), :].rearrange("(p j) r -> p j r", j=PACK))
-        wu_raw = keep([P, PASSES, R], I32, "wu_raw", "slot_d")
+        wg_raw = {}
+
+        def load_wg(a, s):
+            wg_raw[a, s] = keep([P, PACK, R // 2], F32, "wg_raw%d%d" % (a, s))
+            rows = wg[512 * a : 512 * (a + 1), s * (R // 2) : (s + 1) * (R // 2)]
+            nc.sync.dma_start(wg_raw[a, s][:], rows.rearrange("(p j) r -> p j r", j=PACK))
+
+        load_wg(0, 0)
+        wu_raw = keep([P, PASSES, R], I32, "wu_raw")
         nc.sync.dma_start(wu_raw[:], wu_words.rearrange("a p r i -> p a (r i)").bitcast(I32))
 
-        wu_sc_raw = keep([P, PASSES, R], U8, "wu_sc_raw", "slot_u")
+        wu_sc_raw = keep([P, PASSES, R], U8, "wu_sc_raw")
         v_sc = [keep([P, J], U8, "v_sc%d" % a) for a in range(PASSES)]
         nc.vector.memset(wu_sc_raw[:].bitcast(I32), 0)
+        wd_raw = keep([P, 3 * N], U8, "wd_raw")
+        nc.vector.memset(wd_raw[:, 2 * N :].bitcast(I32), 0)
         for q in range(4):
             nc.vector.memset(tab_sc[32 * q : 32 * q + 24, :].bitcast(I32), 0)
         warm = keep([P, 8], F32, "warm")
@@ -75,14 +83,15 @@ def tile_list_modp_gsilu_resP_kernel(
                 wu_sc_raw[32 * q : 32 * q + 4, :, :].bitcast(I32),
                 wu_scales[:, 4 * q : 4 * q + 4, :].rearrange("a r n -> r a n").bitcast(I32),
             )
+        load_wg(0, 1)
+        load_wg(1, 0)
+        load_wg(1, 1)
 
         picked_sc = keep([P, J], U8, "picked_sc")
         nc.vector.tensor_copy(picked_sc[:], tab_sc[:].indirect(offsets[:]))
         for a in range(PASSES):
             nc.sync.dma_start(v_sc[a][0:100, :].bitcast(I32), picked_sc[24 + 4 * a : 124 + 4 * a, :].bitcast(I32))
         rT_rows = rT.rearrange("(p i) t -> p i t", i=PACK)
-        res = [keep([P, T], F32, "res0", "slot_s")]
-        nc.sync.dma_start(res[0][:], rT_rows[:, 0, :])
 
         v_w = []
         for g, (j0, j1) in enumerate(GATHERS):
@@ -92,31 +101,33 @@ def tile_list_modp_gsilu_resP_kernel(
             nc.vector.tensor_copy(parted[:].bitcast(U16), both[:].bitcast(U16).rearrange("p (j d) -> p d j", d=2))
             v_w.append(parted)
 
-        wd_raw = keep([P, 3 * N], U8, "wd_raw", "slot_w")
-        nc.vector.memset(wd_raw[:, 2 * N :].bitcast(I32), 0)
         nc.sync.dma_start(wd_raw[:, : 2 * N].bitcast(I32), wd_words[0].bitcast(I32))
         for q in range(4):
             nc.sync.dma_start(
                 wd_raw[32 * q : 32 * q + 4, 2 * N :].bitcast(I32), wd_scales[0, 4 * q : 4 * q + 4, :].bitcast(I32)
             )
 
+        res = {}
+        gate = keep([P, J], F32, "gate", "wg_raw00")
+        for i, slot in zip(ORDER, ("slot_s", "slot_w", "wg_raw01", "wg_raw10")):
+            res[i] = keep([P, T], F32, "res%d" % i, slot)
+            nc.sync.dma_start(res[i][:], rT_rows[:, i, :])
+            if i == ORDER[0]:
+                nc.sync.dma_start(gate[:], wgo)
+
         wg_c, wg_s = [], []
-        for a in range(PASSES):
+
+        def quantise_wg(a):
             bf = keep([P, R * PACK], BF16, "wg_bf%d" % a, "slot_f%d" % a)
-            src = wg_raw[a][:].rearrange("p j (m t) -> p m t j", t=PACK)
             dst = bf[:].rearrange("p (t m j) -> p m t j", t=PACK, j=PACK)
-            if a == 0:
-                nc.scalar.copy(dst, src)
-            else:
-                nc.vector.tensor_copy(dst, src)
-            codes = keep([P, R], U32, "wg_c%d" % a)
-            scales = keep([P, R], U8, "wg_s%d" % a)
+            for s in range(2):
+                src = wg_raw[a, s][:].rearrange("p j (m t) -> p m t j", t=PACK)
+                nc.scalar.copy(dst[:, 64 * s : 64 * (s + 1)], src)
+            codes = keep([P, R], U32, "wg_c%d" % a, "wu_raw" if a == 0 else None)
+            scales = keep([P, R], U8, "wg_s%d" % a, "wu_sc_raw" if a == 0 else None)
             nc.vector.quantize_mx(codes[:].bitcast(FP8X4), scales[:], bf[:])
             wg_c.append(codes)
             wg_s.append(scales)
-
-        gate = keep([P, J], F32, "gate", "slot_a")
-        nc.sync.dma_start(gate[:], wgo)
 
         wu_s = keep([P, PASSES, R], U8, "wu_s")
         wu_c = keep([P, PASSES, R], I32, "wu_c")
@@ -128,12 +139,14 @@ def tile_list_modp_gsilu_resP_kernel(
             wu_s[:].rearrange("p a (t m) -> p a t m", t=PACK), wu_sc_raw[:].rearrange("p a (m t) -> p a t m", t=PACK)
         )
 
-        for i, slot in ((1, "slot_b"), (2, "slot_u"), (3, "slot_h0")):
-            res.append(keep([P, T], F32, "res%d" % i, slot))
-            nc.sync.dma_start(res[i][:], rT_rows[:, i, :])
-
-        wd_c = keep([P, 2 * N], U8, "wd_c")
-        wd_s = keep([P, N], U8, "wd_s")
+        two = [keep([P, T], F32, "page0")]
+        nc.vector.memset(two[0][:], 0.0)
+        quantise_wg(0)
+        quantise_wg(1)
+        two.append(keep([P, T], F32, "page1", "slot_f1"))
+        nc.vector.memset(two[1][:], 0.0)
+        wd_c = keep([P, 2 * N], U8, "wd_c", "slot_f0")
+        wd_s = keep([P, N], U8, "wd_s", "wg_raw11")
         nc.vector.tensor_copy(
             wd_c[:].bitcast(U16).rearrange("p (i m) -> p i m", i=PACK),
             wd_raw[:, : 2 * N].bitcast(U16).rearrange("p (m i) -> p i m", i=PACK),
@@ -142,9 +155,7 @@ def tile_list_modp_gsilu_resP_kernel(
             wd_s[:].rearrange("p (i m) -> p i m", i=PACK), wd_raw[:, 2 * N :].rearrange("p (m i) -> p i m", i=PACK)
         )
 
-        pages = [keep([P, T], F32, "page%d" % i, slot) for i, slot in enumerate((None, "slot_g1", "slot_d", "slot_f1"))]
-        for page in pages:
-            nc.vector.memset(page[:], 0.0)
+        pages = [two[i // 2] for i in range(PACK)]
 
         def moving(a, j0):
             g = [x for x, (lo, hi) in enumerate(GATHERS) if lo <= j0 < hi][0]
@@ -191,12 +202,12 @@ def tile_list_modp_gsilu_resP_kernel(
                 g_bank = ps3.tile([P, PACK, TOK], F32, name="g_bank")
                 u_bank = ps3.tile([P, PACK, TOK], F32, name="u_bank")
                 stage1(
-                    g_bank, lambda a, t: wg_c[a][:, P * t : P * (t + 1)].bitcast(FP8X4),
-                    lambda a, t: wg_s[a][:, P * t : P * (t + 1)], j0,
-                )
-                stage1(
                     u_bank, lambda a, t: wu_c[:, a, P * t : P * (t + 1)].bitcast(FP8X4),
                     lambda a, t: wu_s[:, a, P * t : P * (t + 1)], j0,
+                )
+                stage1(
+                    g_bank, lambda a, t: wg_c[a][:, P * t : P * (t + 1)].bitcast(FP8X4),
+                    lambda a, t: wg_s[a][:, P * t : P * (t + 1)], j0,
                 )
                 act = keep([P, TOK, PACK], F32, "act%d" % (j0 // TOK))
                 nc.scalar.activation(act[:], g_bank[:].rearrange("p t j -> p j t"), SILU)
@@ -211,32 +222,28 @@ def tile_list_modp_gsilu_resP_kernel(
             stage2(0, cols.start, cols.stop)
             if q > 0:
                 put(z, 0, cols.start - QUARTER, cols.start)
-        for i in range(1, PACK):
+        for i in ORDER[1:]:
             for j0 in range(0, J, HALF):
                 stage2(i, j0, j0 + HALF)
         place(0, J - QUARTER, J)
 
         out_rows = out_0.rearrange("(p i) t -> p i t", i=PACK)
         woven = [
-            keep([P, CHUNK, PACK], BF16, "woven%d" % c, slot) for c, slot in enumerate(("h_c", "h_s", "wd_c", "wd_s"))
+            keep([P, CHUNK, PACK], BF16, "woven%d" % c, slot) for c, slot in enumerate(("h_c", "h_s", "slot_f0", "wg_raw11"))
         ]
         out_c = keep([P, T], U32, "out_c")
         out_s = keep([P, T], U8, "out_s")
         mid = CHUNK // 2
-        for i in range(PACK):
+        for i in ORDER:
             if i > 0:
                 place(i, 0, J)
             nc.sync.dma_start(out_rows[:, i, :], pages[i][:])
-            if i < 2:
+            if i != ORDER[-1]:
                 for c in range(T // CHUNK):
                     nc.scalar.copy(woven[c][:, :, i], pages[i][:, c * CHUNK : (c + 1) * CHUNK])
                 continue
             for c in range(T // CHUNK):
-                low = pages[i][:, c * CHUNK : c * CHUNK + mid]
-                if i == 2:
-                    nc.scalar.copy(woven[c][:, :mid, 2:4], low.unsqueeze(2).to_broadcast([P, mid, 2]))
-                else:
-                    nc.vector.tensor_copy(woven[c][:, :mid, i], low)
+                nc.vector.tensor_copy(woven[c][:, :mid, i], pages[i][:, c * CHUNK : c * CHUNK + mid])
             for c in range(T // CHUNK):
                 nc.scalar.copy(woven[c][:, mid:, i], pages[i][:, c * CHUNK + mid : (c + 1) * CHUNK])
         words_out = out_1[0].rearrange("p t b -> p (t b)").bitcast(I32)

@@ -1,6 +1,7 @@
 from contextlib import ExitStack
 
 import concourse.mybir as mybir
+from concourse.masks import make_identity
 
 K, R, N, T, J = 1024, 512, 512, 2048, 1024
 FLOPS = 2 * J * (2 * K * R + R * N)
@@ -16,6 +17,7 @@ FP4X4 = mybir.dt.float4_e2m1fn_x4
 MULT = mybir.AluOpType.mult
 ADD = mybir.AluOpType.add
 SILU = mybir.ActivationFunctionType.Silu
+COPY = mybir.ActivationFunctionType.Copy
 
 P = 128
 PACK = 4
@@ -25,7 +27,7 @@ QUARTER = 256
 HALF = 512
 GATHERS = ((0, 512), (512, 1024))
 CHUNK = 512
-ORDER = (0, 2, 1, 3)
+ORDER = (0, 2, 3, 1)
 
 
 def tile_list_modp_gsilu_resP_kernel(
@@ -35,8 +37,8 @@ def tile_list_modp_gsilu_resP_kernel(
     with ExitStack() as ctx:
         held = ctx.enter_context(tc.tile_pool(name="held", bufs=1))
         pair = ctx.enter_context(tc.tile_pool(name="pair", bufs=2))
-        ps3 = ctx.enter_context(tc.psum_pool(name="ps3", bufs=3))
         ps2 = ctx.enter_context(tc.psum_pool(name="ps2", bufs=2))
+        ps3 = ctx.enter_context(tc.psum_pool(name="ps3", bufs=3))
 
         def keep(shape, dtype, name, tag=None):
             return held.tile(shape, dtype, name=name, tag=tag or name, align_bytes=64)
@@ -48,10 +50,9 @@ def tile_list_modp_gsilu_resP_kernel(
             return offsets[:, j0 // 16 : j1 // 16]
 
         tab_sc = keep([P, T], U8, "tab_sc", "slot_s")
-        for q in range(4):
-            nc.sync.dma_start(
-                tab_sc[32 * q + 24 : 32 * q + 32, :].bitcast(I32), tab_scales[:, 4 * q : 4 * q + 4, :].bitcast(I32)
-            )
+        sc_rows = tab_scales.rearrange("a (h u r) t -> u (a h) r t", h=2, u=2)
+        for u in range(2):
+            nc.sync.dma_start(tab_sc[32 * u + 16 : 32 * u + 32, :].bitcast(I32), sc_rows[u].bitcast(I32))
         tab_w = keep([P, T], I32, "tab_w", "slot_w")
         nc.sync.dma_start(tab_w[:], tab_words[0].rearrange("p t b -> p (t b)").bitcast(I32))
         wg_raw = {}
@@ -62,35 +63,41 @@ def tile_list_modp_gsilu_resP_kernel(
             nc.sync.dma_start(wg_raw[a, s][:], rows.rearrange("(p j) r -> p j r", j=PACK))
 
         load_wg(0, 0)
+        load_wg(0, 1)
         wu_raw = keep([P, PASSES, R], I32, "wu_raw")
         nc.sync.dma_start(wu_raw[:], wu_words.rearrange("a p r i -> p a (r i)").bitcast(I32))
 
         wu_sc_raw = keep([P, PASSES, R], U8, "wu_sc_raw")
         v_sc = [keep([P, J], U8, "v_sc%d" % a) for a in range(PASSES)]
+        w_rows = keep([P, P], F32, "w_rows")
         nc.vector.memset(wu_sc_raw[:].bitcast(I32), 0)
-        wd_raw = keep([P, 3 * N], U8, "wd_raw")
-        nc.vector.memset(wd_raw[:, 2 * N :].bitcast(I32), 0)
-        for q in range(4):
-            nc.vector.memset(tab_sc[32 * q : 32 * q + 24, :].bitcast(I32), 0)
+        nc.vector.memset(w_rows[:], 0.0)
+        ident = keep([P, P], F32, "ident")
+        make_identity(nc, ident[:])
+        z = {i: keep([P, J], F32, "z%d" % i) for i in ORDER[:3]}
+        nc.vector.memset(z[ORDER[0]][:, HALF : HALF + 1], 0.0)
+        nc.vector.memset(z[ORDER[1]][:, 0:J:HALF], 0.0)
+        for lo, hi in ((0, 16), (32, 48), (64, 128)):
+            nc.vector.memset(tab_sc[lo:hi, :].bitcast(I32), 0)
         warm = keep([P, 8], F32, "warm")
         warm_out = keep([P, 8], F32, "warm_out")
         nc.vector.memset(warm[:], 0.0)
         nc.scalar.activation(warm_out[:], warm[:], SILU)
-        for a in range(PASSES):
-            nc.vector.memset(v_sc[a][96:128, :].bitcast(I32), 0)
         for q in range(4):
-            nc.sync.dma_start(
+            nc.gpsimd.dma_start(
                 wu_sc_raw[32 * q : 32 * q + 4, :, :].bitcast(I32),
                 wu_scales[:, 4 * q : 4 * q + 4, :].rearrange("a r n -> r a n").bitcast(I32),
             )
-        load_wg(0, 1)
+        nc.gpsimd.dma_start(w_rows[0 : J // P, :], wgo[0].rearrange("(c j) -> c j", j=P))
         load_wg(1, 0)
         load_wg(1, 1)
 
         picked_sc = keep([P, J], U8, "picked_sc")
         nc.vector.tensor_copy(picked_sc[:], tab_sc[:].indirect(offsets[:]))
         for a in range(PASSES):
-            nc.sync.dma_start(v_sc[a][0:100, :].bitcast(I32), picked_sc[24 + 4 * a : 124 + 4 * a, :].bitcast(I32))
+            for h in range(2):
+                lo = 16 + 8 * a + 4 * h
+                nc.scalar.dma_start(v_sc[a][64 * h : 64 * h + 64, :].bitcast(I32), picked_sc[lo : lo + 64, :].bitcast(I32))
         rT_rows = rT.rearrange("(p i) t -> p i t", i=PACK)
 
         v_w = []
@@ -101,19 +108,23 @@ def tile_list_modp_gsilu_resP_kernel(
             nc.vector.tensor_copy(parted[:].bitcast(U16), both[:].bitcast(U16).rearrange("p (j d) -> p d j", d=2))
             v_w.append(parted)
 
-        nc.sync.dma_start(wd_raw[:, : 2 * N].bitcast(I32), wd_words[0].bitcast(I32))
-        for q in range(4):
-            nc.sync.dma_start(
-                wd_raw[32 * q : 32 * q + 4, 2 * N :].bitcast(I32), wd_scales[0, 4 * q : 4 * q + 4, :].bitcast(I32)
-            )
-
         res = {}
-        gate = keep([P, J], F32, "gate", "wg_raw00")
-        for i, slot in zip(ORDER, ("slot_s", "slot_w", "wg_raw01", "wg_raw10")):
+
+        def load_res(i, slot):
             res[i] = keep([P, T], F32, "res%d" % i, slot)
             nc.sync.dma_start(res[i][:], rT_rows[:, i, :])
-            if i == ORDER[0]:
-                nc.sync.dma_start(gate[:], wgo)
+
+        gate = keep([P, J], F32, "gate", "slot_s")
+        nc.sync.dma_start(gate[:], wgo)
+        load_res(ORDER[0], "slot_w")
+        wd_w = keep([P, 2 * N], U8, "wd_w", "wg_raw00")
+        nc.sync.dma_start(wd_w[:].bitcast(I32), wd_words[0].bitcast(I32))
+        wd_s = keep([P, N], U8, "wd_s", "wg_raw01")
+        nc.vector.memset(wd_s[:].bitcast(I32), 0)
+        for q in range(4):
+            nc.sync.dma_start(wd_s[32 * q : 32 * q + 4, :].bitcast(I32), wd_scales[0, 4 * q : 4 * q + 4, :].bitcast(I32))
+        load_res(ORDER[1], "wg_raw10")
+        load_res(ORDER[2], "wg_raw11")
 
         wg_c, wg_s = [], []
 
@@ -139,23 +150,19 @@ def tile_list_modp_gsilu_resP_kernel(
             wu_s[:].rearrange("p a (t m) -> p a t m", t=PACK), wu_sc_raw[:].rearrange("p a (m t) -> p a t m", t=PACK)
         )
 
-        two = [keep([P, T], F32, "page0")]
-        nc.vector.memset(two[0][:], 0.0)
+        three = [keep([P, T], F32, "page0")]
+        nc.vector.memset(three[0][:], 0.0)
         quantise_wg(0)
         quantise_wg(1)
-        two.append(keep([P, T], F32, "page1", "slot_f1"))
-        nc.vector.memset(two[1][:], 0.0)
-        wd_c = keep([P, 2 * N], U8, "wd_c", "slot_f0")
-        wd_s = keep([P, N], U8, "wd_s", "wg_raw11")
-        nc.vector.tensor_copy(
-            wd_c[:].bitcast(U16).rearrange("p (i m) -> p i m", i=PACK),
-            wd_raw[:, : 2 * N].bitcast(U16).rearrange("p (m i) -> p i m", i=PACK),
-        )
-        nc.vector.tensor_copy(
-            wd_s[:].rearrange("p (i m) -> p i m", i=PACK), wd_raw[:, 2 * N :].rearrange("p (m i) -> p i m", i=PACK)
-        )
+        load_res(ORDER[3], "slot_f1")
+        three.append(keep([P, T], F32, "page1", "warm"))
+        nc.gpsimd.memset(three[1][:], 0.0)
+        pages = {ORDER[0]: three[0], ORDER[1]: three[1], ORDER[3]: three[0]}
 
-        pages = [two[i // 2] for i in range(PACK)]
+        w_bank = ps3.tile([P, PACK, TOK], F32, name="w_bank", tag="late")
+        nc.tensor.transpose(w_bank[:, 0, :], w_rows[:], ident[:])
+        w_col = keep([P, J // P], F32, "w_col")
+        nc.scalar.copy(w_col[:], w_bank[:, 0, 0 : J // P])
 
         def moving(a, j0):
             g = [x for x, (lo, hi) in enumerate(GATHERS) if lo <= j0 < hi][0]
@@ -173,33 +180,48 @@ def tile_list_modp_gsilu_resP_kernel(
 
         h_c = keep([P, J], U32, "h_c")
         h_s = keep([P, J], U8, "h_s")
-        y = [keep([P, J], F32, "y%d" % i) for i in range(PACK)]
+        yw = keep([P, PACK, J], F32, "yw")
 
-        def stage2(i, j0, j1):
-            bank = ps2.tile([P, HALF], F32, name="y_bank")
+        def stage2(j0):
+            bank = ps3.tile([P, N], F32, name="y_bank", tag="late")
             nc.tensor.matmul_mx(
-                bank[:, : j1 - j0],
-                lhsT=wd_c[:, 2 * P * i : 2 * P * (i + 1)].bitcast(FP4X4), lhsT_scale=wd_s[:, P * i : P * (i + 1)],
-                rhs=h_c[:, j0:j1].bitcast(FP8X4), rhs_scale=h_s[:, j0:j1], start=True, stop=True,
+                bank[:], lhsT=h_c[:, j0 : j0 + TOK].bitcast(FP8X4), lhsT_scale=h_s[:, j0 : j0 + TOK],
+                rhs=wd_w[:].bitcast(FP4X4), rhs_scale=wd_s[:], start=True, stop=True,
             )
-            nc.scalar.copy(y[i][:, j0:j1], bank[:, : j1 - j0])
+            ys = pair.tile([P, PACK, P], F32, name="ys")
+            c = j0 // TOK
+            nc.scalar.activation(ys[:], bank[:].rearrange("p (m i) -> p i m", i=PACK), COPY, scale=w_col[:, c : c + 1])
+            return ys
 
-        def pick(z, i, j0, j1):
-            nc.vector.tensor_tensor(z[:], res[i][:].indirect(listed(j0, j1)), y[i][:, j0:j1], ADD)
+        def turn(ys, j0):
+            bank = ps3.tile([P, PACK, TOK], F32, name="t_bank", tag="late")
+            for i in range(PACK):
+                nc.tensor.transpose(bank[:, i, :], ys[:, i, :], ident[:])
+            nc.scalar.copy(yw[:, :, j0 : j0 + TOK], bank[:])
 
-        def put(z, i, j0, j1):
-            nc.vector.tensor_tensor(pages[i][:].indirect(listed(j0, j1)), z[:], gate[:, j0:j1], MULT)
+        def second_product(q):
+            made = [(stage2(j0), j0) for j0 in range(q * QUARTER, (q + 1) * QUARTER, TOK)]
+            for ys, j0 in made:
+                turn(ys, j0)
 
-        def place(i, j0, j1):
-            z = pair.tile([P, j1 - j0], F32, name="z")
-            pick(z, i, j0, j1)
-            put(z, i, j0, j1)
+        def pick(i, j0, j1):
+            nc.vector.tensor_tensor(z[i][:, j0:j1], res[i][:].indirect(listed(j0, j1)), gate[:, j0:j1], MULT)
 
-        for q in range(J // QUARTER):
-            h_bf = pair.tile([P, QUARTER, PACK], BF16, name="h_bf", align_bytes=64)
+        def put(i, j0, j1):
+            nc.vector.tensor_tensor(pages[i][:].indirect(listed(j0, j1)), z[i][:, j0:j1], yw[:, i, j0:j1], ADD)
+
+        first, second, third, last = ORDER
+        picks = {2: (first, HALF), 4: (second, 0), 6: (second, HALF)}
+        quarters = J // QUARTER
+        pick(first, 0, HALF)
+        for q in range(quarters):
+            if q < quarters - 1:
+                h_bf = pair.tile([P, QUARTER * PACK], BF16, name="h_bf", align_bytes=64)[:]
+            else:
+                h_bf = z[third][:, QUARTER : J - QUARTER].bitcast(BF16)
             for c in range(QUARTER // TOK):
                 j0 = q * QUARTER + c * TOK
-                g_bank = ps3.tile([P, PACK, TOK], F32, name="g_bank")
+                g_bank = ps2.tile([P, PACK, TOK], F32, name="g_bank")
                 u_bank = ps3.tile([P, PACK, TOK], F32, name="u_bank")
                 stage1(
                     u_bank, lambda a, t: wu_c[:, a, P * t : P * (t + 1)].bitcast(FP8X4),
@@ -209,34 +231,47 @@ def tile_list_modp_gsilu_resP_kernel(
                     g_bank, lambda a, t: wg_c[a][:, P * t : P * (t + 1)].bitcast(FP8X4),
                     lambda a, t: wg_s[a][:, P * t : P * (t + 1)], j0,
                 )
-                act = keep([P, TOK, PACK], F32, "act%d" % (j0 // TOK))
-                nc.scalar.activation(act[:], g_bank[:].rearrange("p t j -> p j t"), SILU)
+                act = pair.tile([P, TOK, PACK], F32, name="act")
+                tile_no = j0 // TOK
+                if tile_no in picks:
+                    i, lo = picks[tile_no]
+                    nc.scalar.activation(act[:], g_bank[:].rearrange("p t j -> p j t"), SILU, bias=z[i][:, lo : lo + 1])
+                else:
+                    nc.scalar.activation(act[:], g_bank[:].rearrange("p t j -> p j t"), SILU)
                 nc.vector.tensor_tensor(
-                    h_bf[:, c * TOK : (c + 1) * TOK, :], u_bank[:].rearrange("p t j -> p j t"), act[:], MULT
+                    h_bf[:, c * TOK * PACK : (c + 1) * TOK * PACK].rearrange("p (j t) -> p j t", t=PACK),
+                    u_bank[:].rearrange("p t j -> p j t"), act[:], MULT,
                 )
-            cols = slice(q * QUARTER, (q + 1) * QUARTER)
+                if c == QUARTER // TOK - 1:
+                    cols = slice(q * QUARTER, (q + 1) * QUARTER)
+                    nc.vector.quantize_mx(h_c[:, cols].bitcast(FP8X4), h_s[:, cols], h_bf)
+                if tile_no in picks:
+                    pick(i, lo, lo + HALF)
             if q > 0:
-                z = keep([P, QUARTER], F32, "z%d" % q, "act%d" % (2 * q + 1))
-                pick(z, 0, cols.start - QUARTER, cols.start)
-            nc.vector.quantize_mx(h_c[:, cols].bitcast(FP8X4), h_s[:, cols], h_bf[:].rearrange("p j t -> p (j t)"))
-            stage2(0, cols.start, cols.stop)
-            if q > 0:
-                put(z, 0, cols.start - QUARTER, cols.start)
-        for i in ORDER[1:]:
-            for j0 in range(0, J, HALF):
-                stage2(i, j0, j0 + HALF)
-        place(0, J - QUARTER, J)
+                second_product(q - 1)
+            if 0 < q < quarters - 1:
+                put(first, cols.start - QUARTER, cols.start)
+        second_product(quarters - 1)
+        pick(third, 0, HALF)
+        put(first, J - HALF, J - QUARTER)
+        pick(third, HALF, J)
+        put(first, J - QUARTER, J)
+        pages[third] = keep([P, T], F32, "page2", "z%d" % first)
+        nc.gpsimd.memset(pages[third][:], 0.0)
 
         out_rows = out_0.rearrange("(p i) t -> p i t", i=PACK)
         woven = [
-            keep([P, CHUNK, PACK], BF16, "woven%d" % c, slot) for c, slot in enumerate(("h_c", "h_s", "slot_f0", "wg_raw11"))
+            keep([P, CHUNK, PACK], BF16, "woven%d" % c, slot) for c, slot in enumerate(("h_c", "h_s", "slot_h0", "slot_h1"))
         ]
         out_c = keep([P, T], U32, "out_c")
         out_s = keep([P, T], U8, "out_s")
         mid = CHUNK // 2
         for i in ORDER:
-            if i > 0:
-                place(i, 0, J)
+            if i == last:
+                z[i] = keep([P, J], F32, "z%d" % i, "z%d" % second)
+                pick(i, 0, J)
+            if i != first:
+                put(i, 0, J)
             nc.sync.dma_start(out_rows[:, i, :], pages[i][:])
             if i != ORDER[-1]:
                 for c in range(T // CHUNK):

@@ -53,6 +53,13 @@ def tile_list_modp_gsilu_resP_kernel(
         sc_rows = tab_scales.rearrange("a (h u r) t -> u (a h) r t", h=2, u=2)
         for u in range(2):
             nc.sync.dma_start(tab_sc[32 * u + 16 : 32 * u + 32, :].bitcast(I32), sc_rows[u].bitcast(I32))
+        wu_sc_raw = keep([P, PASSES, R], U8, "wu_sc_raw")
+        nc.gpsimd.memset(wu_sc_raw[:].bitcast(I32), 0)
+        for q in range(4):
+            nc.sync.dma_start(
+                wu_sc_raw[32 * q : 32 * q + 4, :, :].bitcast(I32),
+                wu_scales[:, 4 * q : 4 * q + 4, :].rearrange("a r n -> r a n").bitcast(I32),
+            )
         tab_w = keep([P, T], I32, "tab_w", "slot_w")
         nc.sync.dma_start(tab_w[:], tab_words[0].rearrange("p t b -> p (t b)").bitcast(I32))
         wg_raw = {}
@@ -67,28 +74,18 @@ def tile_list_modp_gsilu_resP_kernel(
         wu_raw = keep([P, PASSES, R], I32, "wu_raw")
         nc.sync.dma_start(wu_raw[:], wu_words.rearrange("a p r i -> p a (r i)").bitcast(I32))
 
-        wu_sc_raw = keep([P, PASSES, R], U8, "wu_sc_raw")
         v_sc = [keep([P, J], U8, "v_sc%d" % a) for a in range(PASSES)]
-        w_rows = keep([P, P], F32, "w_rows")
-        nc.vector.memset(wu_sc_raw[:].bitcast(I32), 0)
-        nc.vector.memset(w_rows[:], 0.0)
         ident = keep([P, P], F32, "ident")
         make_identity(nc, ident[:])
         z = {i: keep([P, J], F32, "z%d" % i) for i in ORDER[:3]}
-        nc.vector.memset(z[ORDER[0]][:, HALF : HALF + 1], 0.0)
-        nc.vector.memset(z[ORDER[1]][:, 0:J:HALF], 0.0)
+        for i in ORDER[:2]:
+            nc.vector.memset(z[i][:, 0:J:HALF], 0.0)
         for lo, hi in ((0, 16), (32, 48), (64, 128)):
             nc.vector.memset(tab_sc[lo:hi, :].bitcast(I32), 0)
         warm = keep([P, 8], F32, "warm")
         warm_out = keep([P, 8], F32, "warm_out")
         nc.vector.memset(warm[:], 0.0)
         nc.scalar.activation(warm_out[:], warm[:], SILU)
-        for q in range(4):
-            nc.gpsimd.dma_start(
-                wu_sc_raw[32 * q : 32 * q + 4, :, :].bitcast(I32),
-                wu_scales[:, 4 * q : 4 * q + 4, :].rearrange("a r n -> r a n").bitcast(I32),
-            )
-        nc.gpsimd.dma_start(w_rows[0 : J // P, :], wgo[0].rearrange("(c j) -> c j", j=P))
         load_wg(1, 0)
         load_wg(1, 1)
 
@@ -123,8 +120,10 @@ def tile_list_modp_gsilu_resP_kernel(
         nc.vector.memset(wd_s[:].bitcast(I32), 0)
         for q in range(4):
             nc.sync.dma_start(wd_s[32 * q : 32 * q + 4, :].bitcast(I32), wd_scales[0, 4 * q : 4 * q + 4, :].bitcast(I32))
-        load_res(ORDER[1], "wg_raw10")
-        load_res(ORDER[2], "wg_raw11")
+        w_rows = keep([P, P], F32, "w_rows", "wg_raw10")
+        nc.vector.memset(w_rows[:], 0.0)
+        nc.sync.dma_start(w_rows[0 : J // P, :], wgo[0].rearrange("(c j) -> c j", j=P))
+        load_res(ORDER[1], "wg_raw11")
 
         wg_c, wg_s = [], []
 
@@ -133,7 +132,10 @@ def tile_list_modp_gsilu_resP_kernel(
             dst = bf[:].rearrange("p (t m j) -> p m t j", t=PACK, j=PACK)
             for s in range(2):
                 src = wg_raw[a, s][:].rearrange("p j (m t) -> p m t j", t=PACK)
-                nc.scalar.copy(dst[:, 64 * s : 64 * (s + 1)], src)
+                if (a, s) == (1, 1):
+                    nc.vector.tensor_copy(dst[:, 64 * s : 64 * (s + 1)], src)
+                else:
+                    nc.scalar.copy(dst[:, 64 * s : 64 * (s + 1)], src)
             codes = keep([P, R], U32, "wg_c%d" % a, "wu_raw" if a == 0 else None)
             scales = keep([P, R], U8, "wg_s%d" % a, "wu_sc_raw" if a == 0 else None)
             nc.vector.quantize_mx(codes[:].bitcast(FP8X4), scales[:], bf[:])
@@ -154,15 +156,16 @@ def tile_list_modp_gsilu_resP_kernel(
         nc.vector.memset(three[0][:], 0.0)
         quantise_wg(0)
         quantise_wg(1)
-        load_res(ORDER[3], "slot_f1")
-        three.append(keep([P, T], F32, "page1", "warm"))
-        nc.gpsimd.memset(three[1][:], 0.0)
+        load_res(ORDER[2], "slot_f0")
+        three.append(keep([P, T], F32, "page1", "slot_f1"))
+        nc.vector.memset(three[1][:], 0.0)
         pages = {ORDER[0]: three[0], ORDER[1]: three[1], ORDER[3]: three[0]}
 
         w_bank = ps3.tile([P, PACK, TOK], F32, name="w_bank", tag="late")
         nc.tensor.transpose(w_bank[:, 0, :], w_rows[:], ident[:])
         w_col = keep([P, J // P], F32, "w_col")
         nc.scalar.copy(w_col[:], w_bank[:, 0, 0 : J // P])
+        load_res(ORDER[3], "wg_raw10")
 
         def moving(a, j0):
             g = [x for x, (lo, hi) in enumerate(GATHERS) if lo <= j0 < hi][0]
@@ -211,9 +214,8 @@ def tile_list_modp_gsilu_resP_kernel(
             nc.vector.tensor_tensor(pages[i][:].indirect(listed(j0, j1)), z[i][:, j0:j1], yw[:, i, j0:j1], ADD)
 
         first, second, third, last = ORDER
-        picks = {2: (first, HALF), 4: (second, 0), 6: (second, HALF)}
+        picks = {1: (first, 0), 2: (first, HALF), 4: (second, 0), 6: (second, HALF)}
         quarters = J // QUARTER
-        pick(first, 0, HALF)
         for q in range(quarters):
             if q < quarters - 1:
                 h_bf = pair.tile([P, QUARTER * PACK], BF16, name="h_bf", align_bytes=64)[:]

@@ -78,7 +78,8 @@ def tile_list_modp_gsilu_resP_kernel(
         ident = keep([P, P], F32, "ident")
         make_identity(nc, ident[:])
         z = {i: keep([P, J], F32, "z%d" % i) for i in ORDER[:3]}
-        for i in ORDER[:2]:
+        nc.vector.memset(z[ORDER[0]][:, HALF : HALF + 1], 0.0)
+        for i in ORDER[1:3]:
             nc.vector.memset(z[i][:, 0:J:HALF], 0.0)
         for lo, hi in ((0, 16), (32, 48), (64, 128)):
             nc.vector.memset(tab_sc[lo:hi, :].bitcast(I32), 0)
@@ -113,7 +114,7 @@ def tile_list_modp_gsilu_resP_kernel(
 
         gate = keep([P, J], F32, "gate", "slot_s")
         nc.sync.dma_start(gate[:], wgo)
-        load_res(ORDER[0], "slot_w")
+        load_res(ORDER[1], "slot_w")
         wd_w = keep([P, 2 * N], U8, "wd_w", "wg_raw00")
         nc.sync.dma_start(wd_w[:].bitcast(I32), wd_words[0].bitcast(I32))
         wd_s = keep([P, N], U8, "wd_s", "wg_raw01")
@@ -123,7 +124,7 @@ def tile_list_modp_gsilu_resP_kernel(
         w_rows = keep([P, P], F32, "w_rows", "wg_raw10")
         nc.vector.memset(w_rows[:], 0.0)
         nc.sync.dma_start(w_rows[0 : J // P, :], wgo[0].rearrange("(c j) -> c j", j=P))
-        load_res(ORDER[1], "wg_raw11")
+        load_res(ORDER[2], "wg_raw11")
 
         wg_c, wg_s = [], []
 
@@ -156,12 +157,12 @@ def tile_list_modp_gsilu_resP_kernel(
         nc.vector.memset(three[0][:], 0.0)
         quantise_wg(0)
         quantise_wg(1)
-        load_res(ORDER[2], "slot_f0")
+        load_res(ORDER[0], "slot_f0")
         three.append(keep([P, T], F32, "page1", "slot_f1"))
         nc.vector.memset(three[1][:], 0.0)
         pages = {ORDER[0]: three[0], ORDER[1]: three[1], ORDER[3]: three[0]}
 
-        w_bank = ps3.tile([P, PACK, TOK], F32, name="w_bank", tag="late")
+        w_bank = ps3.tile([P, PACK, TOK], F32, name="w_bank", tag="y_bank")
         nc.tensor.transpose(w_bank[:, 0, :], w_rows[:], ident[:])
         w_col = keep([P, J // P], F32, "w_col")
         nc.scalar.copy(w_col[:], w_bank[:, 0, 0 : J // P])
@@ -185,27 +186,23 @@ def tile_list_modp_gsilu_resP_kernel(
         h_s = keep([P, J], U8, "h_s")
         yw = keep([P, PACK, J], F32, "yw")
 
-        def stage2(j0):
-            bank = ps3.tile([P, N], F32, name="y_bank", tag="late")
+        ys = {}
+
+        def stage2(c):
+            bank = ps3.tile([P, N], F32, name="y_bank")
+            tok = slice(c * TOK, (c + 1) * TOK)
             nc.tensor.matmul_mx(
-                bank[:], lhsT=h_c[:, j0 : j0 + TOK].bitcast(FP8X4), lhsT_scale=h_s[:, j0 : j0 + TOK],
+                bank[:], lhsT=h_c[:, tok].bitcast(FP8X4), lhsT_scale=h_s[:, tok],
                 rhs=wd_w[:].bitcast(FP4X4), rhs_scale=wd_s[:], start=True, stop=True,
             )
-            ys = pair.tile([P, PACK, P], F32, name="ys")
-            c = j0 // TOK
-            nc.scalar.activation(ys[:], bank[:].rearrange("p (m i) -> p i m", i=PACK), COPY, scale=w_col[:, c : c + 1])
-            return ys
+            ys[c] = keep([P, PACK, P], F32, "ys%d" % c)
+            nc.scalar.activation(ys[c][:], bank[:].rearrange("p (m i) -> p i m", i=PACK), COPY, scale=w_col[:, c : c + 1])
 
-        def turn(ys, j0):
-            bank = ps3.tile([P, PACK, TOK], F32, name="t_bank", tag="late")
-            for i in range(PACK):
-                nc.tensor.transpose(bank[:, i, :], ys[:, i, :], ident[:])
-            nc.scalar.copy(yw[:, :, j0 : j0 + TOK], bank[:])
-
-        def second_product(q):
-            made = [(stage2(j0), j0) for j0 in range(q * QUARTER, (q + 1) * QUARTER, TOK)]
-            for ys, j0 in made:
-                turn(ys, j0)
+        def turn(i, j0, pool, tag):
+            bank = pool.tile([P, HALF // TOK, TOK], F32, name="t_bank", tag=tag)
+            for c in range(HALF // TOK):
+                nc.tensor.transpose(bank[:, c, :], ys[j0 // TOK + c][:, i, :], ident[:])
+            nc.scalar.copy(yw[:, i, j0 : j0 + HALF], bank[:].rearrange("p c j -> p (c j)"))
 
         def pick(i, j0, j1):
             nc.vector.tensor_tensor(z[i][:, j0:j1], res[i][:].indirect(listed(j0, j1)), gate[:, j0:j1], MULT)
@@ -214,17 +211,17 @@ def tile_list_modp_gsilu_resP_kernel(
             nc.vector.tensor_tensor(pages[i][:].indirect(listed(j0, j1)), z[i][:, j0:j1], yw[:, i, j0:j1], ADD)
 
         first, second, third, last = ORDER
-        picks = {1: (first, 0), 2: (first, HALF), 4: (second, 0), 6: (second, HALF)}
+        picks = {1: (second, 0), 3: (second, HALF), 4: (third, 0), 5: (third, HALF), 6: (first, HALF)}
         quarters = J // QUARTER
         for q in range(quarters):
             if q < quarters - 1:
                 h_bf = pair.tile([P, QUARTER * PACK], BF16, name="h_bf", align_bytes=64)[:]
             else:
-                h_bf = z[third][:, QUARTER : J - QUARTER].bitcast(BF16)
+                h_bf = z[first][:, :HALF].bitcast(BF16)
             for c in range(QUARTER // TOK):
                 j0 = q * QUARTER + c * TOK
-                g_bank = ps2.tile([P, PACK, TOK], F32, name="g_bank")
-                u_bank = ps3.tile([P, PACK, TOK], F32, name="u_bank")
+                g_bank = ps3.tile([P, PACK, TOK], F32, name="g_bank")
+                u_bank = ps2.tile([P, PACK, TOK], F32, name="u_bank")
                 stage1(
                     u_bank, lambda a, t: wu_c[:, a, P * t : P * (t + 1)].bitcast(FP8X4),
                     lambda a, t: wu_s[:, a, P * t : P * (t + 1)], j0,
@@ -250,14 +247,18 @@ def tile_list_modp_gsilu_resP_kernel(
                 if tile_no in picks:
                     pick(i, lo, lo + HALF)
             if q > 0:
-                second_product(q - 1)
-            if 0 < q < quarters - 1:
-                put(first, cols.start - QUARTER, cols.start)
-        second_product(quarters - 1)
-        pick(third, 0, HALF)
-        put(first, J - HALF, J - QUARTER)
-        pick(third, HALF, J)
-        put(first, J - QUARTER, J)
+                stage2(2 * q - 2)
+                stage2(2 * q - 1)
+        stage2(2 * quarters - 2)
+        stage2(2 * quarters - 1)
+        turn(first, 0, ps3, "g_bank")
+        turn(first, HALF, ps3, "g_bank")
+        for i in ORDER[1:]:
+            turn(i, 0, ps2, "u_bank")
+            turn(i, HALF, ps3, "g_bank")
+        pick(first, 0, HALF)
+        put(first, 0, HALF)
+        put(first, HALF, J)
         pages[third] = keep([P, T], F32, "page2", "z%d" % first)
         nc.gpsimd.memset(pages[third][:], 0.0)
 

@@ -27,7 +27,7 @@ QUARTER = 256
 HALF = 512
 GATHERS = ((0, 512), (512, 1024))
 CHUNK = 512
-ORDER = (0, 2, 3, 1)
+ORDER = (0, 2, 1, 3)
 
 
 def tile_list_modp_gsilu_resP_kernel(
@@ -78,8 +78,7 @@ def tile_list_modp_gsilu_resP_kernel(
         ident = keep([P, P], F32, "ident")
         make_identity(nc, ident[:])
         z = {i: keep([P, J], F32, "z%d" % i) for i in ORDER[:3]}
-        nc.vector.memset(z[ORDER[0]][:, HALF : HALF + 1], 0.0)
-        for i in ORDER[1:3]:
+        for i in ORDER[:3]:
             nc.vector.memset(z[i][:, 0:J:HALF], 0.0)
         for lo, hi in ((0, 16), (32, 48), (64, 128)):
             nc.vector.memset(tab_sc[lo:hi, :].bitcast(I32), 0)
@@ -160,9 +159,9 @@ def tile_list_modp_gsilu_resP_kernel(
         load_res(ORDER[0], "slot_f0")
         three.append(keep([P, T], F32, "page1", "slot_f1"))
         nc.vector.memset(three[1][:], 0.0)
-        pages = {ORDER[0]: three[0], ORDER[1]: three[1], ORDER[3]: three[0]}
+        pages = {i: three[n % 2] for n, i in enumerate(ORDER)}
 
-        w_bank = ps3.tile([P, PACK, TOK], F32, name="w_bank", tag="y_bank")
+        w_bank = ps2.tile([P, PACK, TOK], F32, name="w_bank", tag="y_bank")
         nc.tensor.transpose(w_bank[:, 0, :], w_rows[:], ident[:])
         w_col = keep([P, J // P], F32, "w_col")
         nc.scalar.copy(w_col[:], w_bank[:, 0, 0 : J // P])
@@ -189,7 +188,7 @@ def tile_list_modp_gsilu_resP_kernel(
         ys = {}
 
         def stage2(c):
-            bank = ps3.tile([P, N], F32, name="y_bank")
+            bank = ps2.tile([P, N], F32, name="y_bank")
             tok = slice(c * TOK, (c + 1) * TOK)
             nc.tensor.matmul_mx(
                 bank[:], lhsT=h_c[:, tok].bitcast(FP8X4), lhsT_scale=h_s[:, tok],
@@ -204,24 +203,26 @@ def tile_list_modp_gsilu_resP_kernel(
                 nc.tensor.transpose(bank[:, c, :], ys[j0 // TOK + c][:, i, :], ident[:])
             nc.scalar.copy(yw[:, i, j0 : j0 + HALF], bank[:].rearrange("p c j -> p (c j)"))
 
+        def picked(i, j0, j1):
+            if i != ORDER[3]:
+                return z[i][:, j0:j1]
+            return z[ORDER[0]][:, HALF:] if j0 == 0 else z[ORDER[2]][:, :HALF]
+
         def pick(i, j0, j1):
-            nc.vector.tensor_tensor(z[i][:, j0:j1], res[i][:].indirect(listed(j0, j1)), gate[:, j0:j1], MULT)
+            nc.vector.tensor_tensor(picked(i, j0, j1), res[i][:].indirect(listed(j0, j1)), gate[:, j0:j1], MULT)
 
         def put(i, j0, j1):
-            nc.vector.tensor_tensor(pages[i][:].indirect(listed(j0, j1)), z[i][:, j0:j1], yw[:, i, j0:j1], ADD)
+            nc.vector.tensor_tensor(pages[i][:].indirect(listed(j0, j1)), picked(i, j0, j1), yw[:, i, j0:j1], ADD)
 
         first, second, third, last = ORDER
-        picks = {1: (second, 0), 3: (second, HALF), 4: (third, 0), 5: (third, HALF), 6: (first, HALF)}
+        picks = {1: (second, 0), 3: (second, HALF), 4: (third, 0), 5: (third, HALF), 6: (first, HALF), 7: (first, 0)}
         quarters = J // QUARTER
         for q in range(quarters):
-            if q < quarters - 1:
-                h_bf = pair.tile([P, QUARTER * PACK], BF16, name="h_bf", align_bytes=64)[:]
-            else:
-                h_bf = z[first][:, :HALF].bitcast(BF16)
+            h_bf = pair.tile([P, QUARTER * PACK], BF16, name="h_bf", align_bytes=64)
             for c in range(QUARTER // TOK):
                 j0 = q * QUARTER + c * TOK
                 g_bank = ps3.tile([P, PACK, TOK], F32, name="g_bank")
-                u_bank = ps2.tile([P, PACK, TOK], F32, name="u_bank")
+                u_bank = ps3.tile([P, PACK, TOK], F32, name="u_bank")
                 stage1(
                     u_bank, lambda a, t: wu_c[:, a, P * t : P * (t + 1)].bitcast(FP8X4),
                     lambda a, t: wu_s[:, a, P * t : P * (t + 1)], j0,
@@ -241,9 +242,13 @@ def tile_list_modp_gsilu_resP_kernel(
                     h_bf[:, c * TOK * PACK : (c + 1) * TOK * PACK].rearrange("p (j t) -> p j t", t=PACK),
                     u_bank[:].rearrange("p t j -> p j t"), act[:], MULT,
                 )
-                if c == QUARTER // TOK - 1:
+                if q == quarters - 1:
+                    cols = slice(j0, j0 + TOK)
+                    part = h_bf[:, c * TOK * PACK : (c + 1) * TOK * PACK]
+                    nc.vector.quantize_mx(h_c[:, cols].bitcast(FP8X4), h_s[:, cols], part)
+                elif c == QUARTER // TOK - 1:
                     cols = slice(q * QUARTER, (q + 1) * QUARTER)
-                    nc.vector.quantize_mx(h_c[:, cols].bitcast(FP8X4), h_s[:, cols], h_bf)
+                    nc.vector.quantize_mx(h_c[:, cols].bitcast(FP8X4), h_s[:, cols], h_bf[:])
                 if tile_no in picks:
                     pick(i, lo, lo + HALF)
             if q > 0:
@@ -254,13 +259,10 @@ def tile_list_modp_gsilu_resP_kernel(
         turn(first, 0, ps3, "g_bank")
         turn(first, HALF, ps3, "g_bank")
         for i in ORDER[1:]:
-            turn(i, 0, ps2, "u_bank")
+            turn(i, 0, ps3, "u_bank")
             turn(i, HALF, ps3, "g_bank")
-        pick(first, 0, HALF)
         put(first, 0, HALF)
         put(first, HALF, J)
-        pages[third] = keep([P, T], F32, "page2", "z%d" % first)
-        nc.gpsimd.memset(pages[third][:], 0.0)
 
         out_rows = out_0.rearrange("(p i) t -> p i t", i=PACK)
         woven = [
@@ -270,10 +272,13 @@ def tile_list_modp_gsilu_resP_kernel(
         out_s = keep([P, T], U8, "out_s")
         mid = CHUNK // 2
         for i in ORDER:
+            if i == third:
+                pick(last, 0, HALF)
             if i == last:
-                z[i] = keep([P, J], F32, "z%d" % i, "z%d" % second)
-                pick(i, 0, J)
-            if i != first:
+                put(i, 0, HALF)
+                pick(i, HALF, J)
+                put(i, HALF, J)
+            elif i != first:
                 put(i, 0, J)
             nc.sync.dma_start(out_rows[:, i, :], pages[i][:])
             if i != ORDER[-1]:

@@ -27,7 +27,7 @@ QUARTER = 256
 HALF = 512
 GATHERS = ((0, 512), (512, 1024))
 CHUNK = 512
-ORDER = (0, 2, 1, 3)
+ORDER = (0, 1, 2, 3)
 
 
 def tile_list_modp_gsilu_resP_kernel(
@@ -203,16 +203,11 @@ def tile_list_modp_gsilu_resP_kernel(
                 nc.tensor.transpose(bank[:, c, :], ys[j0 // TOK + c][:, i, :], ident[:])
             nc.scalar.copy(yw[:, i, j0 : j0 + HALF], bank[:].rearrange("p c j -> p (c j)"))
 
-        def picked(i, j0, j1):
-            if i != ORDER[3]:
-                return z[i][:, j0:j1]
-            return z[ORDER[0]][:, HALF:] if j0 == 0 else z[ORDER[2]][:, :HALF]
-
         def pick(i, j0, j1):
-            nc.vector.tensor_tensor(picked(i, j0, j1), res[i][:].indirect(listed(j0, j1)), gate[:, j0:j1], MULT)
+            nc.vector.tensor_tensor(z[i][:, j0:j1], res[i][:].indirect(listed(j0, j1)), gate[:, j0:j1], MULT)
 
         def put(i, j0, j1):
-            nc.vector.tensor_tensor(pages[i][:].indirect(listed(j0, j1)), picked(i, j0, j1), yw[:, i, j0:j1], ADD)
+            nc.vector.tensor_tensor(pages[i][:].indirect(listed(j0, j1)), z[i][:, j0:j1], yw[:, i, j0:j1], ADD)
 
         first, second, third, last = ORDER
         picks = {1: (second, 0), 3: (second, HALF), 4: (third, 0), 5: (third, HALF), 6: (first, HALF), 7: (first, 0)}
@@ -270,25 +265,29 @@ def tile_list_modp_gsilu_resP_kernel(
         ]
         out_c = keep([P, T], U32, "out_c")
         out_s = keep([P, T], U8, "out_s")
-        mid = CHUNK // 2
+        chunks = T // CHUNK
+        pairs = [keep([P, 2, CHUNK, 2], BF16, "pairs%d" % c, "ys%d" % c) for c in range(chunks)]
         for i in ORDER:
-            if i == third:
-                pick(last, 0, HALF)
             if i == last:
-                put(i, 0, HALF)
-                pick(i, HALF, J)
-                put(i, HALF, J)
-            elif i != first:
+                z[i] = keep([P, J], F32, "z%d" % i, "z%d" % first)
+                pick(i, 0, J)
+            if i != first:
                 put(i, 0, J)
             nc.sync.dma_start(out_rows[:, i, :], pages[i][:])
-            if i != ORDER[-1]:
-                for c in range(T // CHUNK):
-                    nc.scalar.copy(woven[c][:, :, i], pages[i][:, c * CHUNK : (c + 1) * CHUNK])
-                continue
-            for c in range(T // CHUNK):
-                nc.vector.tensor_copy(woven[c][:, :mid, i], pages[i][:, c * CHUNK : c * CHUNK + mid])
-            for c in range(T // CHUNK):
-                nc.scalar.copy(woven[c][:, mid:, i], pages[i][:, c * CHUNK + mid : (c + 1) * CHUNK])
+            for c in range(chunks):
+                values = pages[i][:, c * CHUNK : (c + 1) * CHUNK]
+                if i == third:
+                    nc.scalar.copy(pairs[c][:, 1], values.unsqueeze(2).to_broadcast([P, CHUNK, 2]))
+                elif i == last and c < chunks // 2:
+                    nc.vector.tensor_copy(pairs[c][:, 1, :, 1], values)
+                else:
+                    nc.scalar.copy(pairs[c][:, i // 2, :, i % 2], values)
+        for c in range(chunks):
+            words = pairs[c][:].rearrange("p w t e -> p w (t e)")
+            if c < chunks // 2:
+                nc.vector.tensor_copy(woven[c][:].bitcast(I32), words.bitcast(I32).rearrange("p w t -> p t w"))
+            else:
+                nc.scalar.copy(woven[c][:].bitcast(U32), words.bitcast(U32).rearrange("p w t -> p t w"))
         words_out = out_1[0].rearrange("p t b -> p (t b)").bitcast(I32)
         for c in range(T // CHUNK):
             cols = slice(c * CHUNK, (c + 1) * CHUNK)

@@ -23,11 +23,11 @@ P = 128
 PACK = 4
 PASSES = K // (P * PACK)
 TOK = 128
-QUARTER = 256
-HALF = 512
-GATHERS = ((0, 512), (512, 1024))
+TILES = J // TOK
+HALF = J // 2
 CHUNK = 512
-ORDER = (0, 1, 2, 3)
+SCALAR_GROUPS = 48
+GATHER_AFTER = {1: (1, HALF), 3: (2, 0), 4: (2, HALF), 5: (0, HALF), 6: (3, 0), 7: (0, 0)}
 
 
 def tile_list_modp_gsilu_resP_kernel(
@@ -40,8 +40,8 @@ def tile_list_modp_gsilu_resP_kernel(
         ps2 = ctx.enter_context(tc.psum_pool(name="ps2", bufs=2))
         ps3 = ctx.enter_context(tc.psum_pool(name="ps3", bufs=3))
 
-        def keep(shape, dtype, name, tag=None):
-            return held.tile(shape, dtype, name=name, tag=tag or name, align_bytes=64)
+        def keep(shape, dtype, name, after=None):
+            return held.tile(shape, dtype, name=name, tag=after or name, align_bytes=64)
 
         offsets = held.tile([P, J // 16], U16, name="offsets")
         nc.sync.dma_start(offsets[:], offs)
@@ -49,10 +49,11 @@ def tile_list_modp_gsilu_resP_kernel(
         def listed(j0, j1):
             return offsets[:, j0 // 16 : j1 // 16]
 
-        tab_sc = keep([P, T], U8, "tab_sc", "slot_s")
+        tab_sc = keep([P, T], U8, "tab_sc")
         sc_rows = tab_scales.rearrange("a (h u r) t -> u (a h) r t", h=2, u=2)
         for u in range(2):
-            nc.sync.dma_start(tab_sc[32 * u + 16 : 32 * u + 32, :].bitcast(I32), sc_rows[u].bitcast(I32))
+            nc.scalar.dma_start(tab_sc[32 * u + 16 : 32 * u + 32, :].bitcast(I32), sc_rows[u].bitcast(I32))
+
         wu_sc_raw = keep([P, PASSES, R], U8, "wu_sc_raw")
         nc.gpsimd.memset(wu_sc_raw[:].bitcast(I32), 0)
         for q in range(4):
@@ -60,238 +61,224 @@ def tile_list_modp_gsilu_resP_kernel(
                 wu_sc_raw[32 * q : 32 * q + 4, :, :].bitcast(I32),
                 wu_scales[:, 4 * q : 4 * q + 4, :].rearrange("a r n -> r a n").bitcast(I32),
             )
-        tab_w = keep([P, T], I32, "tab_w", "slot_w")
+        tab_w = keep([P, T], I32, "tab_w")
         nc.sync.dma_start(tab_w[:], tab_words[0].rearrange("p t b -> p (t b)").bitcast(I32))
-        wg_raw = {}
+        w_rows = keep([P, P], F32, "w_rows")
+        nc.gpsimd.memset(w_rows[:], 0.0)
+        nc.sync.dma_start(w_rows[0:TILES, :], wgo[0].rearrange("(c j) -> c j", j=TOK))
 
-        def load_wg(a, s):
-            wg_raw[a, s] = keep([P, PACK, R // 2], F32, "wg_raw%d%d" % (a, s))
-            rows = wg[512 * a : 512 * (a + 1), s * (R // 2) : (s + 1) * (R // 2)]
-            nc.sync.dma_start(wg_raw[a, s][:], rows.rearrange("(p j) r -> p j r", j=PACK))
-
-        load_wg(0, 0)
-        load_wg(0, 1)
+        wg_raw = [keep([P, PACK, R], F32, "wg_raw%d" % a) for a in range(PASSES)]
         wu_raw = keep([P, PASSES, R], I32, "wu_raw")
+        wg_rows = wg.rearrange("(a p j) r -> a p j r", p=P, j=PACK)
+        nc.sync.dma_start(wg_raw[0][:], wg_rows[0])
         nc.sync.dma_start(wu_raw[:], wu_words.rearrange("a p r i -> p a (r i)").bitcast(I32))
+        nc.sync.dma_start(wg_raw[1][:], wg_rows[1])
 
-        v_sc = [keep([P, J], U8, "v_sc%d" % a) for a in range(PASSES)]
         ident = keep([P, P], F32, "ident")
         make_identity(nc, ident[:])
-        z = {i: keep([P, J], F32, "z%d" % i) for i in ORDER[:3]}
-        for i in ORDER[:3]:
-            nc.vector.memset(z[i][:, 0:J:HALF], 0.0)
         for lo, hi in ((0, 16), (32, 48), (64, 128)):
             nc.vector.memset(tab_sc[lo:hi, :].bitcast(I32), 0)
-        warm = keep([P, 8], F32, "warm")
-        warm_out = keep([P, 8], F32, "warm_out")
-        nc.vector.memset(warm[:], 0.0)
-        nc.scalar.activation(warm_out[:], warm[:], SILU)
-        load_wg(1, 0)
-        load_wg(1, 1)
+
+        rw = [keep([P, J], F32, "rw%d" % i) for i in range(PACK)]
+        zero = keep([P, 1], F32, "zero")
+        nc.vector.memset(zero[:], 0.0)
+        for i, j0 in GATHER_AFTER.values():
+            nc.scalar.activation(rw[i][:, j0 : j0 + 1], zero[:], SILU)
 
         picked_sc = keep([P, J], U8, "picked_sc")
         nc.vector.tensor_copy(picked_sc[:], tab_sc[:].indirect(offsets[:]))
+        v_sc = [keep([P, J], U8, "v_sc%d" % a) for a in range(PASSES)]
         for a in range(PASSES):
             for h in range(2):
                 lo = 16 + 8 * a + 4 * h
                 nc.scalar.dma_start(v_sc[a][64 * h : 64 * h + 64, :].bitcast(I32), picked_sc[lo : lo + 64, :].bitcast(I32))
-        rT_rows = rT.rearrange("(p i) t -> p i t", i=PACK)
 
         v_w = []
-        for g, (j0, j1) in enumerate(GATHERS):
-            both = keep([P, j1 - j0], U32, "both%d" % g, "slot_g%d" % g)
-            nc.vector.tensor_copy(both[:], tab_w[:].bitcast(U32).indirect(listed(j0, j1)))
-            parted = keep([P, PASSES, 2 * (j1 - j0)], U8, "parted%d" % g, "slot_h%d" % g)
+        for g in range(2):
+            both = keep([P, HALF], U32, "both%d" % g)
+            nc.vector.tensor_copy(both[:], tab_w[:].bitcast(U32).indirect(listed(g * HALF, (g + 1) * HALF)))
+            parted = keep([P, PASSES, 2 * HALF], U8, "parted%d" % g)
             nc.vector.tensor_copy(parted[:].bitcast(U16), both[:].bitcast(U16).rearrange("p (j d) -> p d j", d=2))
             v_w.append(parted)
 
+        rT_rows = rT.rearrange("(p i) t -> p i t", i=PACK)
         res = {}
 
-        def load_res(i, slot):
-            res[i] = keep([P, T], F32, "res%d" % i, slot)
+        def load_res(i, after):
+            res[i] = keep([P, T], F32, "res%d" % i, after)
             nc.sync.dma_start(res[i][:], rT_rows[:, i, :])
 
-        gate = keep([P, J], F32, "gate", "slot_s")
-        nc.sync.dma_start(gate[:], wgo)
-        load_res(ORDER[1], "slot_w")
-        wd_w = keep([P, 2 * N], U8, "wd_w", "wg_raw00")
+        load_res(1, "tab_sc")
+        wd_w = keep([P, 2 * N], U8, "wd_w", "both0")
         nc.sync.dma_start(wd_w[:].bitcast(I32), wd_words[0].bitcast(I32))
-        wd_s = keep([P, N], U8, "wd_s", "wg_raw01")
+        wd_s = keep([P, N], U8, "wd_s", "both1")
         nc.vector.memset(wd_s[:].bitcast(I32), 0)
         for q in range(4):
             nc.sync.dma_start(wd_s[32 * q : 32 * q + 4, :].bitcast(I32), wd_scales[0, 4 * q : 4 * q + 4, :].bitcast(I32))
-        w_rows = keep([P, P], F32, "w_rows", "wg_raw10")
-        nc.vector.memset(w_rows[:], 0.0)
-        nc.sync.dma_start(w_rows[0 : J // P, :], wgo[0].rearrange("(c j) -> c j", j=P))
-        load_res(ORDER[2], "wg_raw11")
 
-        wg_c, wg_s = [], []
+        w_bank = ps2.tile([P, P], F32, name="w_bank", tag="y_bank")
+        nc.tensor.transpose(w_bank[:], w_rows[:], ident[:])
+        w_col = keep([P, TILES], F32, "w_col")
+        nc.scalar.copy(w_col[:], w_bank[:, 0:TILES])
+        gate = keep([P, J], F32, "gate")
+        for j0 in range(0, J, HALF):
+            gate_bank = ps2.tile([P, HALF], F32, name="gate_bank", tag="y_bank")
+            for j in range(0, HALF, TOK):
+                c = (j0 + j) // TOK
+                nc.tensor.transpose(gate_bank[:, j : j + TOK], w_col[:, c : c + 1].to_broadcast([P, P]), ident[:])
+            nc.scalar.copy(gate[:, j0 : j0 + HALF], gate_bank[:])
 
-        def quantise_wg(a):
-            bf = keep([P, R * PACK], BF16, "wg_bf%d" % a, "slot_f%d" % a)
-            dst = bf[:].rearrange("p (t m j) -> p m t j", t=PACK, j=PACK)
-            for s in range(2):
-                src = wg_raw[a, s][:].rearrange("p j (m t) -> p m t j", t=PACK)
-                if (a, s) == (1, 1):
-                    nc.vector.tensor_copy(dst[:, 64 * s : 64 * (s + 1)], src)
-                else:
-                    nc.scalar.copy(dst[:, 64 * s : 64 * (s + 1)], src)
-            codes = keep([P, R], U32, "wg_c%d" % a, "wu_raw" if a == 0 else None)
-            scales = keep([P, R], U8, "wg_s%d" % a, "wu_sc_raw" if a == 0 else None)
-            nc.vector.quantize_mx(codes[:].bitcast(FP8X4), scales[:], bf[:])
-            wg_c.append(codes)
-            wg_s.append(scales)
-
-        wu_s = keep([P, PASSES, R], U8, "wu_s")
         wu_c = keep([P, PASSES, R], I32, "wu_c")
+        wu_s = keep([P, PASSES, R], U8, "wu_s")
         nc.vector.tensor_copy(
-            wu_c[:].rearrange("p a (t c m) -> p a c t m", t=PACK, m=4),
-            wu_raw[:].rearrange("p a (c m t) -> p a c t m", t=PACK, m=4),
+            wu_c[:].rearrange("p a (t c e) -> p a c t e", t=PACK, e=4),
+            wu_raw[:].rearrange("p a (c e t) -> p a c t e", t=PACK, e=4),
         )
         nc.vector.tensor_copy(
             wu_s[:].rearrange("p a (t m) -> p a t m", t=PACK), wu_sc_raw[:].rearrange("p a (m t) -> p a t m", t=PACK)
         )
 
-        three = [keep([P, T], F32, "page0")]
-        nc.vector.memset(three[0][:], 0.0)
-        quantise_wg(0)
-        quantise_wg(1)
-        load_res(ORDER[0], "slot_f0")
-        three.append(keep([P, T], F32, "page1", "slot_f1"))
-        nc.vector.memset(three[1][:], 0.0)
-        pages = {i: three[n % 2] for n, i in enumerate(ORDER)}
+        wg_c, wg_s = [], []
+        for a in range(PASSES):
+            wg_bf = keep([P, R * PACK], BF16, "wg_bf%d" % a)
+            dst = wg_bf[:].rearrange("p (t m j) -> p m t j", t=PACK, j=PACK)
+            src = wg_raw[a][:].rearrange("p j (m t) -> p m t j", t=PACK)
+            if a == 0:
+                nc.scalar.copy(dst, src)
+            else:
+                nc.scalar.copy(dst[:, :SCALAR_GROUPS], src[:, :SCALAR_GROUPS])
+                nc.vector.tensor_copy(dst[:, SCALAR_GROUPS:], src[:, SCALAR_GROUPS:])
+            wg_c.append(keep([P, R], U32, "wg_c%d" % a))
+            wg_s.append(keep([P, R], U8, "wg_s%d" % a))
+            nc.vector.quantize_mx(wg_c[a][:].bitcast(FP8X4), wg_s[a][:], wg_bf[:])
+        load_res(2, "wg_raw0")
+        load_res(0, "wg_bf0")
+        load_res(3, "wg_raw1")
 
-        w_bank = ps2.tile([P, PACK, TOK], F32, name="w_bank", tag="y_bank")
-        nc.tensor.transpose(w_bank[:, 0, :], w_rows[:], ident[:])
-        w_col = keep([P, J // P], F32, "w_col")
-        nc.scalar.copy(w_col[:], w_bank[:, 0, 0 : J // P])
-        load_res(ORDER[3], "wg_raw10")
+        two = [keep([P, T], F32, "page_even"), keep([P, T], F32, "page_odd", "wg_bf1")]
+        for page in two:
+            nc.vector.memset(page[:], 0.0)
 
-        def moving(a, j0):
-            g = [x for x, (lo, hi) in enumerate(GATHERS) if lo <= j0 < hi][0]
-            c = j0 - GATHERS[g][0]
-            return v_w[g][:, a, 2 * c : 2 * (c + TOK)].bitcast(FP4X4), v_sc[a][:, j0 : j0 + TOK]
+        def pick(i, j0):
+            cols = slice(j0, j0 + HALF)
+            nc.vector.tensor_tensor(rw[i][:, cols], res[i][:].indirect(listed(j0, j0 + HALF)), gate[:, cols], MULT)
 
-        def stage1(bank, words, scales, j0):
+        pick(1, 0)
+
+        def first_product(bank, codes, scales, c):
+            g, j = divmod(c * TOK, HALF)
             for t in range(PACK):
+                cols = slice(P * t, P * (t + 1))
                 for a in range(PASSES):
-                    rhs, rhs_s = moving(a, j0)
                     nc.tensor.matmul_mx(
-                        bank[:, t, :], lhsT=words(a, t), lhsT_scale=scales(a, t), rhs=rhs, rhs_scale=rhs_s,
-                        start=(a == 0), stop=(a == PASSES - 1),
+                        bank[:, t, :], lhsT=codes[a][:, cols].bitcast(FP8X4), lhsT_scale=scales[a][:, cols],
+                        rhs=v_w[g][:, a, 2 * j : 2 * (j + TOK)].bitcast(FP4X4),
+                        rhs_scale=v_sc[a][:, c * TOK : (c + 1) * TOK], start=(a == 0), stop=(a == PASSES - 1),
                     )
 
         h_c = keep([P, J], U32, "h_c")
         h_s = keep([P, J], U8, "h_s")
+        y_tok = {}
         yw = keep([P, PACK, J], F32, "yw")
 
-        ys = {}
+        def quantise_h(h_bf, j0, j1):
+            nc.vector.quantize_mx(h_c[:, j0:j1].bitcast(FP8X4), h_s[:, j0:j1], h_bf)
 
-        def stage2(c):
-            bank = ps2.tile([P, N], F32, name="y_bank")
+        def second_product(c):
+            y_bank = ps2.tile([P, N], F32, name="y_bank")
             tok = slice(c * TOK, (c + 1) * TOK)
             nc.tensor.matmul_mx(
-                bank[:], lhsT=h_c[:, tok].bitcast(FP8X4), lhsT_scale=h_s[:, tok],
+                y_bank[:], lhsT=h_c[:, tok].bitcast(FP8X4), lhsT_scale=h_s[:, tok],
                 rhs=wd_w[:].bitcast(FP4X4), rhs_scale=wd_s[:], start=True, stop=True,
             )
-            ys[c] = keep([P, PACK, P], F32, "ys%d" % c)
-            nc.scalar.activation(ys[c][:], bank[:].rearrange("p (m i) -> p i m", i=PACK), COPY, scale=w_col[:, c : c + 1])
+            y_tok[c] = keep([P, PACK, P], F32, "y_tok%d" % c)
+            nc.scalar.activation(
+                y_tok[c][:], y_bank[:].rearrange("p (m i) -> p i m", i=PACK), COPY, scale=w_col[:, c : c + 1]
+            )
 
-        def turn(i, j0, pool, tag):
-            bank = pool.tile([P, HALF // TOK, TOK], F32, name="t_bank", tag=tag)
-            for c in range(HALF // TOK):
-                nc.tensor.transpose(bank[:, c, :], ys[j0 // TOK + c][:, i, :], ident[:])
-            nc.scalar.copy(yw[:, i, j0 : j0 + HALF], bank[:].rearrange("p c j -> p (c j)"))
-
-        def pick(i, j0, j1):
-            nc.vector.tensor_tensor(z[i][:, j0:j1], res[i][:].indirect(listed(j0, j1)), gate[:, j0:j1], MULT)
-
-        def put(i, j0, j1):
-            nc.vector.tensor_tensor(pages[i][:].indirect(listed(j0, j1)), z[i][:, j0:j1], yw[:, i, j0:j1], ADD)
-
-        first, second, third, last = ORDER
-        picks = {1: (second, 0), 3: (second, HALF), 4: (third, 0), 5: (third, HALF), 6: (first, HALF), 7: (first, 0)}
-        quarters = J // QUARTER
-        for q in range(quarters):
-            h_bf = pair.tile([P, QUARTER * PACK], BF16, name="h_bf", align_bytes=64)
-            for c in range(QUARTER // TOK):
-                j0 = q * QUARTER + c * TOK
+        wu_codes = [wu_c[:, a, :] for a in range(PASSES)]
+        wu_scale = [wu_s[:, a, :] for a in range(PASSES)]
+        for c0 in range(0, TILES, 2):
+            final_pair = c0 + 2 == TILES
+            h_bf = pair.tile([P, 2, TOK * PACK], BF16, name="h_bf", align_bytes=64)
+            for c in (c0, c0 + 1):
                 g_bank = ps3.tile([P, PACK, TOK], F32, name="g_bank")
                 u_bank = ps3.tile([P, PACK, TOK], F32, name="u_bank")
-                stage1(
-                    u_bank, lambda a, t: wu_c[:, a, P * t : P * (t + 1)].bitcast(FP8X4),
-                    lambda a, t: wu_s[:, a, P * t : P * (t + 1)], j0,
-                )
-                stage1(
-                    g_bank, lambda a, t: wg_c[a][:, P * t : P * (t + 1)].bitcast(FP8X4),
-                    lambda a, t: wg_s[a][:, P * t : P * (t + 1)], j0,
-                )
-                act = pair.tile([P, TOK, PACK], F32, name="act")
-                tile_no = j0 // TOK
-                if tile_no in picks:
-                    i, lo = picks[tile_no]
-                    nc.scalar.activation(act[:], g_bank[:].rearrange("p t j -> p j t"), SILU, bias=z[i][:, lo : lo + 1])
+                first_product(u_bank, wu_codes, wu_scale, c)
+                first_product(g_bank, wg_c, wg_s, c)
+                if c < TILES - 1:
+                    act = pair.tile([P, TOK * PACK], F32, name="act")[:]
                 else:
-                    nc.scalar.activation(act[:], g_bank[:].rearrange("p t j -> p j t"), SILU)
+                    act = rw[3][:, HALF:]
+                act = act.rearrange("p (j t) -> p j t", t=PACK)
+                if c in GATHER_AFTER:
+                    i, j0 = GATHER_AFTER[c]
+                    nc.scalar.activation(act, g_bank[:].rearrange("p t j -> p j t"), SILU, bias=rw[i][:, j0 : j0 + 1])
+                else:
+                    nc.scalar.activation(act, g_bank[:].rearrange("p t j -> p j t"), SILU)
                 nc.vector.tensor_tensor(
-                    h_bf[:, c * TOK * PACK : (c + 1) * TOK * PACK].rearrange("p (j t) -> p j t", t=PACK),
-                    u_bank[:].rearrange("p t j -> p j t"), act[:], MULT,
+                    h_bf[:, c - c0, :].rearrange("p (j t) -> p j t", t=PACK),
+                    u_bank[:].rearrange("p t j -> p j t"), act, MULT,
                 )
-                if q == quarters - 1:
-                    cols = slice(j0, j0 + TOK)
-                    part = h_bf[:, c * TOK * PACK : (c + 1) * TOK * PACK]
-                    nc.vector.quantize_mx(h_c[:, cols].bitcast(FP8X4), h_s[:, cols], part)
-                elif c == QUARTER // TOK - 1:
-                    cols = slice(q * QUARTER, (q + 1) * QUARTER)
-                    nc.vector.quantize_mx(h_c[:, cols].bitcast(FP8X4), h_s[:, cols], h_bf[:])
-                if tile_no in picks:
-                    pick(i, lo, lo + HALF)
-            if q > 0:
-                stage2(2 * q - 2)
-                stage2(2 * q - 1)
-        stage2(2 * quarters - 2)
-        stage2(2 * quarters - 1)
-        turn(first, 0, ps3, "g_bank")
-        turn(first, HALF, ps3, "g_bank")
-        for i in ORDER[1:]:
-            turn(i, 0, ps3, "u_bank")
-            turn(i, HALF, ps3, "g_bank")
-        put(first, 0, HALF)
-        put(first, HALF, J)
+                if final_pair:
+                    quantise_h(h_bf[:, c - c0, :], c * TOK, (c + 1) * TOK)
+                elif c > c0:
+                    quantise_h(h_bf[:].rearrange("p c x -> p (c x)"), c0 * TOK, (c0 + 2) * TOK)
+                if c in GATHER_AFTER:
+                    pick(*GATHER_AFTER[c])
+            if c0 > 0:
+                second_product(c0 - 2)
+                second_product(c0 - 1)
+        second_product(TILES - 2)
+        second_product(TILES - 1)
 
-        out_rows = out_0.rearrange("(p i) t -> p i t", i=PACK)
+        for i in range(PACK):
+            for j0 in range(0, J, HALF):
+                tag = "u_bank" if i > 0 and j0 == 0 else "g_bank"
+                t_bank = ps3.tile([P, HALF], F32, name="t_bank", tag=tag)
+                for j in range(0, HALF, TOK):
+                    nc.tensor.transpose(t_bank[:, j : j + TOK], y_tok[(j0 + j) // TOK][:, i, :], ident[:])
+                nc.scalar.copy(yw[:, i, j0 : j0 + HALF], t_bank[:])
+
+        def put(i, j0, j1):
+            nc.vector.tensor_tensor(two[i % 2][:].indirect(listed(j0, j1)), rw[i][:, j0:j1], yw[:, i, j0:j1], ADD)
+
+        put(0, 0, HALF)
+        pick(3, HALF)
+        put(0, HALF, J)
+
+        chunks = [slice(lo, lo + CHUNK) for lo in range(0, T, CHUNK)]
+        on_vector = len(chunks) // 2
         woven = [
-            keep([P, CHUNK, PACK], BF16, "woven%d" % c, slot) for c, slot in enumerate(("h_c", "h_s", "slot_h0", "slot_h1"))
+            keep([P, CHUNK, PACK], BF16, "woven%d" % c, after)
+            for c, after in enumerate(("h_c", "h_s", "parted0", "parted1"))
         ]
-        out_c = keep([P, T], U32, "out_c")
-        out_s = keep([P, T], U8, "out_s")
-        chunks = T // CHUNK
-        pairs = [keep([P, 2, CHUNK, 2], BF16, "pairs%d" % c, "ys%d" % c) for c in range(chunks)]
-        for i in ORDER:
-            if i == last:
-                z[i] = keep([P, J], F32, "z%d" % i, "z%d" % first)
-                pick(i, 0, J)
-            if i != first:
+        pairs = [keep([P, 2, CHUNK, 2], BF16, "pairs%d" % c, "y_tok%d" % c) for c in range(len(chunks))]
+        out_rows = out_0.rearrange("(p i) t -> p i t", i=PACK)
+        for i in range(PACK):
+            if i > 0:
                 put(i, 0, J)
-            nc.sync.dma_start(out_rows[:, i, :], pages[i][:])
-            for c in range(chunks):
-                values = pages[i][:, c * CHUNK : (c + 1) * CHUNK]
-                if i == third:
+            nc.sync.dma_start(out_rows[:, i, :], two[i % 2][:])
+            for c, cols in enumerate(chunks):
+                values = two[i % 2][:, cols]
+                if i == 2:
                     nc.scalar.copy(pairs[c][:, 1], values.unsqueeze(2).to_broadcast([P, CHUNK, 2]))
-                elif i == last and c < chunks // 2:
+                elif i == 3 and c < on_vector:
                     nc.vector.tensor_copy(pairs[c][:, 1, :, 1], values)
                 else:
                     nc.scalar.copy(pairs[c][:, i // 2, :, i % 2], values)
-        for c in range(chunks):
+        for c in range(len(chunks)):
             words = pairs[c][:].rearrange("p w t e -> p w (t e)")
-            if c < chunks // 2:
+            if c < on_vector:
                 nc.vector.tensor_copy(woven[c][:].bitcast(I32), words.bitcast(I32).rearrange("p w t -> p t w"))
             else:
                 nc.scalar.copy(woven[c][:].bitcast(U32), words.bitcast(U32).rearrange("p w t -> p t w"))
+
+        out_c = keep([P, T], U32, "out_c")
+        out_s = keep([P, T], U8, "out_s")
         words_out = out_1[0].rearrange("p t b -> p (t b)").bitcast(I32)
-        for c in range(T // CHUNK):
-            cols = slice(c * CHUNK, (c + 1) * CHUNK)
+        for c, cols in enumerate(chunks):
             nc.vector.quantize_mx(out_c[:, cols].bitcast(FP8X4), out_s[:, cols], woven[c][:].rearrange("p t i -> p (t i)"))
             nc.sync.dma_start(words_out[:, cols], out_c[:, cols].bitcast(I32))
         for q in range(4):
-            nc.sync.dma_start(out_2[0, 4 * q : 4 * q + 4, :].bitcast(I32), out_s[32 * q : 32 * q + 4, :].bitcast(I32))
+            nc.scalar.dma_start(out_2[0, 4 * q : 4 * q + 4, :].bitcast(I32), out_s[32 * q : 32 * q + 4, :].bitcast(I32))

@@ -27,7 +27,9 @@ TILES = J // TOK
 HALF = J // 2
 CHUNK = 512
 SCALAR_GROUPS = 48
-GATHER_AFTER = {1: (1, HALF), 3: (2, 0), 4: (2, HALF), 5: (0, HALF), 6: (3, 0), 7: (0, 0)}
+EARLY_UP = 1
+QUANTISE_FROM = {4: 0, 6: 4, 8: 6}
+COPIED_UP = TILES - 3
 
 
 def tile_list_modp_gsilu_resP_kernel(
@@ -36,7 +38,7 @@ def tile_list_modp_gsilu_resP_kernel(
     nc = tc.nc
     with ExitStack() as ctx:
         held = ctx.enter_context(tc.tile_pool(name="held", bufs=1))
-        pair = ctx.enter_context(tc.tile_pool(name="pair", bufs=2))
+        ring = ctx.enter_context(tc.tile_pool(name="ring", bufs=6))
         ps2 = ctx.enter_context(tc.psum_pool(name="ps2", bufs=2))
         ps3 = ctx.enter_context(tc.psum_pool(name="ps3", bufs=3))
 
@@ -67,23 +69,21 @@ def tile_list_modp_gsilu_resP_kernel(
         nc.gpsimd.memset(w_rows[:], 0.0)
         nc.sync.dma_start(w_rows[0:TILES, :], wgo[0].rearrange("(c j) -> c j", j=TOK))
 
-        wg_raw = [keep([P, PACK, R], F32, "wg_raw%d" % a) for a in range(PASSES)]
-        wu_raw = keep([P, PASSES, R], I32, "wu_raw")
         wg_rows = wg.rearrange("(a p j) r -> a p j r", p=P, j=PACK)
+        wg_raw = [keep([P, PACK, R], F32, "wg_raw0")]
         nc.sync.dma_start(wg_raw[0][:], wg_rows[0])
+        wu_raw = keep([P, PASSES, R], I32, "wu_raw")
         nc.sync.dma_start(wu_raw[:], wu_words.rearrange("a p r i -> p a (r i)").bitcast(I32))
-        nc.sync.dma_start(wg_raw[1][:], wg_rows[1])
 
         ident = keep([P, P], F32, "ident")
         make_identity(nc, ident[:])
         for lo, hi in ((0, 16), (32, 48), (64, 128)):
             nc.vector.memset(tab_sc[lo:hi, :].bitcast(I32), 0)
 
-        rw = [keep([P, J], F32, "rw%d" % i) for i in range(PACK)]
         zero = keep([P, 1], F32, "zero")
         nc.vector.memset(zero[:], 0.0)
-        for i, j0 in GATHER_AFTER.values():
-            nc.scalar.activation(rw[i][:, j0 : j0 + 1], zero[:], SILU)
+        bias = keep([P, 1], F32, "bias")
+        nc.scalar.activation(bias[:], zero[:], SILU)
 
         picked_sc = keep([P, J], U8, "picked_sc")
         nc.vector.tensor_copy(picked_sc[:], tab_sc[:].indirect(offsets[:]))
@@ -91,15 +91,14 @@ def tile_list_modp_gsilu_resP_kernel(
         for a in range(PASSES):
             for h in range(2):
                 lo = 16 + 8 * a + 4 * h
-                nc.scalar.dma_start(v_sc[a][64 * h : 64 * h + 64, :].bitcast(I32), picked_sc[lo : lo + 64, :].bitcast(I32))
+                nc.sync.dma_start(v_sc[a][64 * h : 64 * h + 64, :].bitcast(I32), picked_sc[lo : lo + 64, :].bitcast(I32))
 
-        v_w = []
+        both = [keep([P, HALF], U32, "both%d" % g) for g in range(2)]
+        v_w = [keep([P, PASSES, 2 * HALF], U8, "parted%d" % g) for g in range(2)]
         for g in range(2):
-            both = keep([P, HALF], U32, "both%d" % g)
-            nc.vector.tensor_copy(both[:], tab_w[:].bitcast(U32).indirect(listed(g * HALF, (g + 1) * HALF)))
-            parted = keep([P, PASSES, 2 * HALF], U8, "parted%d" % g)
-            nc.vector.tensor_copy(parted[:].bitcast(U16), both[:].bitcast(U16).rearrange("p (j d) -> p d j", d=2))
-            v_w.append(parted)
+            nc.vector.tensor_copy(both[g][:], tab_w[:].bitcast(U32).indirect(listed(g * HALF, (g + 1) * HALF)))
+        for g in range(2):
+            nc.vector.tensor_copy(v_w[g][:].bitcast(U16), both[g][:].bitcast(U16).rearrange("p (j d) -> p d j", d=2))
 
         rT_rows = rT.rearrange("(p i) t -> p i t", i=PACK)
         res = {}
@@ -109,12 +108,8 @@ def tile_list_modp_gsilu_resP_kernel(
             nc.sync.dma_start(res[i][:], rT_rows[:, i, :])
 
         load_res(1, "tab_sc")
-        wd_w = keep([P, 2 * N], U8, "wd_w", "both0")
-        nc.sync.dma_start(wd_w[:].bitcast(I32), wd_words[0].bitcast(I32))
-        wd_s = keep([P, N], U8, "wd_s", "both1")
-        nc.vector.memset(wd_s[:].bitcast(I32), 0)
-        for q in range(4):
-            nc.sync.dma_start(wd_s[32 * q : 32 * q + 4, :].bitcast(I32), wd_scales[0, 4 * q : 4 * q + 4, :].bitcast(I32))
+        wg_raw.append(keep([P, PACK, R], F32, "wg_raw1", "tab_w"))
+        nc.sync.dma_start(wg_raw[1][:], wg_rows[1])
 
         w_bank = ps2.tile([P, P], F32, name="w_bank", tag="y_bank")
         nc.tensor.transpose(w_bank[:], w_rows[:], ident[:])
@@ -152,18 +147,27 @@ def tile_list_modp_gsilu_resP_kernel(
             wg_s.append(keep([P, R], U8, "wg_s%d" % a))
             nc.vector.quantize_mx(wg_c[a][:].bitcast(FP8X4), wg_s[a][:], wg_bf[:])
         load_res(2, "wg_raw0")
-        load_res(0, "wg_bf0")
-        load_res(3, "wg_raw1")
+        wd_w = keep([P, 2 * N], U8, "wd_w", "wu_raw")
+        nc.sync.dma_start(wd_w[:].bitcast(I32), wd_words[0].bitcast(I32))
+        wd_s = keep([P, N], U8, "wd_s", "wu_sc_raw")
+        nc.gpsimd.memset(wd_s[:].bitcast(I32), 0)
+        for q in range(4):
+            nc.sync.dma_start(wd_s[32 * q : 32 * q + 4, :].bitcast(I32), wd_scales[0, 4 * q : 4 * q + 4, :].bitcast(I32))
+        load_res(3, "wg_bf0")
+        load_res(0, "wg_bf1")
 
-        two = [keep([P, T], F32, "page_even"), keep([P, T], F32, "page_odd", "wg_bf1")]
-        for page in two:
-            nc.vector.memset(page[:], 0.0)
+        two = [keep([P, T], F32, "page_even")]
+        nc.vector.memset(two[0][:], 0.0)
+        rw = {}
 
-        def pick(i, j0):
-            cols = slice(j0, j0 + HALF)
-            nc.vector.tensor_tensor(rw[i][:, cols], res[i][:].indirect(listed(j0, j0 + HALF)), gate[:, cols], MULT)
+        def pick(i, step, after=None):
+            rw[i] = keep([P, J], F32, "rw%d" % i, after)
+            for j0 in range(0, J, step):
+                cols = slice(j0, j0 + step)
+                nc.vector.tensor_tensor(rw[i][:, cols], res[i][:].indirect(listed(j0, j0 + step)), gate[:, cols], MULT)
 
-        pick(1, 0)
+        for i in range(1, PACK):
+            pick(i, J)
 
         def first_product(bank, codes, scales, c):
             g, j = divmod(c * TOK, HALF)
@@ -181,11 +185,8 @@ def tile_list_modp_gsilu_resP_kernel(
         y_tok = {}
         yw = keep([P, PACK, J], F32, "yw")
 
-        def quantise_h(h_bf, j0, j1):
-            nc.vector.quantize_mx(h_c[:, j0:j1].bitcast(FP8X4), h_s[:, j0:j1], h_bf)
-
         def second_product(c):
-            y_bank = ps2.tile([P, N], F32, name="y_bank")
+            y_bank = ps3.tile([P, N], F32, name="y_bank", tag="g_bank")
             tok = slice(c * TOK, (c + 1) * TOK)
             nc.tensor.matmul_mx(
                 y_bank[:], lhsT=h_c[:, tok].bitcast(FP8X4), lhsT_scale=h_s[:, tok],
@@ -198,53 +199,52 @@ def tile_list_modp_gsilu_resP_kernel(
 
         wu_codes = [wu_c[:, a, :] for a in range(PASSES)]
         wu_scale = [wu_s[:, a, :] for a in range(PASSES)]
-        for c0 in range(0, TILES, 2):
-            final_pair = c0 + 2 == TILES
-            h_bf = pair.tile([P, 2, TOK * PACK], BF16, name="h_bf", align_bytes=64)
-            for c in (c0, c0 + 1):
-                g_bank = ps3.tile([P, PACK, TOK], F32, name="g_bank")
-                u_bank = ps3.tile([P, PACK, TOK], F32, name="u_bank")
-                first_product(u_bank, wu_codes, wu_scale, c)
-                first_product(g_bank, wg_c, wg_s, c)
-                if c < TILES - 1:
-                    act = pair.tile([P, TOK * PACK], F32, name="act")[:]
-                else:
-                    act = rw[3][:, HALF:]
-                act = act.rearrange("p (j t) -> p j t", t=PACK)
-                if c in GATHER_AFTER:
-                    i, j0 = GATHER_AFTER[c]
-                    nc.scalar.activation(act, g_bank[:].rearrange("p t j -> p j t"), SILU, bias=rw[i][:, j0 : j0 + 1])
-                else:
-                    nc.scalar.activation(act, g_bank[:].rearrange("p t j -> p j t"), SILU)
-                nc.vector.tensor_tensor(
-                    h_bf[:, c - c0, :].rearrange("p (j t) -> p j t", t=PACK),
-                    u_bank[:].rearrange("p t j -> p j t"), act, MULT,
+        early_up = keep([P, EARLY_UP, TOK, PACK], F32, "early_up")
+        later_up = keep([P, COPIED_UP - EARLY_UP, TOK, PACK], F32, "later_up", "tab_w")
+        h_bf = keep([P, TILES, TOK * PACK], BF16, "h_bf")
+        for c in range(TILES):
+            g_bank = ps3.tile([P, PACK, TOK], F32, name="g_bank")
+            u_bank = ps3.tile([P, PACK, TOK], F32, name="u_bank")
+            first_product(u_bank, wu_codes, wu_scale, c)
+            first_product(g_bank, wg_c, wg_s, c)
+            if c < TILES - 1:
+                act = ring.tile([P, TOK, PACK], F32, name="act")
+            else:
+                act = keep([P, TOK, PACK], F32, "last_act")
+            up = u_bank[:].rearrange("p t j -> p j t")
+            if c < COPIED_UP:
+                copied = early_up[:, c] if c < EARLY_UP else later_up[:, c - EARLY_UP]
+                nc.scalar.copy(copied, up)
+                up = copied
+            nc.scalar.activation(act[:], g_bank[:].rearrange("p t j -> p j t"), SILU, bias=bias[:])
+            nc.vector.tensor_tensor(h_bf[:, c, :].rearrange("p (j t) -> p j t", t=PACK), up, act[:], MULT)
+            if c + 1 in QUANTISE_FROM:
+                c0 = QUANTISE_FROM[c + 1]
+                nc.vector.quantize_mx(
+                    h_c[:, c0 * TOK : (c + 1) * TOK].bitcast(FP8X4), h_s[:, c0 * TOK : (c + 1) * TOK],
+                    h_bf[:, c0 : c + 1, :].rearrange("p c x -> p (c x)"),
                 )
-                if final_pair:
-                    quantise_h(h_bf[:, c - c0, :], c * TOK, (c + 1) * TOK)
-                elif c > c0:
-                    quantise_h(h_bf[:].rearrange("p c x -> p (c x)"), c0 * TOK, (c0 + 2) * TOK)
-                if c in GATHER_AFTER:
-                    pick(*GATHER_AFTER[c])
-            if c0 > 0:
-                second_product(c0 - 2)
-                second_product(c0 - 1)
-        second_product(TILES - 2)
-        second_product(TILES - 1)
+        pick(0, HALF, "last_act")
+        two.append(keep([P, T], F32, "page_odd", "wg_bf1"))
+        nc.gpsimd.memset(two[1][:], 0.0)
+        def turn(i, j0):
+            t_bank = ps2.tile([P, HALF], F32, name="t_bank", tag="y_bank")
+            for j in range(0, HALF, TOK):
+                nc.tensor.transpose(t_bank[:, j : j + TOK], y_tok[(j0 + j) // TOK][:, i, :], ident[:])
+            nc.scalar.copy(yw[:, i, j0 : j0 + HALF], t_bank[:])
 
-        for i in range(PACK):
+        for j0 in range(0, J, HALF):
+            for c in range(j0 // TOK, (j0 + HALF) // TOK):
+                second_product(c)
+            turn(0, j0)
+        for i in range(1, PACK):
             for j0 in range(0, J, HALF):
-                tag = "u_bank" if i > 0 and j0 == 0 else "g_bank"
-                t_bank = ps3.tile([P, HALF], F32, name="t_bank", tag=tag)
-                for j in range(0, HALF, TOK):
-                    nc.tensor.transpose(t_bank[:, j : j + TOK], y_tok[(j0 + j) // TOK][:, i, :], ident[:])
-                nc.scalar.copy(yw[:, i, j0 : j0 + HALF], t_bank[:])
+                turn(i, j0)
 
         def put(i, j0, j1):
             nc.vector.tensor_tensor(two[i % 2][:].indirect(listed(j0, j1)), rw[i][:, j0:j1], yw[:, i, j0:j1], ADD)
 
         put(0, 0, HALF)
-        pick(3, HALF)
         put(0, HALF, J)
 
         chunks = [slice(lo, lo + CHUNK) for lo in range(0, T, CHUNK)]

@@ -27,7 +27,6 @@ TILES = J // TOK
 HALF = J // 2
 CHUNK = 512
 SCALAR_GROUPS = 48
-EARLY_UP = 1
 QUANTISE_FROM = {4: 0, 6: 4, 8: 6}
 COPIED_UP = TILES - 3
 
@@ -38,12 +37,16 @@ def tile_list_modp_gsilu_resP_kernel(
     nc = tc.nc
     with ExitStack() as ctx:
         held = ctx.enter_context(tc.tile_pool(name="held", bufs=1))
+        late = ctx.enter_context(tc.tile_pool(name="late", bufs=1))
         ring = ctx.enter_context(tc.tile_pool(name="ring", bufs=6))
         ps2 = ctx.enter_context(tc.psum_pool(name="ps2", bufs=2))
         ps3 = ctx.enter_context(tc.psum_pool(name="ps3", bufs=3))
 
         def keep(shape, dtype, name, after=None):
             return held.tile(shape, dtype, name=name, tag=after or name, align_bytes=64)
+
+        def place(shape, dtype, name, offset):
+            return late.tile(shape, dtype, name=name, offset=offset, align_bytes=64)
 
         offsets = held.tile([P, J // 16], U16, name="offsets")
         nc.sync.dma_start(offsets[:], offs)
@@ -75,6 +78,14 @@ def tile_list_modp_gsilu_resP_kernel(
         wu_raw = keep([P, PASSES, R], I32, "wu_raw")
         nc.sync.dma_start(wu_raw[:], wu_words.rearrange("a p r i -> p a (r i)").bitcast(I32))
 
+        rT_rows = rT.rearrange("(p i) t -> p i t", i=PACK)
+        res = {}
+
+        def load_res(i, after=None):
+            res[i] = keep([P, T], F32, "res%d" % i, after)
+            nc.sync.dma_start(res[i][:], rT_rows[:, i, :])
+
+        load_res(1)
         ident = keep([P, P], F32, "ident")
         make_identity(nc, ident[:])
         for lo, hi in ((0, 16), (32, 48), (64, 128)):
@@ -100,15 +111,7 @@ def tile_list_modp_gsilu_resP_kernel(
         for g in range(2):
             nc.vector.tensor_copy(v_w[g][:].bitcast(U16), both[g][:].bitcast(U16).rearrange("p (j d) -> p d j", d=2))
 
-        rT_rows = rT.rearrange("(p i) t -> p i t", i=PACK)
-        res = {}
-
-        def load_res(i, after):
-            res[i] = keep([P, T], F32, "res%d" % i, after)
-            nc.sync.dma_start(res[i][:], rT_rows[:, i, :])
-
-        load_res(1, "tab_sc")
-        wg_raw.append(keep([P, PACK, R], F32, "wg_raw1", "tab_w"))
+        wg_raw.append(keep([P, PACK, R], F32, "wg_raw1", "tab_sc"))
         nc.sync.dma_start(wg_raw[1][:], wg_rows[1])
 
         w_bank = ps2.tile([P, P], F32, name="w_bank", tag="y_bank")
@@ -123,38 +126,39 @@ def tile_list_modp_gsilu_resP_kernel(
                 nc.tensor.transpose(gate_bank[:, j : j + TOK], w_col[:, c : c + 1].to_broadcast([P, P]), ident[:])
             nc.scalar.copy(gate[:, j0 : j0 + HALF], gate_bank[:])
 
-        wu_c = keep([P, PASSES, R], I32, "wu_c")
+        wu_c = keep([P, PASSES, R], U32, "wu_c")
         wu_s = keep([P, PASSES, R], U8, "wu_s")
-        nc.vector.tensor_copy(
-            wu_c[:].rearrange("p a (t c e) -> p a c t e", t=PACK, e=4),
-            wu_raw[:].rearrange("p a (c e t) -> p a c t e", t=PACK, e=4),
-        )
         nc.vector.tensor_copy(
             wu_s[:].rearrange("p a (t m) -> p a t m", t=PACK), wu_sc_raw[:].rearrange("p a (m t) -> p a t m", t=PACK)
         )
 
         wg_c, wg_s = [], []
         for a in range(PASSES):
-            wg_bf = keep([P, R * PACK], BF16, "wg_bf%d" % a)
+            wg_bf = keep([P, R * PACK], BF16, "wg_bf0") if a == 0 else place([P, R * PACK], BF16, "wg_bf1", 0)
             dst = wg_bf[:].rearrange("p (t m j) -> p m t j", t=PACK, j=PACK)
             src = wg_raw[a][:].rearrange("p j (m t) -> p m t j", t=PACK)
             if a == 0:
                 nc.scalar.copy(dst, src)
+                nc.scalar.copy(
+                    wu_c[:].rearrange("p a (t c e) -> p a c t e", t=PACK, e=4),
+                    wu_raw[:].bitcast(U32).rearrange("p a (c e t) -> p a c t e", t=PACK, e=4),
+                )
             else:
                 nc.scalar.copy(dst[:, :SCALAR_GROUPS], src[:, :SCALAR_GROUPS])
                 nc.vector.tensor_copy(dst[:, SCALAR_GROUPS:], src[:, SCALAR_GROUPS:])
             wg_c.append(keep([P, R], U32, "wg_c%d" % a))
             wg_s.append(keep([P, R], U8, "wg_s%d" % a))
             nc.vector.quantize_mx(wg_c[a][:].bitcast(FP8X4), wg_s[a][:], wg_bf[:])
-        load_res(2, "wg_raw0")
-        wd_w = keep([P, 2 * N], U8, "wd_w", "wu_raw")
+        load_res(2, "tab_w")
+        load_res(3, "wg_bf0")
+        wd_w = place([P, 2 * N], U8, "wd_w", 0)
         nc.sync.dma_start(wd_w[:].bitcast(I32), wd_words[0].bitcast(I32))
-        wd_s = keep([P, N], U8, "wd_s", "wu_sc_raw")
+        res[0] = place([P, T], F32, "res0", 3 * N)
+        nc.sync.dma_start(res[0][:], rT_rows[:, 0, :])
+        wd_s = place([P, N], U8, "wd_s", 2 * N)
         nc.gpsimd.memset(wd_s[:].bitcast(I32), 0)
         for q in range(4):
             nc.sync.dma_start(wd_s[32 * q : 32 * q + 4, :].bitcast(I32), wd_scales[0, 4 * q : 4 * q + 4, :].bitcast(I32))
-        load_res(3, "wg_bf0")
-        load_res(0, "wg_bf1")
 
         two = [keep([P, T], F32, "page_even")]
         nc.vector.memset(two[0][:], 0.0)
@@ -171,13 +175,14 @@ def tile_list_modp_gsilu_resP_kernel(
 
         def first_product(bank, codes, scales, c):
             g, j = divmod(c * TOK, HALF)
-            for t in range(PACK):
-                cols = slice(P * t, P * (t + 1))
-                for a in range(PASSES):
+            for a in range(PASSES):
+                for t in range(PACK):
+                    cols = slice(P * t, P * (t + 1))
                     nc.tensor.matmul_mx(
                         bank[:, t, :], lhsT=codes[a][:, cols].bitcast(FP8X4), lhsT_scale=scales[a][:, cols],
                         rhs=v_w[g][:, a, 2 * j : 2 * (j + TOK)].bitcast(FP4X4),
-                        rhs_scale=v_sc[a][:, c * TOK : (c + 1) * TOK], start=(a == 0), stop=(a == PASSES - 1),
+                        rhs_scale=v_sc[a][:, c * TOK : (c + 1) * TOK],
+                        start=(a, t) == (0, 0), stop=(a, t) == (PASSES - 1, PACK - 1),
                     )
 
         h_c = keep([P, J], U32, "h_c")
@@ -199,8 +204,7 @@ def tile_list_modp_gsilu_resP_kernel(
 
         wu_codes = [wu_c[:, a, :] for a in range(PASSES)]
         wu_scale = [wu_s[:, a, :] for a in range(PASSES)]
-        early_up = keep([P, EARLY_UP, TOK, PACK], F32, "early_up")
-        later_up = keep([P, COPIED_UP - EARLY_UP, TOK, PACK], F32, "later_up", "tab_w")
+        copied_up = keep([P, COPIED_UP, TOK, PACK], F32, "copied_up", "tab_sc")
         h_bf = keep([P, TILES, TOK * PACK], BF16, "h_bf")
         for c in range(TILES):
             g_bank = ps3.tile([P, PACK, TOK], F32, name="g_bank")
@@ -213,9 +217,8 @@ def tile_list_modp_gsilu_resP_kernel(
                 act = keep([P, TOK, PACK], F32, "last_act")
             up = u_bank[:].rearrange("p t j -> p j t")
             if c < COPIED_UP:
-                copied = early_up[:, c] if c < EARLY_UP else later_up[:, c - EARLY_UP]
-                nc.scalar.copy(copied, up)
-                up = copied
+                nc.scalar.copy(copied_up[:, c], up)
+                up = copied_up[:, c]
             nc.scalar.activation(act[:], g_bank[:].rearrange("p t j -> p j t"), SILU, bias=bias[:])
             nc.vector.tensor_tensor(h_bf[:, c, :].rearrange("p (j t) -> p j t", t=PACK), up, act[:], MULT)
             if c + 1 in QUANTISE_FROM:
@@ -225,7 +228,7 @@ def tile_list_modp_gsilu_resP_kernel(
                     h_bf[:, c0 : c + 1, :].rearrange("p c x -> p (c x)"),
                 )
         pick(0, HALF, "last_act")
-        two.append(keep([P, T], F32, "page_odd", "wg_bf1"))
+        two.append(place([P, T], F32, "page_odd", 3 * N))
         nc.gpsimd.memset(two[1][:], 0.0)
         def turn(i, j0):
             t_bank = ps2.tile([P, HALF], F32, name="t_bank", tag="y_bank")

@@ -27,8 +27,10 @@ TILES = J // TOK
 HALF = J // 2
 CHUNK = 512
 SCALAR_GROUPS = 48
-QUANTISE_FROM = {4: 0, 6: 4, 8: 6}
-COPIED_UP = TILES - 3
+SUM_BANKS = 3
+COPIED_UP = TILES - SUM_BANKS
+PIECES = ((0, J // 4), (J // 4, HALF), (HALF, J))
+ACT_TILES = 6
 
 
 def tile_list_modp_gsilu_resP_kernel(
@@ -38,9 +40,9 @@ def tile_list_modp_gsilu_resP_kernel(
     with ExitStack() as ctx:
         held = ctx.enter_context(tc.tile_pool(name="held", bufs=1))
         late = ctx.enter_context(tc.tile_pool(name="late", bufs=1))
-        ring = ctx.enter_context(tc.tile_pool(name="ring", bufs=6))
+        ring = ctx.enter_context(tc.tile_pool(name="ring", bufs=ACT_TILES))
         ps2 = ctx.enter_context(tc.psum_pool(name="ps2", bufs=2))
-        ps3 = ctx.enter_context(tc.psum_pool(name="ps3", bufs=3))
+        ps3 = ctx.enter_context(tc.psum_pool(name="ps3", bufs=SUM_BANKS))
 
         def keep(shape, dtype, name, after=None):
             return held.tile(shape, dtype, name=name, tag=after or name, align_bytes=64)
@@ -114,13 +116,13 @@ def tile_list_modp_gsilu_resP_kernel(
         wg_raw.append(keep([P, PACK, R], F32, "wg_raw1", "tab_sc"))
         nc.sync.dma_start(wg_raw[1][:], wg_rows[1])
 
-        w_bank = ps2.tile([P, P], F32, name="w_bank", tag="y_bank")
+        w_bank = ps2.tile([P, P], F32, name="w_bank", tag="t_bank")
         nc.tensor.transpose(w_bank[:], w_rows[:], ident[:])
         w_col = keep([P, TILES], F32, "w_col")
         nc.scalar.copy(w_col[:], w_bank[:, 0:TILES])
         gate = keep([P, J], F32, "gate")
         for j0 in range(0, J, HALF):
-            gate_bank = ps2.tile([P, HALF], F32, name="gate_bank", tag="y_bank")
+            gate_bank = ps2.tile([P, HALF], F32, name="gate_bank", tag="t_bank")
             for j in range(0, HALF, TOK):
                 c = (j0 + j) // TOK
                 nc.tensor.transpose(gate_bank[:, j : j + TOK], w_col[:, c : c + 1].to_broadcast([P, P]), ident[:])
@@ -149,6 +151,7 @@ def tile_list_modp_gsilu_resP_kernel(
             wg_c.append(keep([P, R], U32, "wg_c%d" % a))
             wg_s.append(keep([P, R], U8, "wg_s%d" % a))
             nc.vector.quantize_mx(wg_c[a][:].bitcast(FP8X4), wg_s[a][:], wg_bf[:])
+
         load_res(2, "tab_w")
         load_res(3, "wg_bf0")
         wd_w = place([P, 2 * N], U8, "wd_w", 0)
@@ -160,8 +163,8 @@ def tile_list_modp_gsilu_resP_kernel(
         for q in range(4):
             nc.sync.dma_start(wd_s[32 * q : 32 * q + 4, :].bitcast(I32), wd_scales[0, 4 * q : 4 * q + 4, :].bitcast(I32))
 
-        two = [keep([P, T], F32, "page_even")]
-        nc.vector.memset(two[0][:], 0.0)
+        pages = [keep([P, T], F32, "page_0")]
+        nc.vector.memset(pages[0][:], 0.0)
         rw = {}
 
         def pick(i, step, after=None):
@@ -221,34 +224,37 @@ def tile_list_modp_gsilu_resP_kernel(
                 up = copied_up[:, c]
             nc.scalar.activation(act[:], g_bank[:].rearrange("p t j -> p j t"), SILU, bias=bias[:])
             nc.vector.tensor_tensor(h_bf[:, c, :].rearrange("p (j t) -> p j t", t=PACK), up, act[:], MULT)
-            if c + 1 in QUANTISE_FROM:
-                c0 = QUANTISE_FROM[c + 1]
+            if (c + 1) * TOK % HALF == 0:
+                half = slice((c + 1) * TOK - HALF, (c + 1) * TOK)
                 nc.vector.quantize_mx(
-                    h_c[:, c0 * TOK : (c + 1) * TOK].bitcast(FP8X4), h_s[:, c0 * TOK : (c + 1) * TOK],
-                    h_bf[:, c0 : c + 1, :].rearrange("p c x -> p (c x)"),
+                    h_c[:, half].bitcast(FP8X4), h_s[:, half],
+                    h_bf[:, c + 1 - TILES // 2 : c + 1, :].rearrange("p c x -> p (c x)"),
                 )
-        pick(0, HALF, "last_act")
-        two.append(place([P, T], F32, "page_odd", 3 * N))
-        nc.gpsimd.memset(two[1][:], 0.0)
-        def turn(i, j0):
-            t_bank = ps2.tile([P, HALF], F32, name="t_bank", tag="y_bank")
-            for j in range(0, HALF, TOK):
-                nc.tensor.transpose(t_bank[:, j : j + TOK], y_tok[(j0 + j) // TOK][:, i, :], ident[:])
-            nc.scalar.copy(yw[:, i, j0 : j0 + HALF], t_bank[:])
 
-        for j0 in range(0, J, HALF):
-            for c in range(j0 // TOK, (j0 + HALF) // TOK):
-                second_product(c)
-            turn(0, j0)
-        for i in range(1, PACK):
-            for j0 in range(0, J, HALF):
-                turn(i, j0)
+        pick(0, HALF, "last_act")
+        pages.append(keep([P, T], F32, "page_1", "h_bf"))
+        pages.append(place([P, T], F32, "page_2", 3 * N))
+        for page in pages[1:]:
+            nc.gpsimd.memset(page[:], 0.0)
+
+        def turn(i, j0, j1):
+            t_bank = ps2.tile([P, j1 - j0], F32, name="t_bank", tag="t_bank")
+            for j in range(j0, j1, TOK):
+                nc.tensor.transpose(t_bank[:, j - j0 : j - j0 + TOK], y_tok[j // TOK][:, i, :], ident[:])
+            nc.scalar.copy(yw[:, i, j0:j1], t_bank[:])
 
         def put(i, j0, j1):
-            nc.vector.tensor_tensor(two[i % 2][:].indirect(listed(j0, j1)), rw[i][:, j0:j1], yw[:, i, j0:j1], ADD)
+            nc.vector.tensor_tensor(pages[i % len(pages)][:].indirect(listed(j0, j1)), rw[i][:, j0:j1], yw[:, i, j0:j1], ADD)
 
-        put(0, 0, HALF)
-        put(0, HALF, J)
+        for j0, j1 in PIECES:
+            for c in range(j0 // TOK, j1 // TOK):
+                second_product(c)
+            for i in range(2):
+                turn(i, j0, j1)
+                put(i, j0, j1)
+        for i in range(2, PACK):
+            for j0 in range(0, J, HALF):
+                turn(i, j0, j0 + HALF)
 
         chunks = [slice(lo, lo + CHUNK) for lo in range(0, T, CHUNK)]
         on_vector = len(chunks) // 2
@@ -259,11 +265,11 @@ def tile_list_modp_gsilu_resP_kernel(
         pairs = [keep([P, 2, CHUNK, 2], BF16, "pairs%d" % c, "y_tok%d" % c) for c in range(len(chunks))]
         out_rows = out_0.rearrange("(p i) t -> p i t", i=PACK)
         for i in range(PACK):
-            if i > 0:
+            if i > 1:
                 put(i, 0, J)
-            nc.sync.dma_start(out_rows[:, i, :], two[i % 2][:])
+            nc.sync.dma_start(out_rows[:, i, :], pages[i % len(pages)][:])
             for c, cols in enumerate(chunks):
-                values = two[i % 2][:, cols]
+                values = pages[i % len(pages)][:, cols]
                 if i == 2:
                     nc.scalar.copy(pairs[c][:, 1], values.unsqueeze(2).to_broadcast([P, CHUNK, 2]))
                 elif i == 3 and c < on_vector:

@@ -270,18 +270,22 @@ def tile_list_modp_gsilu_resP_kernel(
             nc.sync.dma_start(out_rows[:, i, :], pages[i % len(pages)][:])
             for c, cols in enumerate(chunks):
                 values = pages[i % len(pages)][:, cols]
-                if i == 2:
-                    nc.scalar.copy(pairs[c][:, 1], values.unsqueeze(2).to_broadcast([P, CHUNK, 2]))
-                elif i == 3 and c < on_vector:
-                    nc.vector.tensor_copy(pairs[c][:, 1, :, 1], values)
+                upper = woven[c][:, :, 2:4] if c < on_vector else pairs[c][:, 1]
+                if i < 2:
+                    nc.scalar.copy(pairs[c][:, 0, :, i], values)
+                elif i == 2:
+                    nc.scalar.copy(upper, values.unsqueeze(2).to_broadcast([P, CHUNK, 2]))
+                elif c < on_vector:
+                    nc.vector.tensor_copy(upper[:, :, 1], values)
                 else:
-                    nc.scalar.copy(pairs[c][:, i // 2, :, i % 2], values)
-        for c in range(len(chunks)):
-            words = pairs[c][:].rearrange("p w t e -> p w (t e)")
-            if c < on_vector:
-                nc.vector.tensor_copy(woven[c][:].bitcast(I32), words.bitcast(I32).rearrange("p w t -> p t w"))
-            else:
-                nc.scalar.copy(woven[c][:].bitcast(U32), words.bitcast(U32).rearrange("p w t -> p t w"))
+                    nc.scalar.copy(upper[:, :, 1], values)
+            if i == 1:
+                for c in range(on_vector):
+                    lower = pairs[c][:, 0].rearrange("p t e -> p (t e)").bitcast(U32)
+                    nc.scalar.copy(woven[c][:].bitcast(U32), lower.unsqueeze(2).to_broadcast([P, CHUNK, 2]))
+        for c in range(on_vector, len(chunks)):
+            words = pairs[c][:].rearrange("p w t e -> p w (t e)").bitcast(U32)
+            nc.scalar.copy(woven[c][:].bitcast(U32), words.rearrange("p w t -> p t w"))
 
         out_c = keep([P, T], U32, "out_c")
         out_s = keep([P, T], U8, "out_s")

@@ -27,10 +27,8 @@ TILES = J // TOK
 HALF = J // 2
 CHUNK = 512
 SCALAR_GROUPS = 48
-SUM_BANKS = 3
-COPIED_UP = TILES - SUM_BANKS
+ON_GPSIMD = 2
 PIECES = ((0, J // 4), (J // 4, HALF), (HALF, J))
-ACT_TILES = 6
 
 
 def tile_list_modp_gsilu_resP_kernel(
@@ -40,15 +38,16 @@ def tile_list_modp_gsilu_resP_kernel(
     with ExitStack() as ctx:
         held = ctx.enter_context(tc.tile_pool(name="held", bufs=1))
         late = ctx.enter_context(tc.tile_pool(name="late", bufs=1))
-        ring = ctx.enter_context(tc.tile_pool(name="ring", bufs=ACT_TILES))
-        ps2 = ctx.enter_context(tc.psum_pool(name="ps2", bufs=2))
-        ps3 = ctx.enter_context(tc.psum_pool(name="ps3", bufs=SUM_BANKS))
+        psum = ctx.enter_context(tc.psum_pool(name="psum", bufs=1))
 
         def keep(shape, dtype, name, after=None):
             return held.tile(shape, dtype, name=name, tag=after or name, align_bytes=64)
 
         def place(shape, dtype, name, offset):
             return late.tile(shape, dtype, name=name, offset=offset, align_bytes=64)
+
+        def bank(shape, name, b):
+            return psum.tile(shape, F32, name=name, tag="bank%d" % b)
 
         offsets = held.tile([P, J // 16], U16, name="offsets")
         nc.sync.dma_start(offsets[:], offs)
@@ -116,13 +115,13 @@ def tile_list_modp_gsilu_resP_kernel(
         wg_raw.append(keep([P, PACK, R], F32, "wg_raw1", "tab_sc"))
         nc.sync.dma_start(wg_raw[1][:], wg_rows[1])
 
-        w_bank = ps2.tile([P, P], F32, name="w_bank", tag="t_bank")
+        w_bank = bank([P, P], "w_bank", 5)
         nc.tensor.transpose(w_bank[:], w_rows[:], ident[:])
         w_col = keep([P, TILES], F32, "w_col")
         nc.scalar.copy(w_col[:], w_bank[:, 0:TILES])
         gate = keep([P, J], F32, "gate")
         for j0 in range(0, J, HALF):
-            gate_bank = ps2.tile([P, HALF], F32, name="gate_bank", tag="t_bank")
+            gate_bank = bank([P, HALF], "gate_bank", 6 + j0 // HALF)
             for j in range(0, HALF, TOK):
                 c = (j0 + j) // TOK
                 nc.tensor.transpose(gate_bank[:, j : j + TOK], w_col[:, c : c + 1].to_broadcast([P, P]), ident[:])
@@ -176,13 +175,13 @@ def tile_list_modp_gsilu_resP_kernel(
         for i in range(1, PACK):
             pick(i, J)
 
-        def first_product(bank, codes, scales, c):
+        def first_product(sums, codes, scales, c):
             g, j = divmod(c * TOK, HALF)
             for a in range(PASSES):
                 for t in range(PACK):
                     cols = slice(P * t, P * (t + 1))
                     nc.tensor.matmul_mx(
-                        bank[:, t, :], lhsT=codes[a][:, cols].bitcast(FP8X4), lhsT_scale=scales[a][:, cols],
+                        sums[:, t, :], lhsT=codes[a][:, cols].bitcast(FP8X4), lhsT_scale=scales[a][:, cols],
                         rhs=v_w[g][:, a, 2 * j : 2 * (j + TOK)].bitcast(FP4X4),
                         rhs_scale=v_sc[a][:, c * TOK : (c + 1) * TOK],
                         start=(a, t) == (0, 0), stop=(a, t) == (PASSES - 1, PACK - 1),
@@ -194,7 +193,7 @@ def tile_list_modp_gsilu_resP_kernel(
         yw = keep([P, PACK, J], F32, "yw")
 
         def second_product(c):
-            y_bank = ps3.tile([P, N], F32, name="y_bank", tag="g_bank")
+            y_bank = bank([P, N], "y_bank", c % 2)
             tok = slice(c * TOK, (c + 1) * TOK)
             nc.tensor.matmul_mx(
                 y_bank[:], lhsT=h_c[:, tok].bitcast(FP8X4), lhsT_scale=h_s[:, tok],
@@ -207,38 +206,41 @@ def tile_list_modp_gsilu_resP_kernel(
 
         wu_codes = [wu_c[:, a, :] for a in range(PASSES)]
         wu_scale = [wu_s[:, a, :] for a in range(PASSES)]
-        copied_up = keep([P, COPIED_UP, TOK, PACK], F32, "copied_up", "tab_sc")
-        h_bf = keep([P, TILES, TOK * PACK], BF16, "h_bf")
-        for c in range(TILES):
-            g_bank = ps3.tile([P, PACK, TOK], F32, name="g_bank")
-            u_bank = ps3.tile([P, PACK, TOK], F32, name="u_bank")
-            first_product(u_bank, wu_codes, wu_scale, c)
-            first_product(g_bank, wg_c, wg_s, c)
-            if c < TILES - 1:
-                act = ring.tile([P, TOK, PACK], F32, name="act")
-            else:
-                act = keep([P, TOK, PACK], F32, "last_act")
-            up = u_bank[:].rearrange("p t j -> p j t")
-            if c < COPIED_UP:
-                nc.scalar.copy(copied_up[:, c], up)
-                up = copied_up[:, c]
-            nc.scalar.activation(act[:], g_bank[:].rearrange("p t j -> p j t"), SILU, bias=bias[:])
-            nc.vector.tensor_tensor(h_bf[:, c, :].rearrange("p (j t) -> p j t", t=PACK), up, act[:], MULT)
-            if (c + 1) * TOK % HALF == 0:
-                half = slice((c + 1) * TOK - HALF, (c + 1) * TOK)
-                nc.vector.quantize_mx(
-                    h_c[:, half].bitcast(FP8X4), h_s[:, half],
-                    h_bf[:, c + 1 - TILES // 2 : c + 1, :].rearrange("p c x -> p (c x)"),
-                )
+        copied_up = keep([P, ON_GPSIMD, TOK, PACK], F32, "copied_up", "tab_sc")
+        up = []
 
-        pick(0, HALF, "last_act")
-        pages.append(keep([P, T], F32, "page_1", "h_bf"))
+        def up_sums(c):
+            u_bank = bank([P, PACK, TOK], "u_bank", c if c < ON_GPSIMD else 4 + (c - ON_GPSIMD) % 4)
+            first_product(u_bank, wu_codes, wu_scale, c)
+            up.append(u_bank[:].rearrange("p t j -> p j t"))
+
+        for c in range(ON_GPSIMD):
+            up_sums(c)
+            nc.scalar.copy(copied_up[:, c], up[c])
+            up[c] = copied_up[:, c]
+        h_bf = keep([P, TILES, TOK * PACK], BF16, "h_bf", "wg_bf0")
+        for c in range(TILES):
+            g_bank = bank([P, PACK, TOK], "g_bank", (c + ON_GPSIMD) % 4)
+            first_product(g_bank, wg_c, wg_s, c)
+            if len(up) < ON_GPSIMD + 4 or len(up) == c:
+                up_sums(len(up))
+            act = keep([P, TOK, PACK], F32, "act%d" % c)
+            nc.scalar.activation(act[:], g_bank[:].rearrange("p t j -> p j t"), SILU, bias=bias[:])
+            engine = nc.gpsimd if c < ON_GPSIMD else nc.vector
+            engine.tensor_tensor(h_bf[:, c, :].rearrange("p (j t) -> p j t", t=PACK), up[c], act[:], MULT)
+        for g in range(2):
+            half = slice(g * HALF, (g + 1) * HALF)
+            tiles = h_bf[:, g * TILES // 2 : (g + 1) * TILES // 2, :]
+            nc.vector.quantize_mx(h_c[:, half].bitcast(FP8X4), h_s[:, half], tiles.rearrange("p c x -> p (c x)"))
+
+        pick(0, HALF, "act%d" % (TILES - 1))
+        pages.append(keep([P, T], F32, "page_1", "wg_bf0"))
         pages.append(place([P, T], F32, "page_2", 3 * N))
         for page in pages[1:]:
             nc.gpsimd.memset(page[:], 0.0)
 
         def turn(i, j0, j1):
-            t_bank = ps2.tile([P, j1 - j0], F32, name="t_bank", tag="t_bank")
+            t_bank = bank([P, j1 - j0], "t_bank", 2 + i)
             for j in range(j0, j1, TOK):
                 nc.tensor.transpose(t_bank[:, j - j0 : j - j0 + TOK], y_tok[j // TOK][:, i, :], ident[:])
             nc.scalar.copy(yw[:, i, j0:j1], t_bank[:])

@@ -26,7 +26,8 @@ TOK = 128
 TILES = J // TOK
 HALF = J // 2
 CHUNK = 512
-SCALAR_GROUPS = 48
+SCALAR_GROUPS = (64, 48)
+KIB = 1024
 ON_GPSIMD = 2
 PIECES = ((0, J // 4), (J // 4, HALF), (HALF, J))
 
@@ -74,10 +75,11 @@ def tile_list_modp_gsilu_resP_kernel(
         nc.sync.dma_start(w_rows[0:TILES, :], wgo[0].rearrange("(c j) -> c j", j=TOK))
 
         wg_rows = wg.rearrange("(a p j) r -> a p j r", p=P, j=PACK)
+        shared = 18 * KIB
+        wu_raw = place([P, PASSES, R], I32, "wu_raw", shared)
+        nc.sync.dma_start(wu_raw[:], wu_words.rearrange("a p r i -> p a (r i)").bitcast(I32))
         wg_raw = [keep([P, PACK, R], F32, "wg_raw0")]
         nc.sync.dma_start(wg_raw[0][:], wg_rows[0])
-        wu_raw = keep([P, PASSES, R], I32, "wu_raw")
-        nc.sync.dma_start(wu_raw[:], wu_words.rearrange("a p r i -> p a (r i)").bitcast(I32))
 
         rT_rows = rT.rearrange("(p i) t -> p i t", i=PACK)
         res = {}
@@ -86,7 +88,6 @@ def tile_list_modp_gsilu_resP_kernel(
             res[i] = keep([P, T], F32, "res%d" % i, after)
             nc.sync.dma_start(res[i][:], rT_rows[:, i, :])
 
-        load_res(1)
         ident = keep([P, P], F32, "ident")
         make_identity(nc, ident[:])
         for lo, hi in ((0, 16), (32, 48), (64, 128)):
@@ -114,6 +115,7 @@ def tile_list_modp_gsilu_resP_kernel(
 
         wg_raw.append(keep([P, PACK, R], F32, "wg_raw1", "tab_sc"))
         nc.sync.dma_start(wg_raw[1][:], wg_rows[1])
+        load_res(1, "tab_w")
 
         w_bank = bank([P, P], "w_bank", 5)
         nc.tensor.transpose(w_bank[:], w_rows[:], ident[:])
@@ -133,47 +135,44 @@ def tile_list_modp_gsilu_resP_kernel(
             wu_s[:].rearrange("p a (t m) -> p a t m", t=PACK), wu_sc_raw[:].rearrange("p a (m t) -> p a t m", t=PACK)
         )
 
+        nc.scalar.copy(
+            wu_c[:].rearrange("p a (t c e) -> p a c t e", t=PACK, e=4),
+            wu_raw[:].bitcast(U32).rearrange("p a (c e t) -> p a c t e", t=PACK, e=4),
+        )
+        res[2] = place([P, T], F32, "res2", shared)
+        nc.sync.dma_start(res[2][:], rT_rows[:, 2, :])
+
         wg_c, wg_s = [], []
         for a in range(PASSES):
-            wg_bf = keep([P, R * PACK], BF16, "wg_bf0") if a == 0 else place([P, R * PACK], BF16, "wg_bf1", 0)
+            wg_bf = keep([P, R * PACK], BF16, "wg_bf0") if a == 0 else place([P, R * PACK], BF16, "wg_bf1", 7 * KIB)
             dst = wg_bf[:].rearrange("p (t m j) -> p m t j", t=PACK, j=PACK)
             src = wg_raw[a][:].rearrange("p j (m t) -> p m t j", t=PACK)
-            if a == 0:
-                nc.scalar.copy(dst, src)
-                nc.scalar.copy(
-                    wu_c[:].rearrange("p a (t c e) -> p a c t e", t=PACK, e=4),
-                    wu_raw[:].bitcast(U32).rearrange("p a (c e t) -> p a c t e", t=PACK, e=4),
-                )
-            else:
-                nc.scalar.copy(dst[:, :SCALAR_GROUPS], src[:, :SCALAR_GROUPS])
-                nc.vector.tensor_copy(dst[:, SCALAR_GROUPS:], src[:, SCALAR_GROUPS:])
+            nc.scalar.copy(dst[:, : SCALAR_GROUPS[a]], src[:, : SCALAR_GROUPS[a]])
+            nc.vector.tensor_copy(dst[:, SCALAR_GROUPS[a] :], src[:, SCALAR_GROUPS[a] :])
             wg_c.append(keep([P, R], U32, "wg_c%d" % a))
             wg_s.append(keep([P, R], U8, "wg_s%d" % a))
             nc.vector.quantize_mx(wg_c[a][:].bitcast(FP8X4), wg_s[a][:], wg_bf[:])
 
-        load_res(2, "tab_w")
-        load_res(3, "wg_bf0")
-        wd_w = place([P, 2 * N], U8, "wd_w", 0)
+        load_res(3, "wg_raw0")
+        wd_w = place([P, 2 * N], U8, "wd_w", 8 * KIB)
         nc.sync.dma_start(wd_w[:].bitcast(I32), wd_words[0].bitcast(I32))
-        res[0] = place([P, T], F32, "res0", 3 * N)
+        res[0] = place([P, T], F32, "res0", 9 * KIB + N)
         nc.sync.dma_start(res[0][:], rT_rows[:, 0, :])
-        wd_s = place([P, N], U8, "wd_s", 2 * N)
+        wd_s = place([P, N], U8, "wd_s", 9 * KIB)
         nc.gpsimd.memset(wd_s[:].bitcast(I32), 0)
         for q in range(4):
             nc.sync.dma_start(wd_s[32 * q : 32 * q + 4, :].bitcast(I32), wd_scales[0, 4 * q : 4 * q + 4, :].bitcast(I32))
 
-        pages = [keep([P, T], F32, "page_0")]
-        nc.vector.memset(pages[0][:], 0.0)
+        pages = [place([P, T], F32, "page_0", 0)]
+        nc.gpsimd.memset(pages[0][:], 0.0)
         rw = {}
 
-        def pick(i, step, after=None):
-            rw[i] = keep([P, J], F32, "rw%d" % i, after)
-            for j0 in range(0, J, step):
-                cols = slice(j0, j0 + step)
-                nc.vector.tensor_tensor(rw[i][:, cols], res[i][:].indirect(listed(j0, j0 + step)), gate[:, cols], MULT)
+        def pick(i, j0, j1):
+            nc.vector.tensor_tensor(rw[i][:, j0:j1], res[i][:].indirect(listed(j0, j1)), gate[:, j0:j1], MULT)
 
-        for i in range(1, PACK):
-            pick(i, J)
+        for i in range(1, 3):
+            rw[i] = keep([P, J], F32, "rw%d" % i)
+            pick(i, 0, J)
 
         def first_product(sums, codes, scales, c):
             g, j = divmod(c * TOK, HALF)
@@ -218,7 +217,13 @@ def tile_list_modp_gsilu_resP_kernel(
             up_sums(c)
             nc.scalar.copy(copied_up[:, c], up[c])
             up[c] = copied_up[:, c]
-        h_bf = keep([P, TILES, TOK * PACK], BF16, "h_bf", "wg_bf0")
+        h_bf = place([P, TILES, TOK * PACK], BF16, "h_bf", shared)
+
+        def quantise_h(g):
+            half = slice(g * HALF, (g + 1) * HALF)
+            tiles = h_bf[:, g * TILES // 2 : (g + 1) * TILES // 2, :]
+            nc.vector.quantize_mx(h_c[:, half].bitcast(FP8X4), h_s[:, half], tiles.rearrange("p c x -> p (c x)"))
+
         for c in range(TILES):
             g_bank = bank([P, PACK, TOK], "g_bank", (c + ON_GPSIMD) % 4)
             first_product(g_bank, wg_c, wg_s, c)
@@ -228,14 +233,18 @@ def tile_list_modp_gsilu_resP_kernel(
             nc.scalar.activation(act[:], g_bank[:].rearrange("p t j -> p j t"), SILU, bias=bias[:])
             engine = nc.gpsimd if c < ON_GPSIMD else nc.vector
             engine.tensor_tensor(h_bf[:, c, :].rearrange("p (j t) -> p j t", t=PACK), up[c], act[:], MULT)
-        for g in range(2):
-            half = slice(g * HALF, (g + 1) * HALF)
-            tiles = h_bf[:, g * TILES // 2 : (g + 1) * TILES // 2, :]
-            nc.vector.quantize_mx(h_c[:, half].bitcast(FP8X4), h_s[:, half], tiles.rearrange("p c x -> p (c x)"))
+            if c == TILES - 2:
+                quantise_h(0)
 
-        pick(0, HALF, "act%d" % (TILES - 1))
-        pages.append(keep([P, T], F32, "page_1", "wg_bf0"))
-        pages.append(place([P, T], F32, "page_2", 3 * N))
+        rw[3] = keep([P, J], F32, "rw3", "act%d" % (TILES - 1))
+        pick(3, 0, HALF)
+        quantise_h(1)
+        pick(3, HALF, J)
+        rw[0] = place([P, J], F32, "rw0", shared)
+        pick(0, 0, HALF)
+        pick(0, HALF, J)
+        pages.append(place([P, T], F32, "page_1", shared + 4 * KIB))
+        pages.append(place([P, T], F32, "page_2", 9 * KIB + N))
         for page in pages[1:]:
             nc.gpsimd.memset(page[:], 0.0)
 

@@ -28,8 +28,9 @@ HALF = J // 2
 CHUNK = 512
 SCALAR_GROUPS = (64, 48)
 KIB = 1024
+LAST = 128
 ON_GPSIMD = 2
-PIECES = ((0, J // 4), (J // 4, HALF), (HALF, J))
+PIECES = ((0, HALF), (HALF, J))
 
 
 def tile_list_modp_gsilu_resP_kernel(
@@ -153,11 +154,11 @@ def tile_list_modp_gsilu_resP_kernel(
             wg_s.append(keep([P, R], U8, "wg_s%d" % a))
             nc.vector.quantize_mx(wg_c[a][:].bitcast(FP8X4), wg_s[a][:], wg_bf[:])
 
-        load_res(3, "wg_raw0")
+        load_res(0, "wg_raw0")
         wd_w = place([P, 2 * N], U8, "wd_w", 8 * KIB)
         nc.sync.dma_start(wd_w[:].bitcast(I32), wd_words[0].bitcast(I32))
-        res[0] = place([P, T], F32, "res0", 9 * KIB + N)
-        nc.sync.dma_start(res[0][:], rT_rows[:, 0, :])
+        res[3] = place([P, T], F32, "res3", 9 * KIB + N)
+        nc.sync.dma_start(res[3][:], rT_rows[:, 3, :])
         wd_s = place([P, N], U8, "wd_s", 9 * KIB)
         nc.gpsimd.memset(wd_s[:].bitcast(I32), 0)
         for q in range(4):
@@ -236,13 +237,12 @@ def tile_list_modp_gsilu_resP_kernel(
             if c == TILES - 2:
                 quantise_h(0)
 
-        rw[3] = keep([P, J], F32, "rw3", "act%d" % (TILES - 1))
-        pick(3, 0, HALF)
-        quantise_h(1)
-        pick(3, HALF, J)
-        rw[0] = place([P, J], F32, "rw0", shared)
+        rw[0] = keep([P, J], F32, "rw0", "act%d" % (TILES - 2))
         pick(0, 0, HALF)
+        quantise_h(1)
         pick(0, HALF, J)
+        rw[3] = place([P, J], F32, "rw3", shared)
+        pick(3, 0, J)
         pages.append(place([P, T], F32, "page_1", shared + 4 * KIB))
         pages.append(place([P, T], F32, "page_2", 9 * KIB + N))
         for page in pages[1:]:
@@ -301,8 +301,10 @@ def tile_list_modp_gsilu_resP_kernel(
         out_c = keep([P, T], U32, "out_c")
         out_s = keep([P, T], U8, "out_s")
         words_out = out_1[0].rearrange("p t b -> p (t b)").bitcast(I32)
-        for c, cols in enumerate(chunks):
-            nc.vector.quantize_mx(out_c[:, cols].bitcast(FP8X4), out_s[:, cols], woven[c][:].rearrange("p t i -> p (t i)"))
-            nc.sync.dma_start(words_out[:, cols], out_c[:, cols].bitcast(I32))
+        cuts = list(range(0, T, CHUNK)) + [T - LAST, T]
+        for lo, hi in zip(cuts, cuts[1:]):
+            values = woven[lo // CHUNK][:, lo % CHUNK : lo % CHUNK + hi - lo].rearrange("p t i -> p (t i)")
+            nc.vector.quantize_mx(out_c[:, lo:hi].bitcast(FP8X4), out_s[:, lo:hi], values)
+            nc.sync.dma_start(words_out[:, lo:hi], out_c[:, lo:hi].bitcast(I32))
         for q in range(4):
             nc.scalar.dma_start(out_2[0, 4 * q : 4 * q + 4, :].bitcast(I32), out_s[32 * q : 32 * q + 4, :].bitcast(I32))

@@ -29,8 +29,6 @@ CHUNK = 512
 SCALAR_GROUPS = (64, 48)
 KIB = 1024
 LAST = 128
-ON_GPSIMD = 2
-PIECES = ((0, HALF), (HALF, J))
 
 
 def tile_list_modp_gsilu_resP_kernel(
@@ -76,7 +74,7 @@ def tile_list_modp_gsilu_resP_kernel(
         nc.sync.dma_start(w_rows[0:TILES, :], wgo[0].rearrange("(c j) -> c j", j=TOK))
 
         wg_rows = wg.rearrange("(a p j) r -> a p j r", p=P, j=PACK)
-        shared = 18 * KIB
+        shared = 26 * KIB
         wu_raw = place([P, PASSES, R], I32, "wu_raw", shared)
         nc.sync.dma_start(wu_raw[:], wu_words.rearrange("a p r i -> p a (r i)").bitcast(I32))
         wg_raw = [keep([P, PACK, R], F32, "wg_raw0")]
@@ -116,7 +114,7 @@ def tile_list_modp_gsilu_resP_kernel(
 
         wg_raw.append(keep([P, PACK, R], F32, "wg_raw1", "tab_sc"))
         nc.sync.dma_start(wg_raw[1][:], wg_rows[1])
-        load_res(1, "tab_w")
+        load_res(0, "tab_w")
 
         w_bank = bank([P, P], "w_bank", 5)
         nc.tensor.transpose(w_bank[:], w_rows[:], ident[:])
@@ -140,12 +138,12 @@ def tile_list_modp_gsilu_resP_kernel(
             wu_c[:].rearrange("p a (t c e) -> p a c t e", t=PACK, e=4),
             wu_raw[:].bitcast(U32).rearrange("p a (c e t) -> p a c t e", t=PACK, e=4),
         )
-        res[2] = place([P, T], F32, "res2", shared)
-        nc.sync.dma_start(res[2][:], rT_rows[:, 2, :])
+        res[1] = place([P, T], F32, "res1", shared)
+        nc.sync.dma_start(res[1][:], rT_rows[:, 1, :])
 
         wg_c, wg_s = [], []
         for a in range(PASSES):
-            wg_bf = keep([P, R * PACK], BF16, "wg_bf0") if a == 0 else place([P, R * PACK], BF16, "wg_bf1", 7 * KIB)
+            wg_bf = keep([P, R * PACK], BF16, "wg_bf0") if a == 0 else place([P, R * PACK], BF16, "wg_bf1", 8 * KIB)
             dst = wg_bf[:].rearrange("p (t m j) -> p m t j", t=PACK, j=PACK)
             src = wg_raw[a][:].rearrange("p j (m t) -> p m t j", t=PACK)
             nc.scalar.copy(dst[:, : SCALAR_GROUPS[a]], src[:, : SCALAR_GROUPS[a]])
@@ -154,26 +152,22 @@ def tile_list_modp_gsilu_resP_kernel(
             wg_s.append(keep([P, R], U8, "wg_s%d" % a))
             nc.vector.quantize_mx(wg_c[a][:].bitcast(FP8X4), wg_s[a][:], wg_bf[:])
 
-        load_res(0, "wg_raw0")
+        load_res(2, "wg_raw0")
         wd_w = place([P, 2 * N], U8, "wd_w", 8 * KIB)
         nc.sync.dma_start(wd_w[:].bitcast(I32), wd_words[0].bitcast(I32))
-        res[3] = place([P, T], F32, "res3", 9 * KIB + N)
+        last = 9 * KIB + N
+        res[3] = place([P, T], F32, "res3", last)
         nc.sync.dma_start(res[3][:], rT_rows[:, 3, :])
         wd_s = place([P, N], U8, "wd_s", 9 * KIB)
         nc.gpsimd.memset(wd_s[:].bitcast(I32), 0)
         for q in range(4):
             nc.sync.dma_start(wd_s[32 * q : 32 * q + 4, :].bitcast(I32), wd_scales[0, 4 * q : 4 * q + 4, :].bitcast(I32))
 
-        pages = [place([P, T], F32, "page_0", 0)]
-        nc.gpsimd.memset(pages[0][:], 0.0)
         rw = {}
 
-        def pick(i, j0, j1):
-            nc.vector.tensor_tensor(rw[i][:, j0:j1], res[i][:].indirect(listed(j0, j1)), gate[:, j0:j1], MULT)
-
-        for i in range(1, 3):
-            rw[i] = keep([P, J], F32, "rw%d" % i)
-            pick(i, 0, J)
+        def pick(i, after=None):
+            rw[i] = keep([P, J], F32, "rw%d" % i, after)
+            nc.vector.tensor_tensor(rw[i][:], res[i][:].indirect(offsets[:]), gate[:], MULT)
 
         def first_product(sums, codes, scales, c):
             g, j = divmod(c * TOK, HALF)
@@ -189,11 +183,51 @@ def tile_list_modp_gsilu_resP_kernel(
 
         h_c = keep([P, J], U32, "h_c")
         h_s = keep([P, J], U8, "h_s")
+        wu_codes = [wu_c[:, a, :] for a in range(PASSES)]
+        wu_scale = [wu_s[:, a, :] for a in range(PASSES)]
+        copied_up = keep([P, 2, TOK, PACK], F32, "copied_up", "tab_sc")
+        group = TILES // 2
+
+        def hidden(g, up_banks, gate_banks, h_at):
+            tiles = range(g * group, (g + 1) * group)
+            up = {}
+            for c, b in zip(tiles, up_banks):
+                u_bank = bank([P, PACK, TOK], "u_bank", b)
+                first_product(u_bank, wu_codes, wu_scale, c)
+                up[c] = u_bank[:].rearrange("p t j -> p j t")
+                if c == tiles[0]:
+                    nc.scalar.copy(copied_up[:, g], up[c])
+                    up[c] = copied_up[:, g]
+            h_bf = place([P, group, TOK * PACK], BF16, "h_bf%d" % g, h_at)
+            for c, b in zip(tiles, gate_banks):
+                g_bank = bank([P, PACK, TOK], "g_bank", b)
+                first_product(g_bank, wg_c, wg_s, c)
+                act = keep([P, TOK, PACK], F32, "act%d" % c)
+                nc.scalar.activation(act[:], g_bank[:].rearrange("p t j -> p j t"), SILU, bias=bias[:])
+                engine = nc.gpsimd if c == tiles[0] else nc.vector
+                engine.tensor_tensor(h_bf[:, c % group, :].rearrange("p (j t) -> p j t", t=PACK), up[c], act[:], MULT)
+            for lo, hi in ((0, group - 1), (group - 1, group)):
+                tok = slice(g * HALF + lo * TOK, g * HALF + hi * TOK)
+                nc.vector.quantize_mx(h_c[:, tok].bitcast(FP8X4), h_s[:, tok], h_bf[:, lo:hi, :].rearrange("p c x -> p (c x)"))
+
+        pick(0)
+        pick(1)
+        hidden(0, (0, 1, 2, 3), (4, 5, 6, 7), shared)
+        pages = [place([P, T], F32, "page_0", shared)]
+        nc.gpsimd.memset(pages[0][:], 0.0)
+        pick(2, "act3")
+        pick(3, "act2")
+        hidden(1, (0, 4, 5, 0), (6, 7, 6, 7), 14 * KIB)
+        pages.append(place([P, T], F32, "page_1", last))
+        pages.append(place([P, T], F32, "page_2", last + 8 * KIB))
+        for page in pages[1:]:
+            nc.gpsimd.memset(page[:], 0.0)
+
         y_tok = {}
         yw = keep([P, PACK, J], F32, "yw")
 
-        def second_product(c):
-            y_bank = bank([P, N], "y_bank", c % 2)
+        def second_product(c, b):
+            y_bank = bank([P, N], "y_bank", b)
             tok = slice(c * TOK, (c + 1) * TOK)
             nc.tensor.matmul_mx(
                 y_bank[:], lhsT=h_c[:, tok].bitcast(FP8X4), lhsT_scale=h_s[:, tok],
@@ -204,68 +238,22 @@ def tile_list_modp_gsilu_resP_kernel(
                 y_tok[c][:], y_bank[:].rearrange("p (m i) -> p i m", i=PACK), COPY, scale=w_col[:, c : c + 1]
             )
 
-        wu_codes = [wu_c[:, a, :] for a in range(PASSES)]
-        wu_scale = [wu_s[:, a, :] for a in range(PASSES)]
-        copied_up = keep([P, ON_GPSIMD, TOK, PACK], F32, "copied_up", "tab_sc")
-        up = []
-
-        def up_sums(c):
-            u_bank = bank([P, PACK, TOK], "u_bank", c if c < ON_GPSIMD else 4 + (c - ON_GPSIMD) % 4)
-            first_product(u_bank, wu_codes, wu_scale, c)
-            up.append(u_bank[:].rearrange("p t j -> p j t"))
-
-        for c in range(ON_GPSIMD):
-            up_sums(c)
-            nc.scalar.copy(copied_up[:, c], up[c])
-            up[c] = copied_up[:, c]
-        h_bf = place([P, TILES, TOK * PACK], BF16, "h_bf", shared)
-
-        def quantise_h(g):
-            half = slice(g * HALF, (g + 1) * HALF)
-            tiles = h_bf[:, g * TILES // 2 : (g + 1) * TILES // 2, :]
-            nc.vector.quantize_mx(h_c[:, half].bitcast(FP8X4), h_s[:, half], tiles.rearrange("p c x -> p (c x)"))
-
-        for c in range(TILES):
-            g_bank = bank([P, PACK, TOK], "g_bank", (c + ON_GPSIMD) % 4)
-            first_product(g_bank, wg_c, wg_s, c)
-            if len(up) < ON_GPSIMD + 4 or len(up) == c:
-                up_sums(len(up))
-            act = keep([P, TOK, PACK], F32, "act%d" % c)
-            nc.scalar.activation(act[:], g_bank[:].rearrange("p t j -> p j t"), SILU, bias=bias[:])
-            engine = nc.gpsimd if c < ON_GPSIMD else nc.vector
-            engine.tensor_tensor(h_bf[:, c, :].rearrange("p (j t) -> p j t", t=PACK), up[c], act[:], MULT)
-            if c == TILES - 2:
-                quantise_h(0)
-
-        rw[0] = keep([P, J], F32, "rw0", "act%d" % (TILES - 2))
-        pick(0, 0, HALF)
-        quantise_h(1)
-        pick(0, HALF, J)
-        rw[3] = place([P, J], F32, "rw3", shared)
-        pick(3, 0, J)
-        pages.append(place([P, T], F32, "page_1", shared + 4 * KIB))
-        pages.append(place([P, T], F32, "page_2", 9 * KIB + N))
-        for page in pages[1:]:
-            nc.gpsimd.memset(page[:], 0.0)
-
-        def turn(i, j0, j1):
-            t_bank = bank([P, j1 - j0], "t_bank", 2 + i)
-            for j in range(j0, j1, TOK):
-                nc.tensor.transpose(t_bank[:, j - j0 : j - j0 + TOK], y_tok[j // TOK][:, i, :], ident[:])
-            nc.scalar.copy(yw[:, i, j0:j1], t_bank[:])
+        def turn(i, g, b):
+            t_bank = bank([P, HALF], "t_bank", b)
+            for j in range(0, HALF, TOK):
+                nc.tensor.transpose(t_bank[:, j : j + TOK], y_tok[g * group + j // TOK][:, i, :], ident[:])
+            nc.scalar.copy(yw[:, i, g * HALF : (g + 1) * HALF], t_bank[:])
 
         def put(i, j0, j1):
             nc.vector.tensor_tensor(pages[i % len(pages)][:].indirect(listed(j0, j1)), rw[i][:, j0:j1], yw[:, i, j0:j1], ADD)
 
-        for j0, j1 in PIECES:
-            for c in range(j0 // TOK, j1 // TOK):
-                second_product(c)
+        for g, y_banks, t_banks in ((0, (6, 7), (1, 2, 3, 6)), (1, (1, 2), (7, 3, 6, 4))):
+            for c in range(g * group, (g + 1) * group):
+                second_product(c, y_banks[c % 2])
+            for i in range(PACK):
+                turn(i, g, t_banks[i])
             for i in range(2):
-                turn(i, j0, j1)
-                put(i, j0, j1)
-        for i in range(2, PACK):
-            for j0 in range(0, J, HALF):
-                turn(i, j0, j0 + HALF)
+                put(i, g * HALF, (g + 1) * HALF)
 
         chunks = [slice(lo, lo + CHUNK) for lo in range(0, T, CHUNK)]
         on_vector = len(chunks) // 2

@@ -25,10 +25,10 @@ PASSES = K // (P * PACK)
 TOK = 128
 TILES = J // TOK
 HALF = J // 2
-CHUNK = 512
 SCALAR_GROUPS = (64, 48)
 KIB = 1024
-LAST = 128
+CUTS = (0, 512, 1024, 1408, 1920, 2048)
+ON_VECTOR = 2
 
 
 def tile_list_modp_gsilu_resP_kernel(
@@ -255,44 +255,44 @@ def tile_list_modp_gsilu_resP_kernel(
             for i in range(2):
                 put(i, g * HALF, (g + 1) * HALF)
 
-        chunks = [slice(lo, lo + CHUNK) for lo in range(0, T, CHUNK)]
-        on_vector = len(chunks) // 2
-        woven = [
-            keep([P, CHUNK, PACK], BF16, "woven%d" % c, after)
-            for c, after in enumerate(("h_c", "h_s", "parted0", "parted1"))
-        ]
-        pairs = [keep([P, 2, CHUNK, 2], BF16, "pairs%d" % c, "y_tok%d" % c) for c in range(len(chunks))]
+        spans = [slice(lo, hi) for lo, hi in zip(CUTS, CUTS[1:])]
+        woven = [keep([P, s.stop - s.start, PACK], BF16, "woven%d" % n) for n, s in enumerate(spans)]
+        first = keep([P, 2, CUTS[1], 2], BF16, "first", "y_tok1")
+        pairs = keep([P, T - CUTS[1], 2], BF16, "pairs", "y_tok0")
+        words = pairs[:].rearrange("p t e -> p (t e)").bitcast(U32)
         out_rows = out_0.rearrange("(p i) t -> p i t", i=PACK)
         for i in range(PACK):
+            page = pages[i % len(pages)]
             if i > 1:
                 put(i, 0, J)
-            nc.sync.dma_start(out_rows[:, i, :], pages[i % len(pages)][:])
-            for c, cols in enumerate(chunks):
-                values = pages[i % len(pages)][:, cols]
-                upper = woven[c][:, :, 2:4] if c < on_vector else pairs[c][:, 1]
-                if i < 2:
-                    nc.scalar.copy(pairs[c][:, 0, :, i], values)
-                elif i == 2:
-                    nc.scalar.copy(upper, values.unsqueeze(2).to_broadcast([P, CHUNK, 2]))
-                elif c < on_vector:
-                    nc.vector.tensor_copy(upper[:, :, 1], values)
-                else:
-                    nc.scalar.copy(upper[:, :, 1], values)
-            if i == 1:
-                for c in range(on_vector):
-                    lower = pairs[c][:, 0].rearrange("p t e -> p (t e)").bitcast(U32)
-                    nc.scalar.copy(woven[c][:].bitcast(U32), lower.unsqueeze(2).to_broadcast([P, CHUNK, 2]))
-        for c in range(on_vector, len(chunks)):
-            words = pairs[c][:].rearrange("p w t e -> p w (t e)").bitcast(U32)
-            nc.scalar.copy(woven[c][:].bitcast(U32), words.rearrange("p w t -> p t w"))
+            nc.sync.dma_start(out_rows[:, i, :], page[:])
+            if i < 2:
+                nc.scalar.copy(pairs[:, :, i], page[:, CUTS[1] :])
+            if i == 2:
+                twice = page[:].unsqueeze(2).to_broadcast([P, T, 2])
+                for n in range(1, 1 + ON_VECTOR):
+                    nc.scalar.copy(woven[n][:, :, 2:4], twice[:, spans[n]])
+            nc.scalar.copy(first[:, i // 2, :, i % 2], page[:, spans[0]])
+            if i == PACK - 1:
+                halves = first[:].rearrange("p w t e -> p w (t e)").bitcast(U32)
+                nc.scalar.copy(woven[0][:].bitcast(U32), halves.rearrange("p w t -> p t w"))
+            for n in range(1, len(spans)):
+                if i == 1:
+                    lower = words[:, spans[n].start - CUTS[1] : spans[n].stop - CUTS[1]]
+                    nc.scalar.copy(woven[n][:].bitcast(U32), lower.unsqueeze(2).to_broadcast([P, lower.shape[1], 2]))
+                elif i == PACK - 1 and n <= ON_VECTOR:
+                    nc.vector.tensor_copy(woven[n][:, :, i], page[:, spans[n]])
+                elif i > 1 and n > ON_VECTOR:
+                    nc.scalar.copy(woven[n][:, :, i], page[:, spans[n]])
 
         out_c = keep([P, T], U32, "out_c")
         out_s = keep([P, T], U8, "out_s")
         words_out = out_1[0].rearrange("p t b -> p (t b)").bitcast(I32)
-        cuts = list(range(0, T, CHUNK)) + [T - LAST, T]
-        for lo, hi in zip(cuts, cuts[1:]):
-            values = woven[lo // CHUNK][:, lo % CHUNK : lo % CHUNK + hi - lo].rearrange("p t i -> p (t i)")
-            nc.vector.quantize_mx(out_c[:, lo:hi].bitcast(FP8X4), out_s[:, lo:hi], values)
-            nc.sync.dma_start(words_out[:, lo:hi], out_c[:, lo:hi].bitcast(I32))
-        for q in range(4):
-            nc.scalar.dma_start(out_2[0, 4 * q : 4 * q + 4, :].bitcast(I32), out_s[32 * q : 32 * q + 4, :].bitcast(I32))
+        order = list(range(1, 1 + ON_VECTOR)) + [0] + list(range(1 + ON_VECTOR, len(spans)))
+        for n in order:
+            nc.vector.quantize_mx(out_c[:, spans[n]].bitcast(FP8X4), out_s[:, spans[n]], woven[n][:].rearrange("p t i -> p (t i)"))
+            if n == order[-1]:
+                for q in range(4):
+                    queue = nc.sync if q % 2 else nc.scalar
+                    queue.dma_start(out_2[0, 4 * q : 4 * q + 4, :].bitcast(I32), out_s[32 * q : 32 * q + 4, :].bitcast(I32))
+            nc.sync.dma_start(words_out[:, spans[n]], out_c[:, spans[n]].bitcast(I32))

@@ -75,8 +75,9 @@ def tile_list_modp_gsilu_resP_kernel(
 
         wg_rows = wg.rearrange("(a p j) r -> a p j r", p=P, j=PACK)
         shared = 26 * KIB
-        wu_raw = place([P, PASSES, R], I32, "wu_raw", shared)
-        nc.sync.dma_start(wu_raw[:], wu_words.rearrange("a p r i -> p a (r i)").bitcast(I32))
+        wu_rows = wu_words.rearrange("a p r i -> a p (r i)").bitcast(I32)
+        wu_raw = [place([P, R], I32, "wu_raw0", shared)]
+        nc.sync.dma_start(wu_raw[0][:], wu_rows[0])
         wg_raw = [keep([P, PACK, R], F32, "wg_raw0")]
         nc.sync.dma_start(wg_raw[0][:], wg_rows[0])
 
@@ -128,18 +129,23 @@ def tile_list_modp_gsilu_resP_kernel(
                 nc.tensor.transpose(gate_bank[:, j : j + TOK], w_col[:, c : c + 1].to_broadcast([P, P]), ident[:])
             nc.scalar.copy(gate[:, j0 : j0 + HALF], gate_bank[:])
 
-        wu_c = keep([P, PASSES, R], U32, "wu_c")
+        wu_c = [keep([P, R], U32, "wu_c%d" % a) for a in range(PASSES)]
         wu_s = keep([P, PASSES, R], U8, "wu_s")
         nc.vector.tensor_copy(
             wu_s[:].rearrange("p a (t m) -> p a t m", t=PACK), wu_sc_raw[:].rearrange("p a (m t) -> p a t m", t=PACK)
         )
 
-        nc.scalar.copy(
-            wu_c[:].rearrange("p a (t c e) -> p a c t e", t=PACK, e=4),
-            wu_raw[:].bitcast(U32).rearrange("p a (c e t) -> p a c t e", t=PACK, e=4),
-        )
+        def deal(a):
+            nc.scalar.copy(
+                wu_c[a][:].rearrange("p (t c e) -> p c t e", t=PACK, e=4),
+                wu_raw[a][:].bitcast(U32).rearrange("p (c e t) -> p c t e", t=PACK, e=4),
+            )
+
+        deal(0)
         res[1] = place([P, T], F32, "res1", shared)
         nc.sync.dma_start(res[1][:], rT_rows[:, 1, :])
+        wu_raw.append(keep([P, R], I32, "wu_raw1", "wg_raw0"))
+        nc.sync.dma_start(wu_raw[1][:], wu_rows[1])
 
         wg_c, wg_s = [], []
         for a in range(PASSES):
@@ -152,7 +158,8 @@ def tile_list_modp_gsilu_resP_kernel(
             wg_s.append(keep([P, R], U8, "wg_s%d" % a))
             nc.vector.quantize_mx(wg_c[a][:].bitcast(FP8X4), wg_s[a][:], wg_bf[:])
 
-        load_res(2, "wg_raw0")
+        deal(1)
+        load_res(2, "wg_bf0")
         wd_w = place([P, 2 * N], U8, "wd_w", 8 * KIB)
         nc.sync.dma_start(wd_w[:].bitcast(I32), wd_words[0].bitcast(I32))
         last = 9 * KIB + N
@@ -183,41 +190,46 @@ def tile_list_modp_gsilu_resP_kernel(
 
         h_c = keep([P, J], U32, "h_c")
         h_s = keep([P, J], U8, "h_s")
-        wu_codes = [wu_c[:, a, :] for a in range(PASSES)]
         wu_scale = [wu_s[:, a, :] for a in range(PASSES)]
         copied_up = keep([P, 2, TOK, PACK], F32, "copied_up", "tab_sc")
         group = TILES // 2
 
-        def hidden(g, up_banks, gate_banks, h_at):
-            tiles = range(g * group, (g + 1) * group)
-            up = {}
-            for c, b in zip(tiles, up_banks):
-                u_bank = bank([P, PACK, TOK], "u_bank", b)
-                first_product(u_bank, wu_codes, wu_scale, c)
-                up[c] = u_bank[:].rearrange("p t j -> p j t")
-                if c == tiles[0]:
-                    nc.scalar.copy(copied_up[:, g], up[c])
-                    up[c] = copied_up[:, g]
+        def hidden(g, h_at, act_after):
+            act = keep([P, group, TOK, PACK], F32, "act%d" % g, act_after)
+            up = []
+
+            def up_sums():
+                for n in range(group):
+                    u_bank = bank([P, PACK, TOK], "u_bank", n)
+                    first_product(u_bank, wu_c, wu_scale, g * group + n)
+                    up.append(u_bank[:].rearrange("p t j -> p j t"))
+                    if n == 0:
+                        nc.scalar.copy(copied_up[:, g], up[0])
+
+            def gate_sums():
+                for n in range(group):
+                    g_bank = bank([P, PACK, TOK], "g_bank", group + n)
+                    first_product(g_bank, wg_c, wg_s, g * group + n)
+                    nc.scalar.activation(act[:, n], g_bank[:].rearrange("p t j -> p j t"), SILU, bias=bias[:])
+
+            for sums in (up_sums, gate_sums) if g == 0 else (gate_sums, up_sums):
+                sums()
             h_bf = place([P, group, TOK * PACK], BF16, "h_bf%d" % g, h_at)
-            for c, b in zip(tiles, gate_banks):
-                g_bank = bank([P, PACK, TOK], "g_bank", b)
-                first_product(g_bank, wg_c, wg_s, c)
-                act = keep([P, TOK, PACK], F32, "act%d" % c)
-                nc.scalar.activation(act[:], g_bank[:].rearrange("p t j -> p j t"), SILU, bias=bias[:])
-                engine = nc.gpsimd if c == tiles[0] else nc.vector
-                engine.tensor_tensor(h_bf[:, c % group, :].rearrange("p (j t) -> p j t", t=PACK), up[c], act[:], MULT)
+            for n in range(group):
+                engine, u = (nc.gpsimd, copied_up[:, g]) if n == 0 else (nc.vector, up[n])
+                engine.tensor_tensor(h_bf[:, n, :].rearrange("p (j t) -> p j t", t=PACK), u, act[:, n], MULT)
             for lo, hi in ((0, group - 1), (group - 1, group)):
                 tok = slice(g * HALF + lo * TOK, g * HALF + hi * TOK)
                 nc.vector.quantize_mx(h_c[:, tok].bitcast(FP8X4), h_s[:, tok], h_bf[:, lo:hi, :].rearrange("p c x -> p (c x)"))
 
         pick(0)
         pick(1)
-        hidden(0, (0, 1, 2, 3), (4, 5, 6, 7), shared)
+        hidden(0, shared, None)
         pages = [place([P, T], F32, "page_0", shared)]
         nc.gpsimd.memset(pages[0][:], 0.0)
-        pick(2, "act3")
-        pick(3, "act2")
-        hidden(1, (0, 4, 5, 0), (6, 7, 6, 7), 14 * KIB)
+        pick(2, "act0")
+        pick(3)
+        hidden(1, 14 * KIB, "wg_raw0")
         pages.append(place([P, T], F32, "page_1", last))
         pages.append(place([P, T], F32, "page_2", last + 8 * KIB))
         for page in pages[1:]:
@@ -247,7 +259,7 @@ def tile_list_modp_gsilu_resP_kernel(
         def put(i, j0, j1):
             nc.vector.tensor_tensor(pages[i % len(pages)][:].indirect(listed(j0, j1)), rw[i][:, j0:j1], yw[:, i, j0:j1], ADD)
 
-        for g, y_banks, t_banks in ((0, (6, 7), (1, 2, 3, 6)), (1, (1, 2), (7, 3, 6, 4))):
+        for g, y_banks, t_banks in ((0, (6, 7), (4, 5, 4, 5)), (1, (4, 5), (6, 7, 1, 2))):
             for c in range(g * group, (g + 1) * group):
                 second_product(c, y_banks[c % 2])
             for i in range(PACK):

@@ -62,10 +62,9 @@ def tile_list_modp_gsilu_resP_kernel(
 
         wu_sc_raw = keep([P, PASSES, R], U8, "wu_sc_raw")
         nc.gpsimd.memset(wu_sc_raw[:].bitcast(I32), 0)
-        for q in range(4):
+        for r in range(4):
             nc.sync.dma_start(
-                wu_sc_raw[32 * q : 32 * q + 4, :, :].bitcast(I32),
-                wu_scales[:, 4 * q : 4 * q + 4, :].rearrange("a r n -> r a n").bitcast(I32),
+                wu_sc_raw[r:P:32, :, :].bitcast(I32), wu_scales[:, r:16:4, :].rearrange("a q n -> q a n").bitcast(I32)
             )
         tab_w = keep([P, T], I32, "tab_w")
         nc.sync.dma_start(tab_w[:], tab_words[0].rearrange("p t b -> p (t b)").bitcast(I32))
@@ -167,8 +166,8 @@ def tile_list_modp_gsilu_resP_kernel(
         nc.sync.dma_start(res[3][:], rT_rows[:, 3, :])
         wd_s = place([P, N], U8, "wd_s", 9 * KIB)
         nc.gpsimd.memset(wd_s[:].bitcast(I32), 0)
-        for q in range(4):
-            nc.sync.dma_start(wd_s[32 * q : 32 * q + 4, :].bitcast(I32), wd_scales[0, 4 * q : 4 * q + 4, :].bitcast(I32))
+        for r in range(4):
+            nc.sync.dma_start(wd_s[r:P:32, :].bitcast(I32), wd_scales[0, r:16:4, :].bitcast(I32))
 
         rw = {}
 
@@ -194,7 +193,7 @@ def tile_list_modp_gsilu_resP_kernel(
         copied_up = keep([P, 2, TOK, PACK], F32, "copied_up", "tab_sc")
         group = TILES // 2
 
-        def hidden(g, h_at, act_after):
+        def hidden(g, h_first, h_at, act_after):
             act = keep([P, group, TOK, PACK], F32, "act%d" % g, act_after)
             up = []
 
@@ -214,24 +213,24 @@ def tile_list_modp_gsilu_resP_kernel(
 
             for sums in (up_sums, gate_sums) if g == 0 else (gate_sums, up_sums):
                 sums()
-            h_bf = place([P, group, TOK * PACK], BF16, "h_bf%d" % g, h_at)
+            h_rest = place([P, group - 1, TOK * PACK], BF16, "h_rest%d" % g, h_at)
             for n in range(group):
-                engine, u = (nc.gpsimd, copied_up[:, g]) if n == 0 else (nc.vector, up[n])
-                engine.tensor_tensor(h_bf[:, n, :].rearrange("p (j t) -> p j t", t=PACK), u, act[:, n], MULT)
-            for lo, hi in ((0, group - 1), (group - 1, group)):
+                engine, u, h = (nc.gpsimd, copied_up[:, g], h_first[:]) if n == 0 else (nc.vector, up[n], h_rest[:, n - 1])
+                engine.tensor_tensor(h.rearrange("p (j t) -> p j t", t=PACK), u, act[:, n], MULT)
+            for lo, hi, h in ((0, 1, h_first[:]), (1, group, h_rest[:].rearrange("p c x -> p (c x)"))):
                 tok = slice(g * HALF + lo * TOK, g * HALF + hi * TOK)
-                nc.vector.quantize_mx(h_c[:, tok].bitcast(FP8X4), h_s[:, tok], h_bf[:, lo:hi, :].rearrange("p c x -> p (c x)"))
+                nc.vector.quantize_mx(h_c[:, tok].bitcast(FP8X4), h_s[:, tok], h)
 
         pick(0)
         pick(1)
-        hidden(0, shared, None)
-        pages = [place([P, T], F32, "page_0", shared)]
+        hidden(0, place([P, TOK * PACK], BF16, "h_first0", shared), 34 * KIB, None)
+        pages = [place([P, T], F32, "page_0", 34 * KIB)]
         nc.gpsimd.memset(pages[0][:], 0.0)
         pick(2, "act0")
-        pick(3)
-        hidden(1, 14 * KIB, "wg_raw0")
-        pages.append(place([P, T], F32, "page_1", last))
-        pages.append(place([P, T], F32, "page_2", last + 8 * KIB))
+        hidden(1, keep([P, TOK * PACK], BF16, "h_first1", "wg_bf0"), last + 8 * KIB, "wg_raw0")
+        pick(3, "wg_raw0")
+        pages.append(place([P, T], F32, "page_1", last + 8 * KIB))
+        pages.append(place([P, T], F32, "page_2", last))
         for page in pages[1:]:
             nc.gpsimd.memset(page[:], 0.0)
 
@@ -304,7 +303,7 @@ def tile_list_modp_gsilu_resP_kernel(
         for n in order:
             nc.vector.quantize_mx(out_c[:, spans[n]].bitcast(FP8X4), out_s[:, spans[n]], woven[n][:].rearrange("p t i -> p (t i)"))
             if n == order[-1]:
-                for q in range(4):
-                    queue = nc.sync if q % 2 else nc.scalar
-                    queue.dma_start(out_2[0, 4 * q : 4 * q + 4, :].bitcast(I32), out_s[32 * q : 32 * q + 4, :].bitcast(I32))
+                for r in range(4):
+                    queue = nc.sync if r % 2 else nc.scalar
+                    queue.dma_start(out_2[0, r:16:4, :].bitcast(I32), out_s[r:P:32, :].bitcast(I32))
             nc.sync.dma_start(words_out[:, spans[n]], out_c[:, spans[n]].bitcast(I32))

@@ -25,7 +25,7 @@ PASSES = K // (P * PACK)
 TOK = 128
 TILES = J // TOK
 HALF = J // 2
-SCALAR_GROUPS = (64, 48)
+SCALAR_GROUPS = (72, 48)
 KIB = 1024
 CUTS = (0, 512, 1024, 1408, 1920, 2048)
 ON_VECTOR = 2
@@ -56,9 +56,8 @@ def tile_list_modp_gsilu_resP_kernel(
             return offsets[:, j0 // 16 : j1 // 16]
 
         tab_sc = keep([P, T], U8, "tab_sc")
-        sc_rows = tab_scales.rearrange("a (h u r) t -> u (a h) r t", h=2, u=2)
-        for u in range(2):
-            nc.scalar.dma_start(tab_sc[32 * u + 16 : 32 * u + 32, :].bitcast(I32), sc_rows[u].bitcast(I32))
+        for a in range(PASSES):
+            nc.scalar.dma_start(tab_sc[a:32:2, :].bitcast(I32), tab_scales[a].rearrange("(q r) t -> r q t", r=4).bitcast(I32))
 
         wu_sc_raw = keep([P, PASSES, R], U8, "wu_sc_raw")
         nc.gpsimd.memset(wu_sc_raw[:].bitcast(I32), 0)
@@ -89,8 +88,11 @@ def tile_list_modp_gsilu_resP_kernel(
 
         ident = keep([P, P], F32, "ident")
         make_identity(nc, ident[:])
-        for lo, hi in ((0, 16), (32, 48), (64, 128)):
+        for lo, hi in ((32, 64), (64, 128)):
             nc.vector.memset(tab_sc[lo:hi, :].bitcast(I32), 0)
+
+        v_sc = keep([P, PASSES, J], U8, "v_sc")
+        nc.vector.memset(v_sc[:].bitcast(I32), 0)
 
         zero = keep([P, 1], F32, "zero")
         nc.vector.memset(zero[:], 0.0)
@@ -99,11 +101,8 @@ def tile_list_modp_gsilu_resP_kernel(
 
         picked_sc = keep([P, J], U8, "picked_sc")
         nc.vector.tensor_copy(picked_sc[:], tab_sc[:].indirect(offsets[:]))
-        v_sc = [keep([P, J], U8, "v_sc%d" % a) for a in range(PASSES)]
-        for a in range(PASSES):
-            for h in range(2):
-                lo = 16 + 8 * a + 4 * h
-                nc.sync.dma_start(v_sc[a][64 * h : 64 * h + 64, :].bitcast(I32), picked_sc[lo : lo + 64, :].bitcast(I32))
+        for r in range(4):
+            nc.sync.dma_start(v_sc[r:P:32, :, :].bitcast(I32), picked_sc[8 * r : 8 * r + 8, :].bitcast(I32))
 
         both = [keep([P, HALF], U32, "both%d" % g) for g in range(2)]
         v_w = [keep([P, PASSES, 2 * HALF], U8, "parted%d" % g) for g in range(2)]
@@ -128,7 +127,7 @@ def tile_list_modp_gsilu_resP_kernel(
                 nc.tensor.transpose(gate_bank[:, j : j + TOK], w_col[:, c : c + 1].to_broadcast([P, P]), ident[:])
             nc.scalar.copy(gate[:, j0 : j0 + HALF], gate_bank[:])
 
-        wu_c = [keep([P, R], U32, "wu_c%d" % a) for a in range(PASSES)]
+        wu_c = [keep([P, R], U32, "wu_c0", "w_rows"), keep([P, R], U32, "wu_c1")]
         wu_s = keep([P, PASSES, R], U8, "wu_s")
         nc.vector.tensor_copy(
             wu_s[:].rearrange("p a (t m) -> p a t m", t=PACK), wu_sc_raw[:].rearrange("p a (m t) -> p a t m", t=PACK)
@@ -183,7 +182,7 @@ def tile_list_modp_gsilu_resP_kernel(
                     nc.tensor.matmul_mx(
                         sums[:, t, :], lhsT=codes[a][:, cols].bitcast(FP8X4), lhsT_scale=scales[a][:, cols],
                         rhs=v_w[g][:, a, 2 * j : 2 * (j + TOK)].bitcast(FP4X4),
-                        rhs_scale=v_sc[a][:, c * TOK : (c + 1) * TOK],
+                        rhs_scale=v_sc[:, a, c * TOK : (c + 1) * TOK],
                         start=(a, t) == (0, 0), stop=(a, t) == (PASSES - 1, PACK - 1),
                     )
 

@@ -25,7 +25,7 @@ PASSES = K // (P * PACK)
 TOK = 128
 TILES = J // TOK
 HALF = J // 2
-SCALAR_GROUPS = (72, 48)
+SCALAR_GROUPS = (56, 36)
 KIB = 1024
 CUTS = (0, 512, 1024, 1408, 1920, 2048)
 ON_VECTOR = 2

from contextlib import ExitStack

import concourse.mybir as mybir
from concourse.masks import make_identity

K, R, N, T, J = 1024, 512, 512, 2048, 1024
FLOPS = 2 * J * (2 * K * R + R * N)

F32 = mybir.dt.float32
BF16 = mybir.dt.bfloat16
I32 = mybir.dt.int32
U32 = mybir.dt.uint32
U16 = mybir.dt.uint16
U8 = mybir.dt.uint8
FP8X4 = mybir.dt.float8_e4m3fn_x4
FP4X4 = mybir.dt.float4_e2m1fn_x4
MULT = mybir.AluOpType.mult
ADD = mybir.AluOpType.add
SILU = mybir.ActivationFunctionType.Silu
COPY = mybir.ActivationFunctionType.Copy

P = 128
PACK = 4
PASSES = K // (P * PACK)
TOK = 128
TILES = J // TOK
HALF = J // 2
SCALAR_GROUPS = (56, 36)
KIB = 1024
CUTS = (0, 512, 1024, 1408, 1920, 2048)
ON_VECTOR = 2


def tile_list_modp_gsilu_resP_kernel(
    tc, tab_words, tab_scales, wg, wu_words, wu_scales, wd_words, wd_scales, rT, wgo, offs, out_0, out_1, out_2
):
    nc = tc.nc
    with ExitStack() as ctx:
        held = ctx.enter_context(tc.tile_pool(name="held", bufs=1))
        late = ctx.enter_context(tc.tile_pool(name="late", bufs=1))
        psum = ctx.enter_context(tc.psum_pool(name="psum", bufs=1))

        def keep(shape, dtype, name, after=None):
            return held.tile(shape, dtype, name=name, tag=after or name, align_bytes=64)

        def place(shape, dtype, name, offset):
            return late.tile(shape, dtype, name=name, offset=offset, align_bytes=64)

        def bank(shape, name, b):
            return psum.tile(shape, F32, name=name, tag="bank%d" % b)

        offsets = held.tile([P, J // 16], U16, name="offsets")
        nc.sync.dma_start(offsets[:], offs)

        def listed(j0, j1):
            return offsets[:, j0 // 16 : j1 // 16]

        tab_sc = keep([P, T], U8, "tab_sc")
        for a in range(PASSES):
            nc.scalar.dma_start(tab_sc[a:32:2, :].bitcast(I32), tab_scales[a].rearrange("(q r) t -> r q t", r=4).bitcast(I32))

        wu_sc_raw = keep([P, PASSES, R], U8, "wu_sc_raw")
        nc.gpsimd.memset(wu_sc_raw[:].bitcast(I32), 0)
        for r in range(4):
            nc.sync.dma_start(
                wu_sc_raw[r:P:32, :, :].bitcast(I32), wu_scales[:, r:16:4, :].rearrange("a q n -> q a n").bitcast(I32)
            )
        tab_w = keep([P, T], I32, "tab_w")
        nc.sync.dma_start(tab_w[:], tab_words[0].rearrange("p t b -> p (t b)").bitcast(I32))
        w_rows = keep([P, P], F32, "w_rows")
        nc.gpsimd.memset(w_rows[:], 0.0)
        nc.sync.dma_start(w_rows[0:TILES, :], wgo[0].rearrange("(c j) -> c j", j=TOK))

        wg_rows = wg.rearrange("(a p j) r -> a p j r", p=P, j=PACK)
        shared = 26 * KIB
        wu_rows = wu_words.rearrange("a p r i -> a p (r i)").bitcast(I32)
        wu_raw = [place([P, R], I32, "wu_raw0", shared)]
        nc.sync.dma_start(wu_raw[0][:], wu_rows[0])
        wg_raw = [keep([P, PACK, R], F32, "wg_raw0")]
        nc.sync.dma_start(wg_raw[0][:], wg_rows[0])

        rT_rows = rT.rearrange("(p i) t -> p i t", i=PACK)
        res = {}

        def load_res(i, after=None):
            res[i] = keep([P, T], F32, "res%d" % i, after)
            nc.sync.dma_start(res[i][:], rT_rows[:, i, :])

        ident = keep([P, P], F32, "ident")
        make_identity(nc, ident[:])
        for lo, hi in ((32, 64), (64, 128)):
            nc.vector.memset(tab_sc[lo:hi, :].bitcast(I32), 0)

        v_sc = keep([P, PASSES, J], U8, "v_sc")
        nc.vector.memset(v_sc[:].bitcast(I32), 0)

        zero = keep([P, 1], F32, "zero")
        nc.vector.memset(zero[:], 0.0)
        bias = keep([P, 1], F32, "bias")
        nc.scalar.activation(bias[:], zero[:], SILU)

        picked_sc = keep([P, J], U8, "picked_sc")
        nc.vector.tensor_copy(picked_sc[:], tab_sc[:].indirect(offsets[:]))
        for r in range(4):
            nc.sync.dma_start(v_sc[r:P:32, :, :].bitcast(I32), picked_sc[8 * r : 8 * r + 8, :].bitcast(I32))

        both = [keep([P, HALF], U32, "both%d" % g) for g in range(2)]
        v_w = [keep([P, PASSES, 2 * HALF], U8, "parted%d" % g) for g in range(2)]
        for g in range(2):
            nc.vector.tensor_copy(both[g][:], tab_w[:].bitcast(U32).indirect(listed(g * HALF, (g + 1) * HALF)))
        for g in range(2):
            nc.vector.tensor_copy(v_w[g][:].bitcast(U16), both[g][:].bitcast(U16).rearrange("p (j d) -> p d j", d=2))

        wg_raw.append(keep([P, PACK, R], F32, "wg_raw1", "tab_sc"))
        nc.sync.dma_start(wg_raw[1][:], wg_rows[1])
        load_res(0, "tab_w")

        w_bank = bank([P, P], "w_bank", 5)
        nc.tensor.transpose(w_bank[:], w_rows[:], ident[:])
        w_col = keep([P, TILES], F32, "w_col")
        nc.scalar.copy(w_col[:], w_bank[:, 0:TILES])
        gate = keep([P, J], F32, "gate")
        for j0 in range(0, J, HALF):
            gate_bank = bank([P, HALF], "gate_bank", 6 + j0 // HALF)
            for j in range(0, HALF, TOK):
                c = (j0 + j) // TOK
                nc.tensor.transpose(gate_bank[:, j : j + TOK], w_col[:, c : c + 1].to_broadcast([P, P]), ident[:])
            nc.scalar.copy(gate[:, j0 : j0 + HALF], gate_bank[:])

        wu_c = [keep([P, R], U32, "wu_c0", "w_rows"), keep([P, R], U32, "wu_c1")]
        wu_s = keep([P, PASSES, R], U8, "wu_s")
        nc.vector.tensor_copy(
            wu_s[:].rearrange("p a (t m) -> p a t m", t=PACK), wu_sc_raw[:].rearrange("p a (m t) -> p a t m", t=PACK)
        )

        def deal(a):
            nc.scalar.copy(
                wu_c[a][:].rearrange("p (t c e) -> p c t e", t=PACK, e=4),
                wu_raw[a][:].bitcast(U32).rearrange("p (c e t) -> p c t e", t=PACK, e=4),
            )

        deal(0)
        res[1] = place([P, T], F32, "res1", shared)
        nc.sync.dma_start(res[1][:], rT_rows[:, 1, :])
        wu_raw.append(keep([P, R], I32, "wu_raw1", "wg_raw0"))
        nc.sync.dma_start(wu_raw[1][:], wu_rows[1])

        wg_c, wg_s = [], []
        for a in range(PASSES):
            wg_bf = keep([P, R * PACK], BF16, "wg_bf0") if a == 0 else place([P, R * PACK], BF16, "wg_bf1", 8 * KIB)
            dst = wg_bf[:].rearrange("p (t m j) -> p m t j", t=PACK, j=PACK)
            src = wg_raw[a][:].rearrange("p j (m t) -> p m t j", t=PACK)
            nc.scalar.copy(dst[:, : SCALAR_GROUPS[a]], src[:, : SCALAR_GROUPS[a]])
            nc.vector.tensor_copy(dst[:, SCALAR_GROUPS[a] :], src[:, SCALAR_GROUPS[a] :])
            wg_c.append(keep([P, R], U32, "wg_c%d" % a))
            wg_s.append(keep([P, R], U8, "wg_s%d" % a))
            nc.vector.quantize_mx(wg_c[a][:].bitcast(FP8X4), wg_s[a][:], wg_bf[:])

        deal(1)
        load_res(2, "wg_bf0")
        wd_w = place([P, 2 * N], U8, "wd_w", 8 * KIB)
        nc.sync.dma_start(wd_w[:].bitcast(I32), wd_words[0].bitcast(I32))
        last = 9 * KIB + N
        res[3] = place([P, T], F32, "res3", last)
        nc.sync.dma_start(res[3][:], rT_rows[:, 3, :])
        wd_s = place([P, N], U8, "wd_s", 9 * KIB)
        nc.gpsimd.memset(wd_s[:].bitcast(I32), 0)
        for r in range(4):
            nc.sync.dma_start(wd_s[r:P:32, :].bitcast(I32), wd_scales[0, r:16:4, :].bitcast(I32))

        rw = {}

        def pick(i, after=None):
            rw[i] = keep([P, J], F32, "rw%d" % i, after)
            nc.vector.tensor_tensor(rw[i][:], res[i][:].indirect(offsets[:]), gate[:], MULT)

        def first_product(sums, codes, scales, c):
            g, j = divmod(c * TOK, HALF)
            for a in range(PASSES):
                for t in range(PACK):
                    cols = slice(P * t, P * (t + 1))
                    nc.tensor.matmul_mx(
                        sums[:, t, :], lhsT=codes[a][:, cols].bitcast(FP8X4), lhsT_scale=scales[a][:, cols],
                        rhs=v_w[g][:, a, 2 * j : 2 * (j + TOK)].bitcast(FP4X4),
                        rhs_scale=v_sc[:, a, c * TOK : (c + 1) * TOK],
                        start=(a, t) == (0, 0), stop=(a, t) == (PASSES - 1, PACK - 1),
                    )

        h_c = keep([P, J], U32, "h_c")
        h_s = keep([P, J], U8, "h_s")
        wu_scale = [wu_s[:, a, :] for a in range(PASSES)]
        copied_up = keep([P, 2, TOK, PACK], F32, "copied_up", "tab_sc")
        group = TILES // 2

        def hidden(g, h_first, h_at, act_after):
            act = keep([P, group, TOK, PACK], F32, "act%d" % g, act_after)
            up = []

            def up_sums():
                for n in range(group):
                    u_bank = bank([P, PACK, TOK], "u_bank", n)
                    first_product(u_bank, wu_c, wu_scale, g * group + n)
                    up.append(u_bank[:].rearrange("p t j -> p j t"))
                    if n == 0:
                        nc.scalar.copy(copied_up[:, g], up[0])

            def gate_sums():
                for n in range(group):
                    g_bank = bank([P, PACK, TOK], "g_bank", group + n)
                    first_product(g_bank, wg_c, wg_s, g * group + n)
                    nc.scalar.activation(act[:, n], g_bank[:].rearrange("p t j -> p j t"), SILU, bias=bias[:])

            for sums in (up_sums, gate_sums) if g == 0 else (gate_sums, up_sums):
                sums()
            h_rest = place([P, group - 1, TOK * PACK], BF16, "h_rest%d" % g, h_at)
            for n in range(group):
                engine, u, h = (nc.gpsimd, copied_up[:, g], h_first[:]) if n == 0 else (nc.vector, up[n], h_rest[:, n - 1])
                engine.tensor_tensor(h.rearrange("p (j t) -> p j t", t=PACK), u, act[:, n], MULT)
            for lo, hi, h in ((0, 1, h_first[:]), (1, group, h_rest[:].rearrange("p c x -> p (c x)"))):
                tok = slice(g * HALF + lo * TOK, g * HALF + hi * TOK)
                nc.vector.quantize_mx(h_c[:, tok].bitcast(FP8X4), h_s[:, tok], h)

        pick(0)
        pick(1)
        hidden(0, place([P, TOK * PACK], BF16, "h_first0", shared), 34 * KIB, None)
        pages = [place([P, T], F32, "page_0", 34 * KIB)]
        nc.gpsimd.memset(pages[0][:], 0.0)
        pick(2, "act0")
        hidden(1, keep([P, TOK * PACK], BF16, "h_first1", "wg_bf0"), last + 8 * KIB, "wg_raw0")
        pick(3, "wg_raw0")
        pages.append(place([P, T], F32, "page_1", last + 8 * KIB))
        pages.append(place([P, T], F32, "page_2", last))
        for page in pages[1:]:
            nc.gpsimd.memset(page[:], 0.0)

        y_tok = {}
        yw = keep([P, PACK, J], F32, "yw")

        def second_product(c, b):
            y_bank = bank([P, N], "y_bank", b)
            tok = slice(c * TOK, (c + 1) * TOK)
            nc.tensor.matmul_mx(
                y_bank[:], lhsT=h_c[:, tok].bitcast(FP8X4), lhsT_scale=h_s[:, tok],
                rhs=wd_w[:].bitcast(FP4X4), rhs_scale=wd_s[:], start=True, stop=True,
            )
            y_tok[c] = keep([P, PACK, P], F32, "y_tok%d" % c)
            nc.scalar.activation(
                y_tok[c][:], y_bank[:].rearrange("p (m i) -> p i m", i=PACK), COPY, scale=w_col[:, c : c + 1]
            )

        def turn(i, g, b):
            t_bank = bank([P, HALF], "t_bank", b)
            for j in range(0, HALF, TOK):
                nc.tensor.transpose(t_bank[:, j : j + TOK], y_tok[g * group + j // TOK][:, i, :], ident[:])
            nc.scalar.copy(yw[:, i, g * HALF : (g + 1) * HALF], t_bank[:])

        def put(i, j0, j1):
            nc.vector.tensor_tensor(pages[i % len(pages)][:].indirect(listed(j0, j1)), rw[i][:, j0:j1], yw[:, i, j0:j1], ADD)

        for g, y_banks, t_banks in ((0, (6, 7), (4, 5, 4, 5)), (1, (4, 5), (6, 7, 1, 2))):
            for c in range(g * group, (g + 1) * group):
                second_product(c, y_banks[c % 2])
            for i in range(PACK):
                turn(i, g, t_banks[i])
            for i in range(2):
                put(i, g * HALF, (g + 1) * HALF)

        spans = [slice(lo, hi) for lo, hi in zip(CUTS, CUTS[1:])]
        woven = [keep([P, s.stop - s.start, PACK], BF16, "woven%d" % n) for n, s in enumerate(spans)]
        first = keep([P, 2, CUTS[1], 2], BF16, "first", "y_tok1")
        pairs = keep([P, T - CUTS[1], 2], BF16, "pairs", "y_tok0")
        words = pairs[:].rearrange("p t e -> p (t e)").bitcast(U32)
        out_rows = out_0.rearrange("(p i) t -> p i t", i=PACK)
        for i in range(PACK):
            page = pages[i % len(pages)]
            if i > 1:
                put(i, 0, J)
            nc.sync.dma_start(out_rows[:, i, :], page[:])
            if i < 2:
                nc.scalar.copy(pairs[:, :, i], page[:, CUTS[1] :])
            if i == 2:
                twice = page[:].unsqueeze(2).to_broadcast([P, T, 2])
                for n in range(1, 1 + ON_VECTOR):
                    nc.scalar.copy(woven[n][:, :, 2:4], twice[:, spans[n]])
            nc.scalar.copy(first[:, i // 2, :, i % 2], page[:, spans[0]])
            if i == PACK - 1:
                halves = first[:].rearrange("p w t e -> p w (t e)").bitcast(U32)
                nc.scalar.copy(woven[0][:].bitcast(U32), halves.rearrange("p w t -> p t w"))
            for n in range(1, len(spans)):
                if i == 1:
                    lower = words[:, spans[n].start - CUTS[1] : spans[n].stop - CUTS[1]]
                    nc.scalar.copy(woven[n][:].bitcast(U32), lower.unsqueeze(2).to_broadcast([P, lower.shape[1], 2]))
                elif i == PACK - 1 and n <= ON_VECTOR:
                    nc.vector.tensor_copy(woven[n][:, :, i], page[:, spans[n]])
                elif i > 1 and n > ON_VECTOR:
                    nc.scalar.copy(woven[n][:, :, i], page[:, spans[n]])

        out_c = keep([P, T], U32, "out_c")
        out_s = keep([P, T], U8, "out_s")
        words_out = out_1[0].rearrange("p t b -> p (t b)").bitcast(I32)
        order = list(range(1, 1 + ON_VECTOR)) + [0] + list(range(1 + ON_VECTOR, len(spans)))
        for n in order:
            nc.vector.quantize_mx(out_c[:, spans[n]].bitcast(FP8X4), out_s[:, spans[n]], woven[n][:].rearrange("p t i -> p (t i)"))
            if n == order[-1]:
                for r in range(4):
                    queue = nc.sync if r % 2 else nc.scalar
                    queue.dma_start(out_2[0, r:16:4, :].bitcast(I32), out_s[r:P:32, :].bitcast(I32))
            nc.sync.dma_start(words_out[:, spans[n]], out_c[:, spans[n]].bitcast(I32))
